import numpy as np, ml_dtypes
CORES = [9,25,41,57]
N = 4
BF = ml_dtypes.bfloat16
def gentries(a):
    return np.ascontiguousarray(a.reshape(8, 16, -1).transpose(0, 2, 1)).reshape(8, -1)
def gtable(e):
    e = np.asarray(e); return np.ascontiguousarray(e.reshape(8, -1, 16).transpose(0, 2, 1)).reshape(128, -1).astype(np.int32)
V, L, SH, EPS, RO = 8192, 256, 2, 5, 4
Q = 256 >> SH; LQ = 8 - SH; E = 16 * Q
TIGHT = (2 ** SH - 1 - EPS, EPS)
def labels(rng):
    slot = np.argsort(rng.random((8, 16, 16)), axis=-1); size = rng.permutation(np.array([6, 7, 8, 8, 10, 12, 14, 16]))[:, None, None]
    high = 8 + np.argsort(rng.random((8, 16, 8)), axis=-1); slot[..., :8] = np.where(size == 8, high, slot[..., :8])
    u = (rng.random((N, 8, 16, V)) * size).astype(np.int64)
    return 16 * np.take_along_axis(np.ascontiguousarray(np.broadcast_to(slot, (N, 8, 16, 16))), u, 3) + 8 + rng.integers(-3, 4, (N, 8, 16, V))
def inverse(rng, s, near, lo, hi):
    near = np.broadcast_to(near, (N, 8, 16, Q, 16)); out = np.empty((N, 8, 16, Q, 16), np.int64); base = np.arange(Q) << SH
    order = np.argsort(s.astype(np.int16), axis=-1, kind="stable")
    for r in range(N):
        for g in range(8):
            for p in range(16):
                o = order[r, g, p]; v = s[r, g, p][o]
                a = np.searchsorted(v, base + lo, "left"); n = (np.searchsorted(v, base + hi, "right") - a)[:, None]
                fa = np.searchsorted(v, base - EPS, "left"); fb = np.searchsorted(v, base + 2 ** SH - 1 + EPS, "right")
                u = rng.random((Q, 16))
                far = (fb[:, None] + (u * (V - (fb - fa))[:, None]).astype(np.int64)) % V
                out[r, g, p] = o[np.where(near[r, g, p] & (n > 0), np.minimum(a[:, None] + (u * n).astype(np.int64), V - 1), far)]
    return np.ascontiguousarray(out.reshape(N, 8, E, 16).transpose(0, 1, 3, 2))
def starts(rng, s, share):
    p = rng.integers(0, 16, (N, 8, L)); c = rng.integers(0, V, (N, 8, L))
    y = s[np.arange(N)[:, None, None], np.arange(8)[None, :, None], p, c]
    return np.where(rng.random((N, 8, L)) < share, Q * p + (y >> SH), rng.integers(0, E, (N, 8, L)))
def pack(s, w, e):
    return {"st": np.ascontiguousarray(s.reshape(N, 128, V)).astype(np.float32).astype(BF), "iv": np.ascontiguousarray(w).reshape(N, 128, E).astype(np.int32), "e0": np.stack([gtable(x) for x in e])}
def setup_inputs(rng):
    s = labels(rng); near = rng.random((N, 8, 16, Q, 16)) < rng.choice(np.array([0.5, 0.7, 0.85, 0.95]), (N, 8, 1, 1, 1))
    return pack(s, inverse(rng, s, near, *TIGHT), starts(rng, s, 0.85))
def setup_inputs_spread(rng):
    pw = rng.permutation(np.array([1.0, 1.0, 1.0, 2.0, 3.0, 4.0, 6.0, 8.0]))[:, None, None]
    s = np.minimum((256 * rng.random((N, 8, 16, V)) ** pw).astype(np.int64), 255)
    s = np.where(rng.random((8, 16, 1)) < 0.5, 255 - s, s); near = rng.random((N, 8, 16, Q, 16)) < 0.6
    return pack(s, inverse(rng, s, near, *TIGHT), starts(rng, s, 0.5))
def setup_inputs_ends(rng):
    s = 255 * rng.integers(0, 2, (N, 8, 16, V))
    s[..., V - 1] = 255; s[..., V - 2] = 255 - EPS - 1; s[..., V - 4:V - 2] = 255 - 2 * EPS - 2; s[:, :, 15, V - 4:] = 255; s[::2, :, 14, V - 4:V - 2] -= 1
    s[..., 0] = 0; s[..., 1] = EPS + 1; s[..., 2] = 2 * EPS + 2; s[:, :, 0, :3] = 0
    w = np.where(rng.random((N, 8, 16, E)) < 0.75, (V - 1) * rng.integers(0, 2, (N, 8, 16, E)), rng.integers(0, V, (N, 8, 16, E)))
    alike = rng.integers(0, 2, (N, 8)); alike[:, 0] = 1; alike[:, 7] = 0
    third = V - 3 - rng.integers(0, 2, (N, 8)); third[0, 7] = V - 3; third[N - 1, 7] = V - 4
    hi = np.where(rng.random((N, 8, 16)) < 0.7, V - 1, 0); hi[:, :, 13] = V - 1; hi[:, :, 14] = V - 2; hi[:, :, 15] = third
    lo = np.where(rng.random((N, 8, 16)) < 0.7, 0, V - 1); lo[:, :, 13] = 0; lo[:, :, 14] = 1; lo[:, :, 15] = 2
    w[..., E - 1] = np.where(alike[:, :, None] == 1, V - 1, hi); w[..., 0] = np.where(alike[:, :, None] == 1, 0, lo)
    e = np.where(rng.random((N, 8, L)) < 0.85, (E - 1) * rng.integers(0, 2, (N, 8, L)), rng.integers(0, E, (N, 8, L)))
    e[:, :, 0] = 0; e[:, :, L - 1] = E - 1
    return pack(s, w, e)
def setup_inputs_corners(rng):
    s = labels(rng); lane = np.arange(L)
    s[:, 1] = rng.integers(0, 256, (16, 1)); s[:, 4] = rng.integers(0, 256, (N, 16, V))
    ta = rng.integers(0, 100, 16); ty = rng.integers(0, 2, (N, 1, V)) ^ (rng.random((N, 16, V)) < 0.03); ty[:, 5] = 0
    s[:, 5] = ta[None, :, None] + 120 * ty
    near = rng.random((N, 8, 16, Q, 16)) < 0.8
    near[:, 0] = False; near[:, 1] = True; near[:, 2] = np.arange(16) == 15; near[:, 3] = np.arange(16) == 0; near[:, 4] = True; near[:, 5] = True
    w = inverse(rng, s, near, *TIGHT); e = starts(rng, s, 0.9)
    w[:, 6] = np.where(rng.random((N, 1, E)) < 0.5, (V - 1) * rng.integers(0, 2, (N, 1, E)), w[:, 6])
    own = lane + L * rng.integers(0, E // L, (N, L)); pick = rng.integers(0, 4, (N, L))
    e[:, 5] = Q * 5 + (ta[5] >> SH)
    e[:, 6] = np.where(pick == 0, 0, np.where(pick == 1, E - 1, np.where(pick == 2, own, e[:, 6])))
    e[:, 7] = np.where(rng.random((N, L)) < 0.5, own, e[:, 7])
    return pack(s, w, e)
def setup_inputs_crowd(rng):
    s = labels(rng); t = rng.integers(0, 256, (6, 16))
    s[:, :6] = t[:, :, None]; s[:, :6, :8, 1::2] = ((t + 128) & 255)[:, :8, None]
    w = inverse(rng, s, rng.random((N, 8, 16, Q, 16)) < 0.8, *TIGHT); e = starts(rng, s, 0.8)
    cnt = (np.arange(6) % 3)[None, :, None, None]; place = np.argsort(rng.random((N, 6, 16, E)), axis=2)
    w[:, :6] = 2 * rng.integers(0, V // 2, (N, 6, 16, E)) + (place < cnt)
    p = rng.integers(8, 16, 6); p[5] = rng.integers(0, 8)
    e[:, :6] = (Q * p + (t[np.arange(6), p] >> SH))[None, :, None]
    for g in (1, 3, 5): e[np.arange(N), g, rng.integers(0, L, N)] = rng.integers(0, E, N)
    e[:, 6] = e[:, 6, :1]
    return pack(s, w, e)
def setup_inputs_ties(rng):
    kinds = rng.permutation(np.array([2, 3, 4, 5, 6, 7, 8, 8]))[:, None, None]
    shift = rng.integers(0, 30 - 2 * EPS, (8, 16, 1)); shift[:, 0] = 0; shift[:, 15] = 29 - 2 * EPS
    off = np.array([0, EPS, EPS + 1, 2 * EPS, 2 * EPS + 1, 2 * EPS + 2])
    s = 32 * (rng.random((N, 8, 16, V)) * kinds).astype(np.int64) + shift + off[rng.integers(0, 6, (N, 8, 16, V))]
    near = rng.random((N, 8, 16, Q, 16)) < 0.9
    return pack(s, inverse(rng, s, near, -EPS - 1, EPS + 2 ** SH), starts(rng, s, 0.95))
def check_inputs(d):
    bad = []
    for k, lo, hi in (("st", 0, 255), ("iv", 0, V - 1), ("e0", 0, E - 1)):
        a = np.asarray(d[k]).astype(np.float64)
        if not (np.min(a) >= lo and np.max(a) <= hi): bad.append("range of " + k)
        if np.any(a != np.floor(a)): bad.append("whole numbers in " + k)
    return bad
def carry(x):
    B = L // N
    return np.concatenate([np.roll(x[..., b * B:(b + 1) * B], b, axis=0) for b in range(N)], axis=-1)
def reference(st, iv, e0):
    s = st.astype(np.float32).astype(np.int64).reshape(N, 8, 16, V); w = iv.astype(np.int64).reshape(N, 8, 16, E)
    e = np.stack([gentries(x) for x in e0]).astype(np.int64)
    row = np.arange(16)[:, None]; lane = np.arange(L)
    core = row == (e >> LQ)[:, :, None]; kl = np.where(core, ((e & (Q - 1)) << SH)[:, :, None], 0)
    p0 = np.zeros((N, 8, 16, L), np.int64); p1 = np.zeros((N, 8, 16, L), np.int64); n = np.zeros((N, 8, L), np.int64); a = np.zeros((N, 8, L), np.int64)
    for step in range(RO):
        if step > 0: e, core, kl, p0, p1, n, a = [carry(x) for x in (e, core, kl, p0, p1, n, a)]
        c = np.take_along_axis(w, e[:, :, None], 3)
        y = np.take_along_axis(s[:, :, None], c[:, :, :, None], 4)
        el = np.all((np.abs(y - kl[:, :, None]) <= EPS) | ~core[:, :, None], axis=3)
        m = (np.abs(y - p0[:, :, None]) <= EPS) & (n > 0)[:, :, None, None]
        m = m | ((np.abs(y - p1[:, :, None]) <= EPS) & (n > 1)[:, :, None, None])
        m = m & ~core[:, :, None] & el[:, :, :, None]
        ok = el & ~np.any(m, axis=3)
        join = np.any(ok, axis=2); some = np.any(el, axis=2); grow = some & ~join; dead = ~some; full = join & (n == 2)
        pr = np.argmax(np.add.reduce(m.astype(np.int64), axis=2), axis=2)
        kr = np.argmax(np.take_along_axis(m, pr[:, :, None, None], 3)[:, :, :, 0], axis=2)
        j = np.where(join, np.argmax(ok, axis=2), kr)
        z = np.take_along_axis(y, j[:, :, None, None], 2)[:, :, 0]
        lab = np.take_along_axis(z, pr[:, :, None], 2)[:, :, 0]
        d = np.repeat((e - (e & (L - 1)) + lane)[:, :, None], 16, axis=2); old = np.take_along_axis(w, d, 3)
        new = (37 * np.take_along_axis(c, j[:, :, None], 2) + (e + a)[:, :, None]) & (V - 1)
        np.put_along_axis(w, d, np.where((row == j[:, :, None]) & join[:, :, None], new, old), 3)
        f = np.minimum(np.minimum(p0, p1), z); q = np.add.reduce(f, axis=2) & 15; lq = np.take_along_axis(f, q[:, :, None], 2)[:, :, 0]
        s0 = (n > 0) & (np.abs(np.take_along_axis(p0, pr[:, :, None], 2)[:, :, 0] - lab) <= EPS)
        s1 = (n > 1) & (np.abs(np.take_along_axis(p1, pr[:, :, None], 2)[:, :, 0] - lab) <= EPS)
        e = np.where(dead, (5 * e + 1 + a) & (E - 1), np.where(full, Q * q + (lq >> SH), np.where(grow, Q * pr + (lab >> SH), e)))
        again = dead | full; one = again[:, :, None]; enter = (row == pr[:, :, None]) & grow[:, :, None]; first = row == (e >> LQ)[:, :, None]
        core = np.where(one, first, core | enter)
        kl = np.where(one, np.where(dead, (e & (Q - 1)) << SH, lq)[:, :, None], np.where(enter, lab[:, :, None], kl))
        p0 = np.where((join & (n == 0))[:, :, None], z, np.where((grow & ~s0)[:, :, None], p1, p0))
        p1 = np.where((join & (n == 1))[:, :, None], z, p1)
        n = np.where(again, 0, np.where(join, n + 1, s0.astype(np.int64) + s1)); a = a + again
    yi = w
    return {"yk": np.where(core, kl, -1).reshape(N, 128, L).astype(np.float32).astype(BF), "y0": np.where((n > 0)[:, :, None], p0, -1).reshape(N, 128, L).astype(np.float32).astype(BF),
            "y1": np.where((n > 1)[:, :, None], p1, -1).reshape(N, 128, L).astype(np.float32).astype(BF), "ye": np.stack([gtable(x) for x in e]).astype(np.float32),
            "ya": np.stack([gtable(x) for x in a]).astype(np.float32), "yi": np.ascontiguousarray(yi).reshape(N, 128, -1).astype(np.float32)}

@@ -1,0 +1,723 @@
+import math
+from concourse.bass import DstId, RemoteDMATransfer
+from concourse.mybir import AluOpType as OP, AxisListType, ActivationFunctionType as AF
+
+N, STEPS, LC = 4, 4, 128
+LANE0 = (128, 0)
+CM = 1.5 * 2 ** 27
+SC, LAM = 1.75, 0.8125
+NEG = -131.0
+
+SCALED = {"i1": 1.0, "in1": -1.0, "i15": 1.5, "in15": -1.5, "ilam": LAM, "inls": -LAM * SC, "ih": 0.5,
+          "in512": -512.0, "i1k": 1024.0, "in1k": -1024.0, "in32": -32.0, "i384": 384.0, "in384": -384.0, "in768": -768.0,
+          "i8": 8.0, "i16k": 16384.0}
+VSHARE, DV, ABS2, EARLY, GP, BIAS = (
+    {(0, 0): 64, (0, 1): 64, (1, 0): 48, (1, 1): 16, (2, 0): 32, (2, 1): 16, (3, 0): 16, (3, 1): 64}, {(0, 0): [0, 0, 0, 0], (0, 1): [0, 0, 0, 0], (1, 0): [0, 0, 0, 0], (1, 1): [0, 0, 1, 0], (2, 0): [0, 0, 0, 0], (2, 1): [0, 0, 0, 1], (3, 0): [0, 0, 0, 0], (3, 1): [1, 0, 0, 0]}, {(0, 0): [1, 0, 0, 1], (0, 1): [1, 1, 1, 1], (1, 0): [0, 0, 0, 1], (1, 1): [1, 0, 0, 0], (2, 0): [0, 0, 1, 0], (2, 1): [1, 1, 0, 1], (3, 0): [0, 0, 1, 1], (3, 1): [1, 0, 0, 0]}, {(0, 0): 0, (0, 1): 1, (1, 0): 0, (1, 1): 1, (2, 0): 1, (2, 1): 1, (3, 0): 0, (3, 1): 0}, [32, 100.0], [[-4300.0, -1000.0, 18800.0, 3300, -4600.0, 3700, 300.0, 5900.0], [1500.0, -4700.0, 11400.0, 1900, 300.0, -400, -4500.0, -300.0], [600.0, 6600.0, -600.0, 7800, 2000.0, 12900, -2600.0, 1300.0], [-7100.0, 8600.0, 400.0, 900, -2200.0, 18800, 4500.0, -13700.0], [-4000, 0, 0, 0, 0, 0, 0, 0]])
+NCS = {(s, c): [0, 0, 0, 0] for s in range(STEPS) for c in range(2)}
+MATS = list(SCALED) + ["inp", "irow", "w2h", "bd", "bdbig", "bdh", "bd1k", "bd256", "w1", "warg", "w2", "wpw", "ones"]
+MOFF = {m: 128 * i for i, m in enumerate(MATS)}
+
+SCRATCH = {
+    "tab": ("sbuf", [128, 8192], "bfloat16"), "ivi": ("sbuf", [128, 1024], "int32"), "wl": ("sbuf", [128, 1024], "float32"),
+    "e0i": ("sbuf", [128, 16], "int32"), "mats": ("sbuf", [128, 128 * len(MATS)], "bfloat16"),
+    "zz": ("sbuf", [128, 4 * 144], "bfloat16"), "iot": ("sbuf", [128, 1032], "float32"), "tk": ("sbuf", [128, 1024], "bfloat16"),
+    "tmpb": ("sbuf", [128, 80], "bfloat16"),
+    "cols": ("sbuf", [128, 16], "float32"), "coli": ("sbuf", [128, 8], "int32"), "cf": ("sbuf", [128, 512], "float32"),
+    "cb": ("sbuf", [128, 512], "bfloat16"), "basel": ("sbuf", [128, 8], "bfloat16"), "lanel": ("sbuf", [128, 16], "float32"),
+    "con": ("sbuf", [128, 3 * 56], "float32"), "thl": ("sbuf", [128, 32], "float32"),
+    "oyk": ("sbuf", [128, 256], "bfloat16"), "oy0": ("sbuf", [128, 256], "bfloat16"), "oy1": ("sbuf", [128, 256], "bfloat16"),
+    "oye": ("sbuf", [128, 16], "float32"), "oya": ("sbuf", [128, 16], "float32"),
+}
+for _b in range(8):
+    SCRATCH["ps%d" % _b] = ("psum", [128, 512], "float32")
+for _k in range(3):
+    SCRATCH["aa%d" % _k] = ("sbuf", [128, 512], "bfloat16")
+    SCRATCH["nc%d" % _k] = ("sbuf", [128, 512], "bfloat16")
+for _k in range(2):
+    SCRATCH["ab%d" % _k] = ("sbuf", [128, 512], "bfloat16")
+    SCRATCH["dd%d" % _k] = ("sbuf", [128, 512], "float32")
+for _c in range(2):
+    SCRATCH["yy%d" % _c] = ("sbuf", [128, 2048], "bfloat16")
+    SCRATCH["me%d" % _c] = ("sbuf", [128, 2048], "bfloat16")
+    SCRATCH["c16_%d" % _c] = ("sbuf", [128, 128], "uint16")
+    SCRATCH["l16_%d" % _c] = ("sbuf", [128, 72], "uint16")
+    SCRATCH["li%d" % _c] = ("sbuf", [128, 64], "int32")
+    SCRATCH["lf%d" % _c] = ("sbuf", [128, 128], "float32")
+    SCRATCH["lq%d" % _c] = ("sbuf", [128, 64], "bfloat16")
+    SCRATCH["rf%d" % _c] = ("sbuf", [128, 128 * 6], "float32")
+    SCRATCH["ri%d" % _c] = ("sbuf", [128, 128 * 4], "int32")
+    SCRATCH["rb%d" % _c] = ("sbuf", [128, 128 * 15], "bfloat16")
+    SCRATCH["stk%d" % _c] = ("sbuf", [128, 128 * 8], "bfloat16")
+    for _s in range(STEPS):
+        SCRATCH["win%d%d" % (_s, _c)] = ("sbuf", [128, 1168], "bfloat16")
+        SCRATCH["el%d%d" % (_s, _c)] = ("sbuf", [128, 16], "float32")
+        SCRATCH["sb%d%d" % (_s, _c)] = ("sbuf", [128, 384], "bfloat16")
+        SCRATCH["sl%d%d" % (_s, _c)] = ("sbuf", [128, 16], "float32")
+
+SEMAPHORES = (["qV", "qS", "qP", "qG", "sent", "ld0", "ld1", "ld2", "outs"]
+              + ["ar%s%d%d" % (k, s, c) for k in "lr" for s in range(1, STEPS) for c in range(2)])
+
+CY = 0.83 * 1.2
+PECY = 0.46
+FIX, HOP = 60.0, 120.0
+GA, SCA = 1.6, 3.8
+
+
+def A(name, lo, n, step=1):
+    return (name, lo, lo + (n - 1) * step + 1, step)
+
+
+def IND(win, off):
+    return ("ind", win, off)
+
+
+def cnt(a):
+    if a[0] == "ind":
+        return 16 * cnt(a[2])
+    return (a[2] - a[1] - 1) // a[3] + 1
+
+
+def two(a):
+    return a[0] != "ind" and SCRATCH[a[0]][2] in ("bfloat16", "uint16")
+
+
+def isps(a):
+    return a[0] != "ind" and SCRATCH[a[0]][0] == "psum"
+
+
+def flat(xs):
+    out = []
+    for a in xs:
+        if not isinstance(a, tuple):
+            continue
+        if a[0] == "ind":
+            out += [a[1], a[2]]
+        else:
+            out.append(a)
+    return out
+
+
+def build():
+    ops = []
+
+    def add(eng, call, outs, ins, cost, sem=None, lat=0.0):
+        w = []
+        r = flat(ins)
+        for a in outs:
+            if a[0] == "ind":
+                w.append(a[1])
+                r.append(a[2])
+            else:
+                w.append(a)
+        ops.append({"eng": eng, "call": call, "w": w, "r": r, "cost": cost, "sem": sem, "lat": lat})
+
+    def ecost(out, ins, base):
+        n = cnt(ins[0]) if ins else cnt(out)
+        if out[0] == "ind":
+            return FIX + n * SCA * CY
+        if ins and ins[0][0] == "ind":
+            return FIX + n * GA * CY
+        return FIX + max(n * base, 16) * CY
+
+    def cp(out, a):
+        add("V", lambda q, R, X: q.tensor_copy(R(out), R(a)), [out], [a], ecost(out, [a], 0.5 if two(out) and two(a) else 1))
+
+    def ts(out, a, s1, o1, s2=None, o2=None):
+        def call(q, R, X):
+            if o2 is None:
+                return q.tensor_scalar(R(out), R(a), R(s1), None, o1)
+            return q.tensor_scalar(R(out), R(a), R(s1), R(s2), o1, o2)
+        add("V", call, [out], [a, s1, s2], ecost(out, [a], 0.5 if two(out) and two(a) else 1))
+
+    def tt(out, a, b, o):
+        add("V", lambda q, R, X: q.tensor_tensor(R(out), R(a), R(b), o), [out], [a, b],
+            ecost(out, [a], 1 if isps(a) or isps(b) else 2))
+
+    def ms(out, v):
+        add("V", lambda q, R, X: q.memset(R(out), v), [out], [], ecost(out, [], 0.5 if two(out) else 1))
+
+    def act(out, a, f, bias=None, scale=1.0, extra=0.0):
+        def call(q, R, X):
+            if bias is None:
+                return q.activation(R(out), R(a), f, scale=R(scale))
+            return q.activation(R(out), R(a), f, bias=R(bias), scale=R(scale))
+        add("S", call, [out], [a, bias, scale], ecost(out, [a], 1) + extra)
+
+    def mm(items):
+        def call(q, R, X):
+            last = None
+            for o, l, r, st, sp in items:
+                last = q.matmul(R(o), R(l), R(r), st, sp)
+            return last
+        add("P", call, [x[0] for x in items], [x[1] for x in items] + [x[2] for x in items],
+            20 + sum(max(64, cnt(x[2])) * PECY + 4 for x in items))
+
+    def grp(out, terms, start=True, stop=True):
+        return [(out, l, r, start and i == 0, stop and i == len(terms) - 1) for i, (l, r) in enumerate(terms)]
+
+    def iota(out, pat, base, cm):
+        def call(q, R, X):
+            if SCRATCH[out[0]][2] == "int32":
+                return q.iota(R(out), pat, base, cm)
+            return q.iota(R(out), pat, base, cm, allow_small_or_imprecise_dtypes=True)
+        add("G", call, [out], [], 130 + 2 * cnt(out) * CY)
+
+    def M(name):
+        return A("mats", MOFF[name], 128)
+
+    def Z(t, k):
+        return A("zz", 144 * t + 15 - k, 128)
+
+    def col(i):
+        return A("cols", i, 1)
+
+    add("Y", lambda q, R, X: q.dma_start(R(A("e0i", 0, 16)), X["T"].e0[:]), [A("e0i", 0, 16)], [], 60, sem=("ld0", 16), lat=2200)
+    add("Y", lambda q, R, X: q.dma_start(R(A("ivi", 0, 1024)), X["T"].iv[:]), [A("ivi", 0, 1024)], [], 60, sem=("ld1", 16), lat=3500)
+    add("Y", lambda q, R, X: q.dma_start(R(A("tab", 0, 8192)), X["T"].st[:]), [A("tab", 0, 8192)], [], 60, sem=("ld2", 16), lat=8000)
+
+    P, G16, PW, NPW, IPW, K16, P64, TKC, NP, G = range(10)
+    iota(A("coli", 0, 1), [[1, 1]], 0, 1)
+    iota(A("iot", 0, 1032), [[1, 1032]], 0, 0)
+    iota(A("cf", 0, 128), [[1, 8], [0, 16]], 0, 0)
+    iota(A("cf", 128, 128), [[0, 8], [1, 16]], 0, 0)
+    iota(A("cf", 256, 128), [[1, 128]], 0, -1)
+    ts(A("coli", 1, 1), A("coli", 0, 1), 15, OP.bitwise_and)
+    ts(A("coli", 2, 1), A("coli", 0, 1), 4, OP.arith_shift_right)
+    cp(col(P), A("coli", 1, 1))
+    cp(col(G), A("coli", 2, 1))
+    ts(col(G16), col(G), 16.0, OP.mult, 15.0, OP.add)
+    ts(col(K16), col(P), 16.0, OP.add)
+    ts(col(P64), col(P), 64.0, OP.mult, -160.0, OP.add)
+    ts(col(NP), col(P), -1.0, OP.mult)
+    act(A("tmpb", 64, 1), col(P), AF.Exp, scale=math.log(2.0), extra=1300.0)
+    act(A("tmpb", 66, 1), col(P), AF.Exp, bias=15 * math.log(2.0), scale=-math.log(2.0))
+    cp(col(PW), A("tmpb", 64, 1))
+    cp(col(IPW), A("tmpb", 66, 1))
+    ts(A("cf", 432, 16), A("cf", 128, 16), col(P), OP.is_equal)
+    ts(col(NPW), col(PW), -1.0, OP.mult)
+    ts(M("i1"), A("cf", 256, 128), 0.0, OP.is_equal)
+    ts(M("bd"), A("cf", 0, 128), col(G), OP.is_equal)
+    for m, v in SCALED.items():
+        if m != "i1":
+            act(M(m), M("i1"), AF.Copy, scale=float(v))
+    ts(M("inp"), M("i1"), col(NP), OP.mult)
+    ts(M("irow"), M("i1"), col(P64), OP.mult)
+    for m, v in (("bdbig", 2.0 ** 96), ("bdh", 2.0 ** -12), ("bd1k", 1024.0), ("bd256", 256.0), ("w2", col(NPW)), ("wpw", col(IPW))):
+        ts(M(m), M("bd"), v, OP.mult)
+    ms(M("ones"), 1.0)
+    ts(A("cb", 0, 128), A("cf", 128, 128), col(P), OP.is_gt, -1.0, OP.mult)
+    tt(A("cb", 128, 128), A("cb", 0, 128), M("bd"), OP.mult)
+    tt(M("w1"), A("cb", 128, 128), M("i1"), OP.add)
+    ts(A("cb", 256, 128), A("cb", 0, 128), -63.0 / 32, OP.mult, 1.0 / 32, OP.add)
+    tt(A("cb", 384, 128), A("cb", 256, 128), M("bd"), OP.mult)
+    ts(A("cb", 0, 128), M("i1"), -33.0 / 32, OP.mult)
+    tt(M("warg"), A("cb", 384, 128), A("cb", 0, 128), OP.add)
+    ts(A("zz", 0, 144), A("iot", 0, 144), col(G16), OP.is_equal, col(PW), OP.mult)
+    ts(A("zz", 144, 144), A("iot", 0, 144), col(G16), OP.is_equal)
+    ts(A("zz", 288, 144), A("iot", 0, 144), col(G16), OP.is_equal, col(K16), OP.mult)
+    act(A("zz", 432, 144), A("zz", 0, 144), AF.Copy, scale=0.5)
+    act(M("w2h"), M("w2"), AF.Copy, scale=-0.5)
+    iota(A("tmpb", 0, 64), [[4, 64]], 6, 0)
+    for r in range(16):
+        if r % 2:
+            ts(A("tk", 64 * r, 64), A("tmpb", 0, 64), A("cf", 432 + r, 1), OP.mult)
+        else:
+            act(A("tk", 64 * r, 64), A("tmpb", 0, 64), AF.Copy, scale=A("cf", 432 + r, 1))
+    ts(A("cf", 496, 8), A("iot", 0, 8), 16.0, OP.mult, col(P), OP.add)
+    ts(A("basel", 0, 8), A("cf", 496, 8), 16.0, OP.mult, -16.0, OP.add)
+    for c in range(2):
+        ts(A("lanel", 8 * c, 8), A("cf", 496, 8), float(LANE0[c]), OP.add, 1.0 / 256, OP.mult)
+    ms(A("thl", 8, 24), 0.5)
+    ts(A("thl", 0, 8), A("cf", 496, 8), 16.0, OP.mult)
+    JJ, FF, JN0, NF = range(4)
+    ST2 = {
+        0: [(768, 1, [("in384", JJ)]), (768, 1, [("in384", JJ)]), (386, 1, [("in384", JJ)]),
+            (1, 0, [("in1", JJ)]), (0, 0, [("i1", JJ)]), (1, 0, [("in1", JJ)])],
+        1: [(768, 1, [("in768", JJ), ("i384", JN0)]), (768, 1, [("in768", JJ), ("i384", FF)]), (386, 1, [("in384", JJ)]),
+            (1, 0, [("in1", JJ)]), (0, 0, [("i1", FF)]), (1, 0, [("in1", JJ)])],
+        2: [(1537, 1, [("in768", JJ), ("in1", FF), ("i384", JN0), ("in768", NF)]),
+            (1152, 1, [("in768", JJ), ("i384", FF), ("in384", NF)]),
+            (1154, 1, [("in384", JJ), ("in768", NF)]),
+            (1, 0, [("in1", JJ)]), (-1, 0, [("i1", FF), ("i1", NF)]), (2, 0, [("in1", JJ), ("in1", NF)])],
+    }
+    for t in range(3):
+        for i, (c0, lane, _) in enumerate(ST2[t]):
+            act(A("con", 56 * t + 8 * i, 8), A("cf", 496, 8), AF.Identity, bias=float(c0), scale=3.0 * lane)
+    cp(A("wl", 0, 1024), A("ivi", 0, 1024))
+    for s in range(STEPS):
+        for c in range(2):
+            if s == 0:
+                ms(A("win0%d" % c, 0, 384), NEG)
+            iota(A("win%d%d" % (s, c), 384, 784), [[0, 784]], int(NEG), 0)
+    for c in range(2):
+        ms(A("el0%d" % c, 0, 16), 0.0)
+        cp(A("el0%d" % c, 0, 8, 2), A("e0i", LANE0[c] // 16, 8))
+
+    WL, TAB = A("wl", 0, 1024), A("tab", 0, 8192)
+    ring = {"b": 0, "t": 0, "a": 0, "d": 0, "e": 0}
+    RB, TB = "ps3", "ps4"
+    slots = [("ps5", 128), ("ps6", 128), ("ps7", 0), ("ps5", 256), ("ps6", 256), ("ps7", 128), ("ps5", 384), ("ps6", 384)]
+
+    def slot(n=128):
+        b, o = slots[ring["t"] % len(slots)]
+        ring["t"] += 1
+        return A(b, o, n)
+
+    def names(s, c):
+        w = "win%d%d" % (s, c)
+        d = {"P0": A(w, 0, 128, 3), "P1": A(w, 1, 128, 3), "K": A(w, 2, 128, 3), "z": A(w, 384, 128, 3), "Kd": A(w, 386, 128, 3),
+             "win": A(w, 0, 1168), "e": A("el%d%d" % (s, c), 0, 8, 2), "A": A("el%d%d" % (s, c), 1, 8, 2),
+             "c16": "c16_%d" % c, "Y": "yy%d" % c, "me": "me%d" % c}
+        for i, x in enumerate(["e16", "ea16", "ed16", "d16", "j16", "o0", "o1", "oK", "ja16"]):
+            d[x] = A("l16_%d" % c, 8 * i, 8)
+        for i, x in enumerate(["e5", "ed", "b"]):
+            d[x] = A("li%d" % c, 8 * i, 8)
+        d["c1"], d["c2"] = A("lf%d" % c, 24, 8), A("lf%d" % c, 112, 8)
+        d["df"], d["m1"], d["m2"] = A("lf%d" % c, 0, 8), A("lf%d" % c, 8, 8), A("lf%d" % c, 16, 8)
+        d["ea"], d["e4"] = A("lf%d" % c, 96, 8), A("lf%d" % c, 104, 8)
+        for i, x in enumerate(["x0", "old", "dv", "t", "Rs", "r"]):
+            d[x] = A("rf%d" % c, 128 * i, 128)
+        d["dv"] = A(RB, 128 + 128 * c, 128)
+        for i, x in enumerate(["xi", "v", "bt", "bt2"]):
+            d[x] = A("ri%d" % c, 128 * i, 128)
+        for i, x in enumerate(["cr", "thq", "mid", "h", "okb", "X", "oh", "gb", "F", "ohq", "cB", "y1p", "ad", "zg", "E"]):
+            d[x] = A("rb%d" % c, 128 * i, 128)
+        for i, x in enumerate(["J", "f", "jn0", "nf", "row", "lab", "s0", "s1"]):
+            d[x] = A("stk%d" % c, 128 * i, 128)
+        return d
+
+    def early(s, c):
+        d = names(s, c)
+        cp(d["e16"], d["e"])
+        cp(A(d["c16"], 0, 128), IND(WL, d["e16"]))
+        nv = VSHARE[(s, c)]
+        pieces = []
+        lo = 0
+        if nv:
+            pieces.append(("V", 0, nv))
+        lo = nv
+        while lo < 128:
+            hi = min(128, lo + GP[0])
+            pieces.append(("S", lo, hi - lo))
+            lo = hi
+        for e, lo, n in pieces:
+            o, i = A(d["Y"], 16 * lo, 16 * n), IND(TAB, A(d["c16"], lo, n))
+            if e == "V":
+                cp(o, i)
+            else:
+                act(o, i, AF.Copy)
+        if s == 0:
+            act(d["mid"], IND(A("tk", 0, 1024), d["e16"]), AF.Identity, bias=-6.0)
+            ts(d["K"], d["mid"], -125.0, OP.add)
+        tt(d["ea"], d["e"], d["A"], OP.add)
+        cp(d["ea16"], d["ea"])
+        act(d["e4"], d["e"], AF.Identity, bias=1.0, scale=4.0)
+        tt(d["e5"], d["e4"], d["ea"], OP.add)
+        ts(d["ed"], d["e5"], 1023, OP.bitwise_and)
+        cp(d["ed16"], d["ed"])
+        ts(d["b"], d["e"], 1.0 / 256, OP.mult, -0.498, OP.add)
+        tt(d["df"], d["b"], A("lanel", 8 * c, 8), OP.add)
+        ts(d["d16"], d["df"], 256.0, OP.mult)
+        act(d["x0"], IND(WL, d["e16"]), AF.Copy, scale=37.0)
+        act(d["old"], IND(WL, d["d16"]), AF.Copy)
+        tt(d["xi"], IND(A("iot", 0, 1032), d["ea16"]), d["x0"], OP.add)
+        ts(d["v"], d["xi"], 8191, OP.bitwise_and)
+        tt(d["dv"], d["v"], d["old"], OP.subtract)
+        act(d["Kd"], IND(A("tk", 0, 1024), d["ed16"]), AF.Identity, bias=NEG)
+
+    def bulk(s, c):
+        d = names(s, c)
+        ts(d["cr"], d["K"], -128.0, OP.is_gt)
+        if s > 0:
+            ts(d["thq"], d["K"], -128.0, OP.is_lt, 10.0 / 1024, OP.max)
+            u = A("ps5", 0, 128)
+            mm(grp(u, [(M("ih"), d["P0"]), (M("ih"), d["P1"]), (M("in512"), d["cr"])]))
+            tt(d["mid"], u, d["K"], OP.max)
+            if s > 1:
+                hh = A("ps6", 0, 128)
+                mm(grp(hh, [(M("i1"), d["P0"]), (M("in1"), d["P1"])]))
+                act(d["h"], hh, AF.Abs, scale=0.5)
+            anyv = any(DV[(s, c)])
+            items = [(A(TB, 128 * j, 128), M("i1k"), d["thq"], True, True) for j in range(2 if anyv else 4)]
+            if anyv:
+                items.append((A(TB, 256, 128), M("i1"), d["mid"], True, True))
+            mm(items)
+        R = A(RB, 0, 128)
+        for b in range(4):
+            if s > 0 and DV[(s, c)][b]:
+                bank = "dd%d" % (ring["d"] % 2)
+                ring["d"] += 1
+                for j in range(4):
+                    tt(A(bank, 128 * j, 128), A(d["Y"], 4 * b + j, 128, 16), A(TB, 256, 128), OP.subtract)
+            else:
+                bank = "ps%d" % (ring["b"] % 3)
+                ring["b"] += 1
+                items = []
+                for j in range(4):
+                    items += grp(A(bank, 128 * j, 128), [(M("i15" if s == 0 else "i1"), A(d["Y"], 4 * b + j, 128, 16)),
+                                                         (M("in15" if s == 0 else "in1"), d["mid"])])
+                mm(items)
+            me = A(d["me"], 512 * b, 512)
+            if s > 0:
+                a, n = A("aa%d" % (ring["a"] % 3), 0, 512), A("nc%d" % (ring["a"] % 3), 0, 512)
+                ring["a"] += 1
+                act(a, A(bank, 0, 512), AF.Abs, bias=-125.0 * SC, scale=SC)
+                if NCS[(s, c)][b]:
+                    bank = "ps%d" % (ring["b"] % 3)
+                    ring["b"] += 1
+                    mm([(A(bank, 0, 512), M("i1"), a, True, False)]
+                       + [(A(bank, 128 * j, 128), M("in1k"), d["thq"], False, j == 3) for j in range(4)])
+                    act(n, A(bank, 0, 512), AF.Relu)
+                elif anyv:
+                    for hf in range(2):
+                        tt(A(n[0], 256 * hf, 256), A(a[0], 256 * hf, 256), A(TB, 0, 256), OP.is_ge)
+                else:
+                    tt(n, a, A(TB, 0, 512), OP.is_ge)
+                bank = "ps%d" % (ring["b"] % 3)
+                ring["b"] += 1
+                x = A(bank, 0, 512)
+                items = [(x, M("ilam"), a, True, False)]
+                if s > 1:
+                    items += [(A(bank, 128 * j, 128), M("inls"), d["h"], False, False) for j in range(4)]
+                items += [(x, M("bd1k"), n, False, True)]
+                mm(items)
+            sg = s == 1 and EARLY[(s, c)]
+            if sg:
+                act(me, A(bank, 0, 512), AF.Sign, bias=7.9, scale=-1.0)
+            elif ABS2[(s, c)][b]:
+                a2 = A("ab%d" % (ring["e"] % 2), 0, 512)
+                ring["e"] += 1
+                act(a2, A(bank, 0, 512), AF.Abs)
+                ts(me, a2, 7.9, OP.is_le)
+            else:
+                ts(me, A(bank, 0, 512), CM, OP.add, CM, OP.is_equal)
+            terms = [(M("w2"), d["cr"])] if b == 0 else []
+            if sg and b == 0:
+                terms.append((M("w2h"), M("ones")))
+            terms += [(Z(3 if sg else 0, 4 * b + j), A(d["me"], 512 * b + 128 * j, 128)) for j in range(4)]
+            mm(grp(R, terms, start=b == 0, stop=b == 3))
+
+    def join(s, c):
+        d = names(s, c)
+        R = A(RB, 0, 128)
+        ts(d["okb"], R, 0.0, OP.is_equal)
+        if s > 0:
+            act(d["Rs"], R, AF.Relu)
+        u1 = slot()
+        mm(grp(u1, [(M("w1"), d["okb"])]))
+        act(d["f"], u1, AF.Relu)
+        tt(d["t"], d["f"], d["dv"], OP.mult)
+        tt(IND(WL, d["d16"]), d["old"], d["t"], OP.add)
+
+    def tolist(out, zt, src, n, extra):
+        items = [(out, Z(zt, r), A(src[0], src[1] + r, n, 16), r == 0, r == 15) for r in range(16)]
+        items[1:1] = [(A(out[0], out[1], cnt(x)), m, x, False, False) for x, m in extra]
+        mm(items)
+
+    def tail(s, c):
+        d = names(s, c)
+        last = s == STEPS - 1
+        J = d["f"]
+        if s > 0:
+            J = d["J"]
+            cn = slot()
+            sg = s == 1 and EARLY[(s, c)]
+            mm(grp(cn, [(M("in32"), d["cr"])] + [(M("ih" if sg else "i1"), A(d["me"], 128 * k, 128)) for k in range(16)]))
+            act(d["X"], cn, AF.Exp, bias=8 * math.log(64.0) if sg else None, scale=math.log(64.0))
+            rg = slot()
+            mm(grp(rg, [(M("warg"), d["X"]), (M("bdbig"), d["f"])]))
+            ts(d["oh"], rg, -8.0, OP.is_lt)
+            pw = slot()
+            mm(grp(pw, [(M("wpw"), d["oh"])]))
+            tt(d["bt"], pw, d["Rs"], OP.mult)
+            ts(d["bt2"], d["bt"], 32768, OP.bitwise_and)
+            ts(d["gb"], d["bt2"], 0.5, OP.is_gt)
+            u2 = slot()
+            mm(grp(u2, [(M("w1"), d["gb"])]))
+            tt(J, u2, d["f"], OP.max)
+            w0 = slot()
+            mm(grp(w0, [(M("bd"), d["f"]), (M("in1"), d["P0"])]))
+            act(d["jn0"], w0, AF.Relu, bias=NEG / 16, scale=1.0 / 16)
+        t = min(s, 2)
+        YW = A(d["Y"], 0, 2048)
+        base = (A("basel", 0, 8), M("i1"))
+        zg = d["z"]
+        if s > 1:
+            w2 = slot()
+            mm(grp(w2, [(M("bd"), d["f"]), (M("bdh"), d["h"])]))
+            ts(d["nf"], w2, 1.0, OP.is_le, 1.0 / 16, OP.mult)
+            if EARLY[(s, c)]:
+                l0 = slot(8)
+                tolist(l0, 2, d["f"], 8, [base])
+                cp(d["ja16"], l0)
+                act(d["z"], IND(YW, d["ja16"]), AF.Identity, bias=-125.0)
+                zg = d["zg"]
+        nq = 8 * (1, 3, 4)[t]
+        l1 = slot(nq)
+        tolist(l1, 2, J, nq, [base])
+        cp(d["j16"], A(l1[0], l1[1], 8))
+        act(zg, IND(YW, d["j16"]), AF.Identity, bias=-125.0)
+        lq, lf = "lq%d" % c, "lf%d" % c
+        tt(A(lq, 0, nq), l1, A("thl", 0, nq), OP.is_ge)
+        q2 = slot(48)
+        items = []
+        for i, (_, _, terms) in enumerate(ST2[t]):
+            items += grp(A(q2[0], q2[1] + 8 * i, 8), [(M(m), A(lq, 8 * x, 8)) for m, x in terms])
+        mm(items)
+        tt(A(lf, 32, 48), q2, A("con", 56 * t, 48), OP.add)
+        dead, keep, again = [A(lf, 32 + 8 * i, 8) for i in (3, 4, 5)]
+        sl, sb = "sl%d%d" % (s, c), "sb%d%d" % (s, c)
+        lo = LANE0[c]
+        en = A("oye", lo // 16, 8) if last else A(sl, 0, 8, 2)
+        tt(d["m1"], dead, d["ed"], OP.mult)
+        tt(d["m2"], keep, d["e"], OP.mult)
+        tt(en if s == 0 else d["c1"], d["m1"], d["m2"], OP.add)
+        tt(A("oya", lo // 16, 8) if last else A(sl, 1, 8, 2), again, d["A"], OP.add)
+        if s > 1:
+            m01 = slot()
+            mm(grp(m01, [(M("ih"), d["P0"]), (M("ih"), d["P1"]), (M("in1"), d["h"]), (M("i16k"), d["nf"])]))
+            tt(d["F"], m01, d["z"], OP.min)
+            v = slot()
+            mm(grp(v, [(M("inp"), M("ones")), (M("i8"), d["nf"]), (M("bd"), d["F"])]))
+            ts(d["r"], v, CM, OP.add, CM, OP.subtract)
+            tt(d["ohq"], v, d["r"], OP.is_equal)
+            if EARLY[(s, c)]:
+                dz = slot()
+                mm(grp(dz, [(M("in1"), d["z"]), (M("i1"), d["F"])]))
+                tt(d["E"], dz, d["ohq"], OP.mult)
+            items = []
+            for i, p in enumerate(("P0", "P1")):
+                items += grp(A("ps7", 256 + 128 * i, 128), [(M("i15"), d[p]), (M("i1k"), d["oh"]), (M("in15"), zg)])
+            mm(items)
+            ts(A(d["s0"][0], d["s0"][1], 256), A("ps7", 256, 256), CM - 1024, OP.add, CM, OP.is_equal)
+        if s > 0:
+            cand = slot()
+            if s == 1:
+                mm(grp(cand, [(M("i1k"), d["oh"]), (M("i1"), zg)]))
+            elif EARLY[(s, c)]:
+                mm(grp(cand, [(M("i1k"), d["oh"]), (M("i1k"), d["ohq"]), (M("i1"), d["E"]), (M("i1"), zg)]))
+            else:
+                mm(grp(cand, [(M("i1k"), d["oh"]), (M("i1"), d["F"]), (M("i1k"), d["ohq"])]))
+            rw = slot()
+            mm(grp(rw, [(M("irow"), d["oh"])] + ([(M("irow"), d["ohq"])] if s > 1 else [])))
+            act(d["row"], rw, AF.Copy)
+            act(d["lab"], cand, AF.Relu, bias=-65.125, scale=0.25)
+            act(d["cB"], cand, AF.Identity, bias=-1024.0)
+            l2 = slot(16 * t)
+            tolist(l2, 1, d["row"], 16 * t, [])
+            tt(d["c2"], A(l2[0], l2[1], 8), d["c1"], OP.add)
+            tt(en, A(l2[0], l2[1] + 8, 8), d["c2"], OP.add)
+        if not last:
+            send(s, c, "l", sl, "el%d%d" % (s + 1, c), 8)
+        if s > 1:
+            tt(A(lf, 32, 8), A(lf, 32, 8), A(l2[0], l2[1] + 16, 8), OP.subtract)
+            tt(A(lf, 40, 8), A(lf, 40, 8), A(l2[0], l2[1] + 24, 8), OP.add)
+        cp(A("l16_%d" % c, 40, 24), A(lf, 32, 24))
+        if not last:
+            act(A(sb, 0, 128, 3), IND(d["win"], d["o0"]), AF.Copy)
+            act(A(sb, 1, 128, 3), IND(d["win"], d["o1"]), AF.Copy)
+            if s == 0:
+                cp(A(sb, 2, 128, 3), IND(d["win"], d["oK"]))
+            else:
+                tt(A(sb, 2, 128, 3), IND(d["win"], d["oK"]), d["cB"], OP.max)
+            send(s, c, "r", sb, "win%d%d" % (s + 1, c), 192)
+        else:
+            y0, y1, yk = A("oy0", lo, 128), A("oy1", lo, 128), A("oyk", lo, 128)
+            ts(y0, IND(d["win"], d["o0"]), 125.0, OP.add, -1.0, OP.max)
+            ts(d["y1p"], IND(d["win"], d["o1"]), 125.0, OP.add, -1.0, OP.max)
+            tt(A(sb, 0, 128), IND(d["win"], d["oK"]), d["cB"], OP.max)
+            ts(yk, A(sb, 0, 128), 125.0, OP.add, -1.0, OP.max)
+            dd = slot()
+            mm(grp(dd, [(M("i1"), y0), (M("in1"), d["y1p"])]))
+            act(d["ad"], dd, AF.Abs)
+            lim = slot()
+            mm(grp(lim, [(M("in1"), M("ones")), (M("bd256"), d["ad"])]))
+            tt(y1, lim, d["y1p"], OP.min)
+
+    def send(s, c, kind, src, dst, w):
+        blocks = [(h, LANE0[c] // 64 + h) for h in range(2)]
+        far = [(h, b) for h, b in blocks if b % N]
+        name = "ar%s%d%d" % (kind, s + 1, c)
+
+        def call(q, R, X):
+            topo, T, core = X["topo"], X["T"], X["core"]
+            trs = []
+            for i, (h, b) in enumerate(far):
+                to = T.cores[(X["rank"] + b) % N]
+                eng = topo.engines(core, to)
+                k = len(eng) // len(far)
+                mask = sum(1 << e for e in eng[i * k:(i + 1) * k])
+                ad = topo.addr(to)
+                trs.append(RemoteDMATransfer(dst_ids=[DstId(rid=ad[0], pnc=ad[1])], dma_engine_mask=mask, remote_sem=T.sem[name],
+                                             src=R(A(src, h * w, w)), dst=R(A(dst, h * w, w))))
+                X["sent"][0] += k
+            return q.remote_dma_fused(trs, local_sem=T.sem["sent"])
+        add("G", call, [A(dst, h * w, w) for h, b in far], [A(src, h * w, w) for h, b in far], 700, sem=(name, "far"), lat=2500)
+        for h, b in blocks:
+            if b % N == 0:
+                cp(A(dst, h * w, w), A(src, h * w, w))
+
+    for s in range(STEPS):
+        for k, (part, c) in enumerate(((early, 0), (early, 1), (bulk, 0), (join, 0), (bulk, 1), (tail, 0), (join, 1), (tail, 1))):
+            first = len(ops)
+            part(s, c)
+            for o in ops[first:]:
+                o["bias"] = BIAS[s][k]
+
+    def store(name, buf, n):
+        add("Y", lambda q, R, X: q.dma_start(X["T"][name][:], R(A(buf, 0, n))), [], [A(buf, 0, n)], 60, sem=("outs", 16), lat=2500)
+    for name, buf, n in (("yi", "wl", 1024), ("ye", "oye", 16), ("ya", "oya", 16), ("y0", "oy0", 256), ("yk", "oyk", 256), ("y1", "oy1", 256)):
+        store(name, buf, n)
+    return ops
+
+
+def plan():
+    ops = build()
+    n = len(ops)
+    acc = {}
+    pred = [set() for _ in ops]
+    for i, o in enumerate(ops):
+        for kind, lst in (("r", o["r"]), ("w", o["w"])):
+            for a in lst:
+                for (j, k2, lo, hi, stp) in acc.get(a[0], ()):
+                    if j != i and (kind == "w" or k2 == "w") and lo < a[2] and a[1] < hi:
+                        if stp == 1 or stp != a[3] or (lo - a[1]) % stp == 0:
+                            pred[i].add(j)
+        for kind, lst in (("r", o["r"]), ("w", o["w"])):
+            for a in lst:
+                old = acc.get(a[0], [])
+                if kind == "w":
+                    old = [x for x in old if not (a[3] == 1 and a[1] <= x[2] and x[3] <= a[2])]
+                acc[a[0]] = old + [(i, kind, a[1], a[2], a[3])]
+        o["banks"] = sorted(set(a[0] for a in o["r"] + o["w"] if isps(a)))
+    succ = [[] for _ in ops]
+    for i in range(n):
+        for j in pred[i]:
+            succ[j].append(i)
+    prio = [0.0] * n
+    for i in range(n - 1, -1, -1):
+        prio[i] = ops[i]["cost"] + ops[i]["lat"] + max([prio[k] + HOP for k in succ[i]] + [0.0])
+    for i in range(n):
+        prio[i] += ops[i].get("bias", BIAS[STEPS][0])
+    left = [len(p) for p in pred]
+    ready = set(i for i in range(n) if left[i] == 0)
+    free = {e: 0.0 for e in "VSPGY"}
+    fin = [0.0] * n
+    bank = {}
+    order = []
+
+    def start(i):
+        o = ops[i]
+        t = free[o["eng"]]
+        for j in pred[i]:
+            if not (o["eng"] == "P" and ops[j]["eng"] == "P"):
+                t = max(t, fin[j] + HOP)
+        for b in o["banks"]:
+            for e, j in bank.get(b, {}).items():
+                if e != o["eng"]:
+                    t = max(t, fin[j] + HOP)
+        return t
+    while ready:
+        st = {i: start(i) for i in ready}
+        i0 = min(ready, key=lambda k: (st[k], k))
+        i = max((k for k in ready if st[k] <= st[i0] + GP[1] and ops[k]["eng"] == ops[i0]["eng"]), key=lambda k: (prio[k], -k))
+        o = ops[i]
+        o["t"] = st[i]
+        free[o["eng"]] = st[i] + o["cost"]
+        fin[i] = st[i] + o["cost"] + o["lat"]
+        for b in o["banks"]:
+            for e, j in bank.get(b, {}).items():
+                if e != o["eng"]:
+                    pred[i].add(j)
+            bank.setdefault(b, {})[o["eng"]] = i
+        order.append(i)
+        ready.discard(i)
+        for k in succ[i]:
+            left[k] -= 1
+            if left[k] == 0:
+                ready.add(k)
+    pos = {}
+    seen = {e: {} for e in "VSPGY"}
+    know = [None] * n
+    k = {e: 0 for e in "VSPGY"}
+    for i in order:
+        k[ops[i]["eng"]] += 1
+        pos[i] = k[ops[i]["eng"]]
+    need = set()
+    for i in order:
+        o = ops[i]
+        e = o["eng"]
+        waits = []
+        for j in sorted(pred[i], key=lambda x: -fin[x]):
+            p = ops[j]
+            if p["sem"] is not None:
+                key, val = ("d", j), 1
+            else:
+                if e == "P" and p["eng"] == "P":
+                    continue
+                key, val = p["eng"], pos[j]
+            if seen[e].get(key, 0) >= val:
+                continue
+            waits.append(j)
+            need.add(j)
+            for kk, vv in know[j].items():
+                if seen[e].get(kk, 0) < vv:
+                    seen[e][kk] = vv
+        o["waits"] = waits
+        o["pred"] = pred[i]
+        kn = dict(seen[e])
+        if o["sem"] is not None:
+            kn[("d", i)] = 1
+        else:
+            kn[e] = max(kn.get(e, 0), pos[i])
+        know[i] = kn
+    tot = {e: 0 for e in "VSPG"}
+    for i in order:
+        o = ops[i]
+        if o["sem"] is None and i in need:
+            tot[o["eng"]] += 1
+            o["inc"] = tot[o["eng"]]
+    return ops, order, tot, max(fin)
+
+
+PLAN = {}
+
+
+def rank_program(g, core, T, topo):
+    rank = T.rank_of(core)
+    if rank is None:
+        return
+    if "p" not in PLAN:
+        PLAN["p"] = plan()
+    ops, order, tot, _ = PLAN["p"]
+    Q = {"V": g.vector, "S": g.scalar, "P": g.tensor, "G": g, "Y": g.sync}
+    X = {"T": T, "topo": topo, "core": core, "rank": rank, "sent": [0]}
+    nfar = len(topo.engines(core, T.cores[(rank + 1) % N]))
+
+    def R(a):
+        if not isinstance(a, tuple):
+            return a
+        if a[0] == "ind":
+            return R(a[1]).indirect(R(a[2]))
+        if a[3] == 1:
+            return T[a[0]][:, a[1]:a[2]]
+        return T[a[0]][:, a[1]:a[2]:a[3]]
+    nout = 0
+    for i in order:
+        o = ops[i]
+        q = Q[o["eng"]]
+        for j in o["waits"]:
+            p = ops[j]
+            if p["sem"] is None:
+                q.wait_ge(T.sem["q" + p["eng"]], p["inc"])
+            else:
+                q.wait_ge(T.sem[p["sem"][0]], nfar if p["sem"][1] == "far" else p["sem"][1])
+        ins = o["call"](q, R, X)
+        if o["sem"] is None:
+            if "inc" in o:
+                ins.then_inc(T.sem["q" + o["eng"]], 1)
+        elif o["sem"][1] != "far":
+            ins.then_inc(T.sem[o["sem"][0]], 16)
+            nout += o["sem"][0] == "outs"
+    g.wait_ge(T.sem["sent"], X["sent"][0])
+    g.sync.wait_ge(T.sem["outs"], 16 * nout)

@@ -3,7 +3,7 @@ from concourse.bass import DstId, RemoteDMATransfer
 from concourse.mybir import AluOpType as OP, AxisListType, ActivationFunctionType as AF
 
 N, STEPS, LC = 4, 4, 128
-LANE0 = (128, 0)
+LANE0 = [0, 128]
 CM = 1.5 * 2 ** 27
 SC, LAM = 1.75, 0.8125
 NEG = -131.0
@@ -14,7 +14,15 @@ SCALED = {"i1": 1.0, "in1": -1.0, "i15": 1.5, "in15": -1.5, "ilam": LAM, "inls":
 VSHARE, DV, ABS2, EARLY, GP, BIAS = (
     {(0, 0): 64, (0, 1): 64, (1, 0): 48, (1, 1): 16, (2, 0): 32, (2, 1): 16, (3, 0): 16, (3, 1): 64}, {(0, 0): [0, 0, 0, 0], (0, 1): [0, 0, 0, 0], (1, 0): [0, 0, 0, 0], (1, 1): [0, 0, 1, 0], (2, 0): [0, 0, 0, 0], (2, 1): [0, 0, 0, 1], (3, 0): [0, 0, 0, 0], (3, 1): [1, 0, 0, 0]}, {(0, 0): [1, 0, 0, 1], (0, 1): [1, 1, 1, 1], (1, 0): [0, 0, 0, 1], (1, 1): [1, 0, 0, 0], (2, 0): [0, 0, 1, 0], (2, 1): [1, 1, 0, 1], (3, 0): [0, 0, 1, 1], (3, 1): [1, 0, 0, 0]}, {(0, 0): 0, (0, 1): 1, (1, 0): 0, (1, 1): 1, (2, 0): 1, (2, 1): 1, (3, 0): 0, (3, 1): 0}, [32, 100.0], [[-4300.0, -1000.0, 18800.0, 3300, -4600.0, 3700, 300.0, 5900.0], [1500.0, -4700.0, 11400.0, 1900, 300.0, -400, -4500.0, -300.0], [600.0, 6600.0, -600.0, 7800, 2000.0, 12900, -2600.0, 1300.0], [-7100.0, 8600.0, 400.0, 900, -2200.0, 18800, 4500.0, -13700.0], [-4000, 0, 0, 0, 0, 0, 0, 0]])
 NCS = {(s, c): [0, 0, 0, 0] for s in range(STEPS) for c in range(2)}
-MATS = list(SCALED) + ["inp", "irow", "w2h", "bd", "bdbig", "bdh", "bd1k", "bd256", "w1", "warg", "w2", "wpw", "ones"]
+SPLIT = [1, 33, 1, 0]
+VSHARE.update({(0, 0): 64, (0, 1): 64, (1, 0): 64, (1, 1): 64, (2, 0): 32, (2, 1): 16, (3, 0): 16, (3, 1): 64})
+DV.update({(1, 0): [0, 0, 0, 0], (1, 1): [0, 0, 1, 0], (2, 0): [0, 0, 0, 0], (2, 1): [0, 0, 1, 1], (3, 0): [0, 0, 1, 0], (3, 1): [1, 0, 0, 1]})
+ABS2.update({(0, 0): [1, 0, 0, 1], (0, 1): [1, 1, 1, 1], (1, 0): [0, 1, 0, 1], (1, 1): [1, 0, 1, 1], (2, 0): [0, 1, 1, 0], (2, 1): [0, 1, 0, 0],
+             (3, 0): [0, 0, 1, 1], (3, 1): [1, 0, 0, 0]})
+EARLY.update({(0, 0): 0, (0, 1): 1, (1, 0): 1, (1, 1): 1, (2, 0): 0, (2, 1): 1, (3, 0): 0, (3, 1): 1})
+CODE = "03063408090a0b021o0g000105072u0k360d1c231p1v1r0n1s1w1q042v0h1z2x30332220241u0c35372w3h3l41211t1x1y0i473u3f0m381d3i2t253z403j3d100z430v0t0x4a0s310o3o320y2y0q0u0p0r2d393k3t1j1m2f283e3c3b2c3v1e0l421l4g3x274c193g3a4h4i3w3m4j4o4l4r3y4s2g2e4m1n2k2i4k3q4p4t3r51524n4q4u55123n3p4d48504v494b4w4x262a3s53562b592l5h2h115d4y4e5a572m5e2o2j2p2q5k4z5l54585i5m5b5n5o5f5p5q5c5t5j445w5g5z155r605v5u451746612n5s2s0w5x4f2r2z1f625y646k63676l68656o69666p6m6b6a6d6c6n7r7s7t6q7u6f6s6u6y716e6r7v7w6g6h6z6v6t706i6w827x736j6x74837y76847z727e7i8075771b858688781g798q8e7a89818s8a878b8f7b8g8r8t8h1h8c0j1i8u1a8i9a997l299c9b1k8v8d8j9q7c7j8k9d0e147d8w8x8y8m9e928l9r8n9s938z9t90a09u9j8o9fa19k9g9h959v949w7k9x969y9z91a27n167f7o7g9m9l7h18a3a5977m9n0f7p7qa48pa6aca713a8ama99oad989i9pafaeagapasabaaahaoanataqauaiavajakalarawayazb8byaxbzb0b1b2blc2b3b4d7dbb5d8b9c3d9b6ddc8bmb7badac0c1c5c4c6bbbdc7cfdec9dcbccachbecbcibkbfdkbgdfbhbnbtbibpbodldgbjbqbudhbvbrdmbwckbsccdidnbxcdcedrdodjdsdpdycgdtdqdzcjducle0cycud1dvcme1eaebeceedwdxe2csczcnede3fgegcvctd0cwe4e6cxd3d4cocrcqcpehe5fhe7efeififsd2eofqeyezf6exfjftewepfkekejflg4d6erelf0fmf9fnfoeqesfrfpfuf7f1f8f2emfafvfcf3fxfbfwg5fyf4etfzg0g1g6fdg9g7g8gcgbgagdeufeeng2g3geggevghglgmgigngjf5ffgfgogpgkgqd5gte8e9grgsgugzgvgwh0gxhdh1gyheh2hbhch9h3hfidieh4iqhaitighqhrh5jjh6jlh7ikifjkilhsimh8hgirjminisioiphjhthhjnjphuivihijhkhihliwhmhniihyhvhwhxhpjqk5k7k6hohzi0i1i2k4jojri3jxk8jyi7i6iui4i5iymdkfmejsi8iai9k9jtjukgj6jajzkaibixk0ick1jvkbkcjwkikhk2k3izj0jdkjkxj3kkj1ktkvkdkuj4kwj2kykeklkzj5kmlzl2l0l3l1lpknl4kplbm0kqjflsl6l5m1lckombl7l8jgm2jbm3m9lrleldm4mclqm5l9lfliltlalglhljm6lulvj7jcm7mpj8m8lkj9jellmajilwjhlxmfmgkrlmmimhmjmqlnmrmsmtksmulomkmmmomlmnlymxmymvnjnendmwnknfmzngn0n1nhnlnzninmn2n4nnp0ntnun5n3n6noo0nxnpnvnyo1n7nqnrnwocn8nansodo2nbn9nco3o4oeo5ofohogo6ojomokoiolo7ono9o8oboooap2oropotosouoqp1ovoyoxp5ozp4owp3"
+ORDER = [int(CODE[_i:_i + 2], 36) for _i in range(0, len(CODE), 2)]
+MATS = list(SCALED) + ["inp", "irow", "w2h", "bd", "bdbig", "bdh", "bd1k", "bdn", "w1", "warg", "w2", "wpw", "ones"]
 MOFF = {m: 128 * i for i, m in enumerate(MATS)}
 
 SCRATCH = {
@@ -58,7 +66,7 @@ SEMAPHORES = (["qV", "qS", "qP", "qG", "sent", "ld0", "ld1", "ld2", "outs"]
               + ["ar%s%d%d" % (k, s, c) for k in "lr" for s in range(1, STEPS) for c in range(2)])
 
 CY = 0.83 * 1.2
-PECY = 0.46
+PECY = 0.42 * 1.2
 FIX, HOP = 60.0, 120.0
 GA, SCA = 1.6, 3.8
 
@@ -202,7 +210,7 @@ def build():
             act(M(m), M("i1"), AF.Copy, scale=float(v))
     ts(M("inp"), M("i1"), col(NP), OP.mult)
     ts(M("irow"), M("i1"), col(P64), OP.mult)
-    for m, v in (("bdbig", 2.0 ** 96), ("bdh", 2.0 ** -12), ("bd1k", 1024.0), ("bd256", 256.0), ("w2", col(NPW)), ("wpw", col(IPW))):
+    for m, v in (("bdbig", 2.0 ** 96), ("bdh", 2.0 ** -12), ("bd1k", 1024.0), ("bdn", -1.0), ("w2", col(NPW)), ("wpw", col(IPW))):
         ts(M(m), M("bd"), v, OP.mult)
     ms(M("ones"), 1.0)
     ts(A("cb", 0, 128), A("cf", 128, 128), col(P), OP.is_gt, -1.0, OP.mult)
@@ -226,7 +234,7 @@ def build():
     ts(A("cf", 496, 8), A("iot", 0, 8), 16.0, OP.mult, col(P), OP.add)
     ts(A("basel", 0, 8), A("cf", 496, 8), 16.0, OP.mult, -16.0, OP.add)
     for c in range(2):
-        ts(A("lanel", 8 * c, 8), A("cf", 496, 8), float(LANE0[c]), OP.add, 1.0 / 256, OP.mult)
+        ts(A("lanel", 8 * c, 8), A("cf", 496, 8), float(LANE0[c] - 160 * 256), OP.add, 1.0 / 256, OP.mult)
     ms(A("thl", 8, 24), 0.5)
     ts(A("thl", 0, 8), A("cf", 496, 8), 16.0, OP.mult)
     JJ, FF, JN0, NF = range(4)
@@ -288,18 +296,26 @@ def build():
 
     def early(s, c):
         d = names(s, c)
-        cp(d["e16"], d["e"])
-        cp(A(d["c16"], 0, 128), IND(WL, d["e16"]))
         nv = VSHARE[(s, c)]
         pieces = []
-        lo = 0
-        if nv:
-            pieces.append(("V", 0, nv))
-        lo = nv
-        while lo < 128:
-            hi = min(128, lo + GP[0])
-            pieces.append(("S", lo, hi - lo))
-            lo = hi
+        if s > 0 and LANE0[c] == 0 and SPLIT[s]:
+            e, e16 = d["e"], d["e16"]
+            for hf in range(2):
+                cp(A(e16[0], e16[1] + 4 * hf, 4), A(e[0], 8 * hf, 4, 2))
+                cp(A(d["c16"], 64 * hf, 64), IND(WL, A(e16[0], e16[1] + 4 * hf, 4)))
+            parts = [(0, 64, min(SPLIT[s] - 1, nv)), (64, 128, min(64, nv - min(SPLIT[s] - 1, nv)))]
+        else:
+            cp(d["e16"], d["e"])
+            cp(A(d["c16"], 0, 128), IND(WL, d["e16"]))
+            parts = [(0, 128, nv)]
+        for lo, end, k in parts:
+            if k:
+                pieces.append(("V", lo, k))
+            lo += k
+            while lo < end:
+                hi = min(end, lo + GP[0])
+                pieces.append(("S", lo, hi - lo))
+                lo = hi
         for e, lo, n in pieces:
             o, i = A(d["Y"], 16 * lo, 16 * n), IND(TAB, A(d["c16"], lo, n))
             if e == "V":
@@ -315,8 +331,8 @@ def build():
         tt(d["e5"], d["e4"], d["ea"], OP.add)
         ts(d["ed"], d["e5"], 1023, OP.bitwise_and)
         cp(d["ed16"], d["ed"])
-        ts(d["b"], d["e"], 1.0 / 256, OP.mult, -0.498, OP.add)
-        tt(d["df"], d["b"], A("lanel", 8 * c, 8), OP.add)
+        act(A("lq%d" % c, 56, 8), d["e"], AF.Identity, bias=160 - 0.498, scale=1.0 / 256)
+        tt(d["df"], A("lq%d" % c, 56, 8), A("lanel", 8 * c, 8), OP.add)
         ts(d["d16"], d["df"], 256.0, OP.mult)
         act(d["x0"], IND(WL, d["e16"]), AF.Copy, scale=37.0)
         act(d["old"], IND(WL, d["d16"]), AF.Copy)
@@ -433,8 +449,8 @@ def build():
             ts(d["bt2"], d["bt"], 32768, OP.bitwise_and)
             ts(d["gb"], d["bt2"], 0.5, OP.is_gt)
             u2 = slot()
-            mm(grp(u2, [(M("w1"), d["gb"])]))
-            tt(J, u2, d["f"], OP.max)
+            mm(grp(u2, [(M("i1"), d["f"]), (M("w1"), d["gb"])]))
+            act(J, u2, AF.Relu)
             w0 = slot()
             mm(grp(w0, [(M("bd"), d["f"]), (M("in1"), d["P0"])]))
             act(d["jn0"], w0, AF.Relu, bias=NEG / 16, scale=1.0 / 16)
@@ -446,6 +462,10 @@ def build():
             w2 = slot()
             mm(grp(w2, [(M("bd"), d["f"]), (M("bdh"), d["h"])]))
             ts(d["nf"], w2, 1.0, OP.is_le, 1.0 / 16, OP.mult)
+            if last:
+                w3 = slot()
+                mm(grp(w3, [(M("bd"), d["h"])]))
+                act(d["ad"], w3, AF.Relu, bias=1.0, scale=-1.0)
             if EARLY[(s, c)]:
                 l0 = slot(8)
                 tolist(l0, 2, d["f"], 8, [base])
@@ -462,6 +482,8 @@ def build():
         q2 = slot(48)
         items = []
         for i, (_, _, terms) in enumerate(ST2[t]):
+            if last and i == 1:
+                terms = [("in384", FF), ("i384", JN0), ("in384", NF), ("i1", JJ), ("in1", FF)]
             items += grp(A(q2[0], q2[1] + 8 * i, 8), [(M(m), A(lq, 8 * x, 8)) for m, x in terms])
         mm(items)
         tt(A(lf, 32, 48), q2, A("con", 56 * t, 48), OP.add)
@@ -475,19 +497,22 @@ def build():
         tt(A("oya", lo // 16, 8) if last else A(sl, 1, 8, 2), again, d["A"], OP.add)
         if s > 1:
             m01 = slot()
-            mm(grp(m01, [(M("ih"), d["P0"]), (M("ih"), d["P1"]), (M("in1"), d["h"]), (M("i16k"), d["nf"])]))
-            tt(d["F"], m01, d["z"], OP.min)
+            terms = [(M("ih"), d["P0"]), (M("ih"), d["P1"]), (M("in1"), d["h"]), (M("i16k"), d["nf"])]
             v = slot()
-            mm(grp(v, [(M("inp"), M("ones")), (M("i8"), d["nf"]), (M("bd"), d["F"])]))
+            if EARLY[(s, c)]:
+                mm(grp(m01, terms + [(M("in1"), d["z"])]))
+                act(d["E"], m01, AF.Relu, scale=-1.0)
+                mm(grp(v, [(M("inp"), M("ones")), (M("i8"), d["nf"]), (M("bd"), d["z"]), (M("bdn"), d["E"])]))
+            else:
+                mm(grp(m01, terms))
+                tt(d["F"], m01, d["z"], OP.min)
+                mm(grp(v, [(M("inp"), M("ones")), (M("i8"), d["nf"]), (M("bd"), d["F"])]))
             ts(d["r"], v, CM, OP.add, CM, OP.subtract)
             tt(d["ohq"], v, d["r"], OP.is_equal)
-            if EARLY[(s, c)]:
-                dz = slot()
-                mm(grp(dz, [(M("in1"), d["z"]), (M("i1"), d["F"])]))
-                tt(d["E"], dz, d["ohq"], OP.mult)
             items = []
             for i, p in enumerate(("P0", "P1")):
-                items += grp(A("ps7", 256 + 128 * i, 128), [(M("i15"), d[p]), (M("i1k"), d["oh"]), (M("in15"), zg)])
+                more = [(M("in1k"), d["ad"])] if last and i else []
+                items += grp(A("ps7", 256 + 128 * i, 128), [(M("i15"), d[p])] + more + [(M("i1k"), d["oh"]), (M("in15"), zg)])
             mm(items)
             ts(A(d["s0"][0], d["s0"][1], 256), A("ps7", 256, 256), CM - 1024, OP.add, CM, OP.is_equal)
         if s > 0:
@@ -495,7 +520,7 @@ def build():
             if s == 1:
                 mm(grp(cand, [(M("i1k"), d["oh"]), (M("i1"), zg)]))
             elif EARLY[(s, c)]:
-                mm(grp(cand, [(M("i1k"), d["oh"]), (M("i1k"), d["ohq"]), (M("i1"), d["E"]), (M("i1"), zg)]))
+                mm(grp(cand, [(M("i1k"), d["oh"]), (M("i1k"), d["ohq"]), (M("in1"), d["E"]), (M("i1"), zg)]))
             else:
                 mm(grp(cand, [(M("i1k"), d["oh"]), (M("i1"), d["F"]), (M("i1k"), d["ohq"])]))
             rw = slot()
@@ -509,7 +534,12 @@ def build():
             tt(en, A(l2[0], l2[1] + 8, 8), d["c2"], OP.add)
         if not last:
             send(s, c, "l", sl, "el%d%d" % (s + 1, c), 8)
-        if s > 1:
+        if last:
+            ts(A(lf, 80, 16), A(l2[0], l2[1] + 16, 16), -384.0, OP.mult)
+            tt(A(lf, 32, 8), A(lf, 32, 8), A(l2[0], l2[1] + 16, 8), OP.subtract)
+            tt(A(lf, 40, 8), A(lf, 40, 8), A(lf, 80, 8), OP.add)
+            tt(A(lf, 40, 8), A(lf, 40, 8), A(lf, 88, 8), OP.add)
+        elif s > 1:
             tt(A(lf, 32, 8), A(lf, 32, 8), A(l2[0], l2[1] + 16, 8), OP.subtract)
             tt(A(lf, 40, 8), A(lf, 40, 8), A(l2[0], l2[1] + 24, 8), OP.add)
         cp(A("l16_%d" % c, 40, 24), A(lf, 32, 24))
@@ -524,15 +554,9 @@ def build():
         else:
             y0, y1, yk = A("oy0", lo, 128), A("oy1", lo, 128), A("oyk", lo, 128)
             ts(y0, IND(d["win"], d["o0"]), 125.0, OP.add, -1.0, OP.max)
-            ts(d["y1p"], IND(d["win"], d["o1"]), 125.0, OP.add, -1.0, OP.max)
+            ts(y1, IND(d["win"], d["o1"]), 125.0, OP.add, -1.0, OP.max)
             tt(A(sb, 0, 128), IND(d["win"], d["oK"]), d["cB"], OP.max)
             ts(yk, A(sb, 0, 128), 125.0, OP.add, -1.0, OP.max)
-            dd = slot()
-            mm(grp(dd, [(M("i1"), y0), (M("in1"), d["y1p"])]))
-            act(d["ad"], dd, AF.Abs)
-            lim = slot()
-            mm(grp(lim, [(M("in1"), M("ones")), (M("bd256"), d["ad"])]))
-            tt(y1, lim, d["y1p"], OP.min)
 
     def send(s, c, kind, src, dst, w):
         blocks = [(h, LANE0[c] // 64 + h) for h in range(2)]
@@ -552,10 +576,11 @@ def build():
                                              src=R(A(src, h * w, w)), dst=R(A(dst, h * w, w))))
                 X["sent"][0] += k
             return q.remote_dma_fused(trs, local_sem=T.sem["sent"])
-        add("G", call, [A(dst, h * w, w) for h, b in far], [A(src, h * w, w) for h, b in far], 700, sem=(name, "far"), lat=2500)
+        add("G", call, [A(dst, h * w, w) for h, b in far], [A(src, h * w, w) for h, b in far], 700, sem=(name, "far"),
+            lat=1700 + 600 * len(far))
         for h, b in blocks:
             if b % N == 0:
-                cp(A(dst, h * w, w), A(src, h * w, w))
+                act(A(dst, h * w, w), A(src, h * w, w), AF.Copy)
 
     for s in range(STEPS):
         for k, (part, c) in enumerate(((early, 0), (early, 1), (bulk, 0), (join, 0), (bulk, 1), (tail, 0), (join, 1), (tail, 1))):
@@ -590,6 +615,7 @@ def plan():
                     old = [x for x in old if not (a[3] == 1 and a[1] <= x[2] and x[3] <= a[2])]
                 acc[a[0]] = old + [(i, kind, a[1], a[2], a[3])]
         o["banks"] = sorted(set(a[0] for a in o["r"] + o["w"] if isps(a)))
+        o["dep"] = sorted(pred[i])
     succ = [[] for _ in ops]
     for i in range(n):
         for j in pred[i]:
@@ -621,6 +647,9 @@ def plan():
         st = {i: start(i) for i in ready}
         i0 = min(ready, key=lambda k: (st[k], k))
         i = max((k for k in ready if st[k] <= st[i0] + GP[1] and ops[k]["eng"] == ops[i0]["eng"]), key=lambda k: (prio[k], -k))
+        if ORDER:
+            i = ORDER[len(order)]
+            assert i in ready
         o = ops[i]
         o["t"] = st[i]
         free[o["eng"]] = st[i] + o["cost"]

@@ -1,73 +1,89 @@
 import math
+import numpy as np
 from concourse.bass import DstId, RemoteDMATransfer
 from concourse.mybir import AluOpType as OP, AxisListType, ActivationFunctionType as AF
 
-N, STEPS, LC = 4, 4, 128
-LANE0 = [0, 128]
+N, STEPS = 4, 4
 CM = 1.5 * 2 ** 27
-SC, LAM = 1.75, 0.8125
 NEG = -131.0
+NB = 3
+SC, LAM = 1.75, 0.8125
 
-SCALED = {"i1": 1.0, "in1": -1.0, "i15": 1.5, "in15": -1.5, "ilam": LAM, "inls": -LAM * SC, "ih": 0.5,
-          "in512": -512.0, "i1k": 1024.0, "in1k": -1024.0, "in32": -32.0, "i384": 384.0, "in384": -384.0, "in768": -768.0,
-          "i8": 8.0, "i16k": 16384.0}
-VSHARE, DV, ABS2, EARLY, GP, BIAS = (
-    {(0, 0): 64, (0, 1): 64, (1, 0): 48, (1, 1): 16, (2, 0): 32, (2, 1): 16, (3, 0): 16, (3, 1): 64}, {(0, 0): [0, 0, 0, 0], (0, 1): [0, 0, 0, 0], (1, 0): [0, 0, 0, 0], (1, 1): [0, 0, 1, 0], (2, 0): [0, 0, 0, 0], (2, 1): [0, 0, 0, 1], (3, 0): [0, 0, 0, 0], (3, 1): [1, 0, 0, 0]}, {(0, 0): [1, 0, 0, 1], (0, 1): [1, 1, 1, 1], (1, 0): [0, 0, 0, 1], (1, 1): [1, 0, 0, 0], (2, 0): [0, 0, 1, 0], (2, 1): [1, 1, 0, 1], (3, 0): [0, 0, 1, 1], (3, 1): [1, 0, 0, 0]}, {(0, 0): 0, (0, 1): 1, (1, 0): 0, (1, 1): 1, (2, 0): 1, (2, 1): 1, (3, 0): 0, (3, 1): 0}, [32, 100.0], [[-4300.0, -1000.0, 18800.0, 3300, -4600.0, 3700, 300.0, 5900.0], [1500.0, -4700.0, 11400.0, 1900, 300.0, -400, -4500.0, -300.0], [600.0, 6600.0, -600.0, 7800, 2000.0, 12900, -2600.0, 1300.0], [-7100.0, 8600.0, 400.0, 900, -2200.0, 18800, 4500.0, -13700.0], [-4000, 0, 0, 0, 0, 0, 0, 0]])
-NCS = {(s, c): [0, 0, 0, 0] for s in range(STEPS) for c in range(2)}
-SPLIT = [1, 33, 1, 0]
-VSHARE.update({(0, 0): 64, (0, 1): 64, (1, 0): 64, (1, 1): 64, (2, 0): 32, (2, 1): 16, (3, 0): 16, (3, 1): 64})
-DV.update({(1, 0): [0, 0, 0, 0], (1, 1): [0, 0, 1, 0], (2, 0): [0, 0, 0, 0], (2, 1): [0, 0, 1, 1], (3, 0): [0, 0, 1, 0], (3, 1): [1, 0, 0, 1]})
-ABS2.update({(0, 0): [1, 0, 0, 1], (0, 1): [1, 1, 1, 1], (1, 0): [0, 1, 0, 1], (1, 1): [1, 0, 1, 1], (2, 0): [0, 1, 1, 0], (2, 1): [0, 1, 0, 0],
-             (3, 0): [0, 0, 1, 1], (3, 1): [1, 0, 0, 0]})
-EARLY.update({(0, 0): 0, (0, 1): 1, (1, 0): 1, (1, 1): 1, (2, 0): 0, (2, 1): 1, (3, 0): 0, (3, 1): 1})
-CODE = "03063408090a0b021o0g000105072u0k360d1c231p1v1r0n1s1w1q042v0h1z2x30332220241u0c35372w3h3l41211t1x1y0i473u3f0m381d3i2t253z403j3d100z430v0t0x4a0s310o3o320y2y0q0u0p0r2d393k3t1j1m2f283e3c3b2c3v1e0l421l4g3x274c193g3a4h4i3w3m4j4o4l4r3y4s2g2e4m1n2k2i4k3q4p4t3r51524n4q4u55123n3p4d48504v494b4w4x262a3s53562b592l5h2h115d4y4e5a572m5e2o2j2p2q5k4z5l54585i5m5b5n5o5f5p5q5c5t5j445w5g5z155r605v5u451746612n5s2s0w5x4f2r2z1f625y646k63676l68656o69666p6m6b6a6d6c6n7r7s7t6q7u6f6s6u6y716e6r7v7w6g6h6z6v6t706i6w827x736j6x74837y76847z727e7i8075771b858688781g798q8e7a89818s8a878b8f7b8g8r8t8h1h8c0j1i8u1a8i9a997l299c9b1k8v8d8j9q7c7j8k9d0e147d8w8x8y8m9e928l9r8n9s938z9t90a09u9j8o9fa19k9g9h959v949w7k9x969y9z91a27n167f7o7g9m9l7h18a3a5977m9n0f7p7qa48pa6aca713a8ama99oad989i9pafaeagapasabaaahaoanataqauaiavajakalarawayazb8byaxbzb0b1b2blc2b3b4d7dbb5d8b9c3d9b6ddc8bmb7badac0c1c5c4c6bbbdc7cfdec9dcbccachbecbcibkbfdkbgdfbhbnbtbibpbodldgbjbqbudhbvbrdmbwckbsccdidnbxcdcedrdodjdsdpdycgdtdqdzcjducle0cycud1dvcme1eaebeceedwdxe2csczcnede3fgegcvctd0cwe4e6cxd3d4cocrcqcpehe5fhe7efeififsd2eofqeyezf6exfjftewepfkekejflg4d6erelf0fmf9fnfoeqesfrfpfuf7f1f8f2emfafvfcf3fxfbfwg5fyf4etfzg0g1g6fdg9g7g8gcgbgagdeufeeng2g3geggevghglgmgigngjf5ffgfgogpgkgqd5gte8e9grgsgugzgvgwh0gxhdh1gyheh2hbhch9h3hfidieh4iqhaitighqhrh5jjh6jlh7ikifjkilhsimh8hgirjminisioiphjhthhjnjphuivihijhkhihliwhmhniihyhvhwhxhpjqk5k7k6hohzi0i1i2k4jojri3jxk8jyi7i6iui4i5iymdkfmejsi8iai9k9jtjukgj6jajzkaibixk0ick1jvkbkcjwkikhk2k3izj0jdkjkxj3kkj1ktkvkdkuj4kwj2kykeklkzj5kmlzl2l0l3l1lpknl4kplbm0kqjflsl6l5m1lckombl7l8jgm2jbm3m9lrleldm4mclqm5l9lfliltlalglhljm6lulvj7jcm7mpj8m8lkj9jellmajilwjhlxmfmgkrlmmimhmjmqlnmrmsmtksmulomkmmmomlmnlymxmymvnjnendmwnknfmzngn0n1nhnlnzninmn2n4nnp0ntnun5n3n6noo0nxnpnvnyo1n7nqnrnwocn8nansodo2nbn9nco3o4oeo5ofohogo6ojomokoiolo7ono9o8oboooap2oropotosouoqp1ovoyoxp5ozp4owp3"
-ORDER = [int(CODE[_i:_i + 2], 36) for _i in range(0, len(CODE), 2)]
-MATS = list(SCALED) + ["inp", "irow", "w2h", "bd", "bdbig", "bdh", "bd1k", "bdn", "w1", "warg", "w2", "wpw", "ones"]
+PAR = {
+    "VSHARE": [[64, 64], [16, 16], [32, 32], [32, 32]],
+    "DV": [[0, 0], [0, 0], [0, 0], [0, 0]],
+    "ABS2": [[2, 2], [0, 0], [0, 0], [0, 0]],
+    "EARLY": [[0, 0], [0, 0], [0, 1], [0, 1]],
+    "GP": 64, "WIN": 100.0, "ROUNDS": 0, "SEED": 1, "NOISE": 200.0, "PUSH": [[0, 0], [0, 0], [0, 0], [0, 0]], "MOVES": 0, "APART": 0, "KM": [[0, 0], [0, 0], [0, 0], [0, 0]], "KEEP": 0.7, "FIFO": 0, "SOFT": 1.0, "PS": 512, "STEP": 1500.0, "RUN": 8, "TEMP": 100.0, "NB": 3, "NB1": 1, "SG": [[0, 0], [0, 0], [0, 0], [0, 0]], "OFF": [[0, 0], [0, 0], [0, 0], [0, 0]],
+    "BIAS": [[0.0] * 9 for _s in range(STEPS)],
+}
+
+PAR.update({'VSHARE': [[64, 64], [48, 16], [16, 32], [32, 32]], 'ABS1': [[0, 0], [0, 0], [0, 0], [0, 0]], 'ABS2': [[2, 4], [0, 0], [0, 0], [3, 0]], 'EARLY': [[0, 0], [0, 0], [0, 1], [1, 1]], 'GP': 128, 'WIN': 100.0, 'ROUNDS': 300, 'SEED': 1, 'BIAS': [[1000.0, 2000.0, 8500.0, 9000.0, 2000.0, -1000.0, 0.0, 2500.0, 4500.0], [-7500.0, 9500.0, -1000.0, 0.0, 1500.0, 0.0, 8000.0, -3000.0, 3500.0], [11000.0, 8000.0, 3500.0, -1000.0, 2000.0, -1500.0, 0.0, -2500.0, 4500.0], [-6500.0, 9000.0, 500.0, -5500.0, 3000.0, 0.0, 0.0, 0.0, 1000.0]]})
+
+PAR.update({'VSHARE': [[64, 64], [48, 16], [32, 32], [32, 32]], 'DV': [[0, 0], [0, 2], [2, 2], [0, 2]], 'ABS2': [[1, 2], [4, 0], [1, 3], [0, 1]], 'EARLY': [[0, 0], [0, 0], [0, 1], [0, 0]], 'GP': 32, 'WIN': 100.0, 'ROUNDS': 2000, 'SEED': 1, 'BIAS': [[6500, -2000, 1500, 3500, -2500, -3000, 20500, -7500, -3500], [7500, 3500, -500, 9000, -2500, -1500, 7000, 8500, 7500], [3000, 500, -7500, -8500, 2000, 500, 14000, 14500, 500], [-4000, -7000, -9500, 0, 6000, 1000, 4000, 4500, 4000]]})
+PAR.update({'VSHARE': [[64, 32], [64, 16], [64, 16], [64, 16]], 'EARLY': [[0, 0], [0, 0], [0, 0], [0, 1]], 'GP': 32, 'WIN': 100.0, 'ROUNDS': 1, 'SEED': 1, 'NOISE': 200.0, 'PUSH': [[4000, 4000], [4000, 0], [4000, 0], [2000, 0]], 'NB': 4, 'NB1': 2, 'OFF': [[1, 1], [1, 1], [1, 1], [1, 1]], 'BIAS': [[2000, 0, -1000, 0, 5000, -2000, 5000, 0, 3000], [0, 0, -3000, 0, 7000, 2000, 5000, 0, 5000], [500, 0, -3000, 0, 5000, 0, 5000, -1000, 5000], [0, 0, -3000, 3000, 5000, 0, 4500, 0, 0]],
+            "MOVES": 80000, "TEMP": 500.0, "SOFT": 1.0, "KEEP": 0.8, "PS": 2000})
+PAR["UN"] = [[[[4, h[b], d[b]] for b in range(4)] for h, d in x] for x in (
+    (([1, 1, 0, 0], [0] * 4), ([1, 1, 0, 0], [0] * 4)), (([2, 2, 0, 0], [0] * 4), ([2, 0, 0, 0], [0] * 4)),
+    (([1, 1, 1, 0], [0, 0, 0, 1]), ([1, 1, 1, 0], [0, 0, 0, 1])), (([1, 1, 1, 0], [0, 0, 0, 1]), ([1, 1, 1, 0], [0, 0, 0, 1])))]
+PAR.update({"SWEEPS": 30, "TEMP": 800.0, "SPAN": 100, "SOFT": 2.0, "MOVES": 250, "OFF": [[0, 0], [1, 1], [1, 1], [1, 1]],
+            "VSHARE": [[64, 48], [48, 0], [48, 16], [48, 16]]})
+PAR["UN"] = [[[[8, 0, 0], [8, 1, 0]], [[8, 2, 0], [8, 0, 0]]], [[[4, 0, 0]] * 4] * 2] + [[[[4, 1, 0]] * 3 + [[4, 0, 1]]] * 2] * 2
+SCALED = {"i1": 1.0, "in1": -1.0, "i15": 1.5, "in15": -1.5, "ih": 0.5, "iq": 0.25, "inq": -0.25,
+          "in512": -512.0, "i512": 512.0, "i1k": 1024.0, "i1536": 1536.0, "in32": -32.0, "i384": 384.0, "in384": -384.0,
+          "in2k": -2048.0, "ia": -1.8125, "ib": 1.0 / 2048, "i10": 10.0, "ilam": LAM, "inls": -LAM * SC}
+MATS = list(SCALED) + ["iw", "bd", "bdbig", "bdp", "bd1k", "bd10", "bdn1k", "w1", "warg", "w2", "wpw", "tri"]
 MOFF = {m: 128 * i for i, m in enumerate(MATS)}
 
 SCRATCH = {
     "tab": ("sbuf", [128, 8192], "bfloat16"), "ivi": ("sbuf", [128, 1024], "int32"), "wl": ("sbuf", [128, 1024], "float32"),
     "e0i": ("sbuf", [128, 16], "int32"), "mats": ("sbuf", [128, 128 * len(MATS)], "bfloat16"),
-    "zz": ("sbuf", [128, 4 * 144], "bfloat16"), "iot": ("sbuf", [128, 1032], "float32"), "tk": ("sbuf", [128, 1024], "bfloat16"),
-    "tmpb": ("sbuf", [128, 80], "bfloat16"),
+    "zz": ("sbuf", [128, 5 * 144], "bfloat16"), "sgc": ("sbuf", [128, 56], "float32"), "zh": ("sbuf", [128, 144 + 128], "float16"),
+    "iot": ("sbuf", [128, 1032], "float32"), "tk": ("sbuf", [128, 1024], "bfloat16"), "tmpb": ("sbuf", [128, 80], "bfloat16"),
     "cols": ("sbuf", [128, 16], "float32"), "coli": ("sbuf", [128, 8], "int32"), "cf": ("sbuf", [128, 512], "float32"),
     "cb": ("sbuf", [128, 512], "bfloat16"), "basel": ("sbuf", [128, 8], "bfloat16"), "lanel": ("sbuf", [128, 16], "float32"),
-    "con": ("sbuf", [128, 3 * 56], "float32"), "thl": ("sbuf", [128, 32], "float32"),
+    "con": ("sbuf", [128, 2 * 24], "float32"), "thl": ("sbuf", [128, 64], "float32"), "kmw": ("sbuf", [128, 2048], "bfloat16"),
     "oyk": ("sbuf", [128, 256], "bfloat16"), "oy0": ("sbuf", [128, 256], "bfloat16"), "oy1": ("sbuf", [128, 256], "bfloat16"),
     "oye": ("sbuf", [128, 16], "float32"), "oya": ("sbuf", [128, 16], "float32"),
+    "wf": ("sbuf", [128, 256 * 3], "float32"), "wi": ("sbuf", [128, 256 * 2], "int32"),
 }
 for _b in range(8):
     SCRATCH["ps%d" % _b] = ("psum", [128, 512], "float32")
 for _k in range(3):
-    SCRATCH["aa%d" % _k] = ("sbuf", [128, 512], "bfloat16")
     SCRATCH["nc%d" % _k] = ("sbuf", [128, 512], "bfloat16")
-for _k in range(2):
     SCRATCH["ab%d" % _k] = ("sbuf", [128, 512], "bfloat16")
-    SCRATCH["dd%d" % _k] = ("sbuf", [128, 512], "float32")
+    SCRATCH["aa%d" % _k] = ("sbuf", [128, 512], "bfloat16")
 for _c in range(2):
-    SCRATCH["yy%d" % _c] = ("sbuf", [128, 2048], "bfloat16")
+    SCRATCH["dd%d" % _c] = ("sbuf", [128, 512], "float32")
+    SCRATCH["yy%d" % _c] = ("sbuf", [128, 2064], "bfloat16")
     SCRATCH["me%d" % _c] = ("sbuf", [128, 2048], "bfloat16")
+    SCRATCH["tb%d" % _c] = ("sbuf", [128, 512], "bfloat16")
     SCRATCH["c16_%d" % _c] = ("sbuf", [128, 128], "uint16")
-    SCRATCH["l16_%d" % _c] = ("sbuf", [128, 72], "uint16")
-    SCRATCH["li%d" % _c] = ("sbuf", [128, 64], "int32")
-    SCRATCH["lf%d" % _c] = ("sbuf", [128, 128], "float32")
-    SCRATCH["lq%d" % _c] = ("sbuf", [128, 64], "bfloat16")
-    SCRATCH["rf%d" % _c] = ("sbuf", [128, 128 * 6], "float32")
-    SCRATCH["ri%d" % _c] = ("sbuf", [128, 128 * 4], "int32")
-    SCRATCH["rb%d" % _c] = ("sbuf", [128, 128 * 15], "bfloat16")
-    SCRATCH["stk%d" % _c] = ("sbuf", [128, 128 * 8], "bfloat16")
+    SCRATCH["l16_%d" % _c] = ("sbuf", [128, 40], "uint16")
+    SCRATCH["u16_%d" % _c] = ("sbuf", [128, 64], "uint16")
+    SCRATCH["si%d" % _c] = ("sbuf", [128, 128], "int32")
+    SCRATCH["li%d" % _c] = ("sbuf", [128, 16], "int32")
+    SCRATCH["lf%d" % _c] = ("sbuf", [128, 64], "float32")
+    SCRATCH["lq%d" % _c] = ("sbuf", [128, 40], "bfloat16")
+    SCRATCH["rf%d" % _c] = ("sbuf", [128, 128 * 2], "float32")
+    SCRATCH["ri%d" % _c] = ("sbuf", [128, 128 * 2], "int32")
+    SCRATCH["rb%d" % _c] = ("sbuf", [128, 128 * 12], "bfloat16")
+    SCRATCH["stk%d" % _c] = ("sbuf", [128, 128 * 4], "bfloat16")
+    SCRATCH["sh%d" % _c] = ("sbuf", [128, 128 * 4], "float16")
     for _s in range(STEPS):
-        SCRATCH["win%d%d" % (_s, _c)] = ("sbuf", [128, 1168], "bfloat16")
-        SCRATCH["el%d%d" % (_s, _c)] = ("sbuf", [128, 16], "float32")
+        SCRATCH["win%d%d" % (_s, _c)] = ("sbuf", [128, 784], "bfloat16")
         SCRATCH["sb%d%d" % (_s, _c)] = ("sbuf", [128, 384], "bfloat16")
-        SCRATCH["sl%d%d" % (_s, _c)] = ("sbuf", [128, 16], "float32")
+        SCRATCH["sl%d%d" % (_s, _c)] = ("sbuf", [128, 16], "int32")
+for _s in range(STEPS):
+    SCRATCH["el%d" % _s] = ("sbuf", [128, 32], "int32")
 
 SEMAPHORES = (["qV", "qS", "qP", "qG", "sent", "ld0", "ld1", "ld2", "outs"]
-              + ["ar%s%d%d" % (k, s, c) for k in "lr" for s in range(1, STEPS) for c in range(2)])
+              + ["ar%s%d%d" % (k, s, c) for k in "lr" for s in range(1, STEPS) for c in range(2)]
+              + ["lo%s%d" % (k, s) for k in "lr" for s in range(1, STEPS)])
 
-CY = 0.83 * 1.2
-PECY = 0.42 * 1.2
-FIX, HOP = 60.0, 120.0
+CY = 0.83 * 1.15
+PECY = 0.42 * 1.15
+FIX, HOP = 60.0, 160.0
 GA, SCA = 1.6, 3.8
 
 
@@ -86,7 +102,7 @@ def cnt(a):
 
 
 def two(a):
-    return a[0] != "ind" and SCRATCH[a[0]][2] in ("bfloat16", "uint16")
+    return a[0] != "ind" and SCRATCH[a[0]][2] in ("bfloat16", "uint16", "float16")
 
 
 def isps(a):
@@ -105,6 +121,15 @@ def flat(xs):
     return out
 
 
+def signs(s, c):
+    k = 0
+    for nk, how, _ in PAR["UN"][s][c]:
+        if how < 2 or (s and PAR["KM"][s][c]):
+            break
+        k += nk
+    return k
+
+
 def build():
     ops = []
 
@@ -117,7 +142,7 @@ def build():
                 r.append(a[2])
             else:
                 w.append(a)
-        ops.append({"eng": eng, "call": call, "w": w, "r": r, "cost": cost, "sem": sem, "lat": lat})
+        ops.append({"eng": eng, "call": call, "w": w, "r": r, "cost": cost, "sem": sem, "lat": lat, "part": None})
 
     def ecost(out, ins, base):
         n = cnt(ins[0]) if ins else cnt(out)
@@ -151,11 +176,23 @@ def build():
             return q.activation(R(out), R(a), f, bias=R(bias), scale=R(scale))
         add("S", call, [out], [a, bias, scale], ecost(out, [a], 1) + extra)
 
+    def mms(items, whole=None):
+        part, n = [], 0
+        for x in items + [None]:
+            if part and (x is None or n + cnt(x[2]) > PAR["PS"]):
+                mm(part)
+                if whole:
+                    ops[-1]["w"].append(whole)
+                part, n = [], 0
+            if x:
+                part.append(x)
+                n += cnt(x[2])
+
     def mm(items):
         def call(q, R, X):
             last = None
             for o, l, r, st, sp in items:
-                last = q.matmul(R(o), R(l), R(r), st, sp)
+                last = q.matmul(R(o), R(l), R(r), bool(st), bool(sp))
             return last
         add("P", call, [x[0] for x in items], [x[1] for x in items] + [x[2] for x in items],
             20 + sum(max(64, cnt(x[2])) * PECY + 4 for x in items))
@@ -174,45 +211,50 @@ def build():
         return A("mats", MOFF[name], 128)
 
     def Z(t, k):
-        return A("zz", 144 * t + 15 - k, 128)
+        return A("zh", 15 - k, 128) if t == "h" else A("zz", 144 * t + 15 - k, 128)
 
     def col(i):
         return A("cols", i, 1)
 
+    def dma(out, a, sem, lat):
+        add("Y", lambda q, R, X: q.dma_start(R(out), R(a)), [out], [a], 60, sem=(sem, 16), lat=lat)
+
     add("Y", lambda q, R, X: q.dma_start(R(A("e0i", 0, 16)), X["T"].e0[:]), [A("e0i", 0, 16)], [], 60, sem=("ld0", 16), lat=2200)
-    add("Y", lambda q, R, X: q.dma_start(R(A("ivi", 0, 1024)), X["T"].iv[:]), [A("ivi", 0, 1024)], [], 60, sem=("ld1", 16), lat=3500)
+    add("Y", lambda q, R, X: q.dma_start(R(A("ivi", 0, 1024)), X["T"].iv[:]), [A("ivi", 0, 1024)], [A("cols", 15, 1)][:0], 60,
+        sem=("ld1", 16), lat=3500)
     add("Y", lambda q, R, X: q.dma_start(R(A("tab", 0, 8192)), X["T"].st[:]), [A("tab", 0, 8192)], [], 60, sem=("ld2", 16), lat=8000)
 
-    P, G16, PW, NPW, IPW, K16, P64, TKC, NP, G = range(10)
+    P, G16, PW, NPW, IPW, K16, WP, KT, G, NW4 = range(10)
     iota(A("coli", 0, 1), [[1, 1]], 0, 1)
     iota(A("iot", 0, 1032), [[1, 1032]], 0, 0)
     iota(A("cf", 0, 128), [[1, 8], [0, 16]], 0, 0)
     iota(A("cf", 128, 128), [[0, 8], [1, 16]], 0, 0)
     iota(A("cf", 256, 128), [[1, 128]], 0, -1)
+    iota(A("cf", 384, 32), [[0, 2], [1, 16]], 0, 0)
     ts(A("coli", 1, 1), A("coli", 0, 1), 15, OP.bitwise_and)
     ts(A("coli", 2, 1), A("coli", 0, 1), 4, OP.arith_shift_right)
     cp(col(P), A("coli", 1, 1))
     cp(col(G), A("coli", 2, 1))
     ts(col(G16), col(G), 16.0, OP.mult, 15.0, OP.add)
     ts(col(K16), col(P), 16.0, OP.add)
-    ts(col(P64), col(P), 64.0, OP.mult, -160.0, OP.add)
-    ts(col(NP), col(P), -1.0, OP.mult)
+    ts(col(WP), col(P), 64.0, OP.mult, 2048.0, OP.add)
+    ts(col(NW4), col(WP), -4.0, OP.mult)
     act(A("tmpb", 64, 1), col(P), AF.Exp, scale=math.log(2.0), extra=1300.0)
     act(A("tmpb", 66, 1), col(P), AF.Exp, bias=15 * math.log(2.0), scale=-math.log(2.0))
     cp(col(PW), A("tmpb", 64, 1))
     cp(col(IPW), A("tmpb", 66, 1))
-    ts(A("cf", 432, 16), A("cf", 128, 16), col(P), OP.is_equal)
+    ts(A("cf", 432, 16), A("cf", 384, 16), col(P), OP.is_equal)
     ts(col(NPW), col(PW), -1.0, OP.mult)
     ts(M("i1"), A("cf", 256, 128), 0.0, OP.is_equal)
     ts(M("bd"), A("cf", 0, 128), col(G), OP.is_equal)
     for m, v in SCALED.items():
         if m != "i1":
             act(M(m), M("i1"), AF.Copy, scale=float(v))
-    ts(M("inp"), M("i1"), col(NP), OP.mult)
-    ts(M("irow"), M("i1"), col(P64), OP.mult)
-    for m, v in (("bdbig", 2.0 ** 96), ("bdh", 2.0 ** -12), ("bd1k", 1024.0), ("bdn", -1.0), ("w2", col(NPW)), ("wpw", col(IPW))):
+    ts(M("iw"), M("i1"), col(WP), OP.mult)
+    for m, v in (("bdbig", 2.0 ** 96), ("bd10", 10.0), ("bd1k", 1024.0), ("bdn1k", -1024.0), ("w2", col(NPW)), ("wpw", col(IPW))):
         ts(M(m), M("bd"), v, OP.mult)
-    ms(M("ones"), 1.0)
+    ts(A("cb", 256, 128), A("cf", 128, 128), -1.0, OP.mult, -0.25, OP.add)
+    tt(M("bdp"), A("cb", 256, 128), M("bd"), OP.mult)
     ts(A("cb", 0, 128), A("cf", 128, 128), col(P), OP.is_gt, -1.0, OP.mult)
     tt(A("cb", 128, 128), A("cb", 0, 128), M("bd"), OP.mult)
     tt(M("w1"), A("cb", 128, 128), M("i1"), OP.add)
@@ -220,205 +262,287 @@ def build():
     tt(A("cb", 384, 128), A("cb", 256, 128), M("bd"), OP.mult)
     ts(A("cb", 0, 128), M("i1"), -33.0 / 32, OP.mult)
     tt(M("warg"), A("cb", 384, 128), A("cb", 0, 128), OP.add)
-    ts(A("zz", 0, 144), A("iot", 0, 144), col(G16), OP.is_equal, col(PW), OP.mult)
     ts(A("zz", 144, 144), A("iot", 0, 144), col(G16), OP.is_equal)
-    ts(A("zz", 288, 144), A("iot", 0, 144), col(G16), OP.is_equal, col(K16), OP.mult)
-    act(A("zz", 432, 144), A("zz", 0, 144), AF.Copy, scale=0.5)
-    act(M("w2h"), M("w2"), AF.Copy, scale=-0.5)
+    ts(A("zz", 0, 144), A("zz", 144, 144), col(PW), OP.mult)
+    ts(A("zz", 288, 144), A("zz", 144, 144), col(K16), OP.mult)
+    cp(A("zh", 0, 144), A("zz", 144, 144))
+    act(A("zz", 432, 288), A("zz", 0, 288), AF.Copy, scale=0.5)
+    for sg in sorted(set(signs(s, c) for s in range(1, STEPS) for c in range(2)) - {0}):
+        ts(A("sgc", 3 * sg, 1), col(P), sg - 0.5, OP.is_lt, -32767.5, OP.mult)
+        ts(A("sgc", 3 * sg + 2, 1), col(P), sg - 0.5, OP.is_lt, 32767.5, OP.mult)
+    for sg in sorted(set(signs(0, c) for c in range(2)) - {0}):
+        ts(A("cf", 448, 1), col(P), sg - 0.5, OP.is_lt, -8.0, OP.mult)
+        ts(A("sgc", 3 * sg + 1, 1), A("cf", 448, 1), 1.0, OP.add)
     iota(A("tmpb", 0, 64), [[4, 64]], 6, 0)
     for r in range(16):
         if r % 2:
             ts(A("tk", 64 * r, 64), A("tmpb", 0, 64), A("cf", 432 + r, 1), OP.mult)
         else:
             act(A("tk", 64 * r, 64), A("tmpb", 0, 64), AF.Copy, scale=A("cf", 432 + r, 1))
-    ts(A("cf", 496, 8), A("iot", 0, 8), 16.0, OP.mult, col(P), OP.add)
-    ts(A("basel", 0, 8), A("cf", 496, 8), 16.0, OP.mult, -16.0, OP.add)
+    ts(A("lanel", 0, 16), A("cf", 384, 16), 16.0, OP.mult, col(P), OP.add)
+    U = A("lanel", 0, 8)
+    ts(A("basel", 0, 8), U, 16.0, OP.mult, -16.0, OP.add)
+    ms(A("thl", 8, 16), 0.5)
+    ms(A("thl", 24, 8), 200000.0)
+    ts(A("thl", 0, 8), U, 16.0, OP.mult, -0.5, OP.add)
     for c in range(2):
-        ts(A("lanel", 8 * c, 8), A("cf", 496, 8), float(LANE0[c] - 160 * 256), OP.add, 1.0 / 256, OP.mult)
-    ms(A("thl", 8, 24), 0.5)
-    ts(A("thl", 0, 8), A("cf", 496, 8), 16.0, OP.mult)
-    JJ, FF, JN0, NF = range(4)
+        ms(A("yy%d" % c, 2048, 16), 0.0)
+    if any(PAR["KM"][s][c] for s in range(1, STEPS) for c in range(2)):
+        ms(A("thl", 40, 16), 0.5)
+        ms(A("thl", 56, 8), 8000.0)
+        ts(A("thl", 32, 8), U, -16.0, OP.mult, 16.5, OP.add)
+        for k in range(16):
+            if k % 2:
+                ts(A("kmw", 128 * k, 128), M("i1"), 4.0 ** (15 - k), OP.mult)
+            else:
+                act(A("kmw", 128 * k, 128), M("i1"), AF.Copy, scale=4.0 ** (15 - k))
+        ts(col(KT), col(IPW), col(IPW), OP.mult, 0.9, OP.mult)
+        ts(A("cb", 384, 128), A("cf", 128, 128), col(P), OP.is_ge, 2.0 ** 41, OP.mult)
+        ts(A("cb", 384, 128), A("cb", 384, 128), -2.0 ** 40, OP.add)
+        tt(M("tri"), A("cb", 384, 128), M("bd"), OP.mult)
+    DD, NF, NN, FL = range(4)
+    for i, (c0, w) in enumerate(((16, 1), (16, 1), (402, 1), (16, 1), (16 - 2048, 2048), (402, 1))):
+        act(A("con", 8 * i, 8), U, AF.Identity, bias=c0 / w, scale=3.0 / w)
     ST2 = {
-        0: [(768, 1, [("in384", JJ)]), (768, 1, [("in384", JJ)]), (386, 1, [("in384", JJ)]),
-            (1, 0, [("in1", JJ)]), (0, 0, [("i1", JJ)]), (1, 0, [("in1", JJ)])],
-        1: [(768, 1, [("in768", JJ), ("i384", JN0)]), (768, 1, [("in768", JJ), ("i384", FF)]), (386, 1, [("in384", JJ)]),
-            (1, 0, [("in1", JJ)]), (0, 0, [("i1", FF)]), (1, 0, [("in1", JJ)])],
-        2: [(1537, 1, [("in768", JJ), ("in1", FF), ("i384", JN0), ("in768", NF)]),
-            (1152, 1, [("in768", JJ), ("i384", FF), ("in384", NF)]),
-            (1154, 1, [("in384", JJ), ("in768", NF)]),
-            (1, 0, [("in1", JJ)]), (-1, 0, [("i1", FF), ("i1", NF)]), (2, 0, [("in1", JJ), ("in1", NF)])],
+        0: [[("in2k", DD)], [("in2k", DD)], [("in384", DD)], [("i1", DD)]],
+        1: [[("in2k", DD), ("i1", NF), ("i384", NN)], [("in2k", DD), ("i384", NF)], [("in384", DD)], [("i1", DD)]],
+        2: [[("in2k", DD), ("i1", NF), ("i384", NN), ("in2k", FL)], [("in2k", DD), ("i384", NF), ("in2k", FL)],
+            [("in384", DD), ("in2k", FL)], [("i1", DD), ("i1", FL)]],
     }
-    for t in range(3):
-        for i, (c0, lane, _) in enumerate(ST2[t]):
-            act(A("con", 56 * t + 8 * i, 8), A("cf", 496, 8), AF.Identity, bias=float(c0), scale=3.0 * lane)
+    ST2[3] = [ST2[2][0], [("ia", NF), ("ib", NF), ("i1", NN), ("in1", FL)], ST2[2][2], ST2[2][3]]
     cp(A("wl", 0, 1024), A("ivi", 0, 1024))
     for s in range(STEPS):
         for c in range(2):
-            if s == 0:
-                ms(A("win0%d" % c, 0, 384), NEG)
-            iota(A("win%d%d" % (s, c), 384, 784), [[0, 784]], int(NEG), 0)
-    for c in range(2):
-        ms(A("el0%d" % c, 0, 16), 0.0)
-        cp(A("el0%d" % c, 0, 8, 2), A("e0i", LANE0[c] // 16, 8))
+            w = 400 if s else 784
+            iota(A("win%d%d" % (s, c), 0, w), [[0, w]], -126 if s == STEPS - 1 else int(NEG), 0)
+    ms(A("el0", 0, 32), 0)
+    cp(A("el0", 0, 16, 2), A("e0i", 0, 16))
 
     WL, TAB = A("wl", 0, 1024), A("tab", 0, 8192)
-    ring = {"b": 0, "t": 0, "a": 0, "d": 0, "e": 0}
-    RB, TB = "ps3", "ps4"
-    slots = [("ps5", 128), ("ps6", 128), ("ps7", 0), ("ps5", 256), ("ps6", 256), ("ps7", 128), ("ps5", 384), ("ps6", 384)]
+    ring = {"b": 0, "c": 0, "t": 0, "a": 0, "e": 0, "d": 0}
+    NB = PAR["NB"]
+    RB, TB = "ps%d" % NB, "ps%d" % (NB + 1)
 
     def slot(n=128):
-        b, o = slots[ring["t"] % len(slots)]
-        ring["t"] += 1
+        b, o = ring["t"].pop(0)
         return A(b, o, n)
+
+    def places(part, s, c):
+        own = "ps%d" % (6 + c)
+        l0, l1, q2, l2 = [(own, o) for o in (320, 256, 288, 128)]
+        soon = s > 1 and PAR["EARLY"][s][c]
+        v = (own, 384) if soon else (own, 128)
+        m01, s01 = (own, 384), (own, 256)
+        if NB == 3 and not PAR["APART"]:
+            l0, l1, q2, l2, m01 = [("ps5", 256 * c + o) for o in (96, 0, 32, 64, 128)]
+        if (s, c) == (STEPS - 1, 1):
+            l0, l1, q2, l2, m01, v, s01 = [("ps%d" % b, o) for b, o in ((0, 0), (1, 0), (0, 128), (1, 128), (2, 0), (2, 128), (0, 256))]
+        if part is tail:
+            return (([(own, 128), (own, 0), (own, 128)] if s else []) + ([m01] if s > 1 else []) + ([l0] if soon else [])
+                    + [l1, q2] + ([v, s01] if s > 1 else []) + [(own, 0), l2])
+        return [(own, 0), (own, 128), (own, 0)]
+
+    def aside(s):
+        return not PAR["APART"] and s > 0 and any(PAR["KM"][s])
 
     def names(s, c):
         w = "win%d%d" % (s, c)
-        d = {"P0": A(w, 0, 128, 3), "P1": A(w, 1, 128, 3), "K": A(w, 2, 128, 3), "z": A(w, 384, 128, 3), "Kd": A(w, 386, 128, 3),
-             "win": A(w, 0, 1168), "e": A("el%d%d" % (s, c), 0, 8, 2), "A": A("el%d%d" % (s, c), 1, 8, 2),
-             "c16": "c16_%d" % c, "Y": "yy%d" % c, "me": "me%d" % c}
-        for i, x in enumerate(["e16", "ea16", "ed16", "d16", "j16", "o0", "o1", "oK", "ja16"]):
+        u16, si = "u16_%d" % (s % 2), "si%d" % (s % 2)
+        d = {"P0": A(w, 400, 128, 3), "P1": A(w, 401, 128, 3), "K": A(w, 402, 128, 3), "z": A(w, 16, 128, 3), "Kd": A(w, 18, 128, 3),
+             "win": A(w, 0, 784), "e": A("el%d" % s, 16 * c, 8, 2), "A": A("el%d" % s, 16 * c + 1, 8, 2),
+             "c16": "c16_%d" % c, "Y": "yy%d" % c, "me": "me%d" % c, "tb": "tb%d" % c,
+             "e16": A(u16, 8 * c, 8), "ed16": A(u16, 32 + 8 * c, 8), "d16": A(u16, 48 + 8 * c, 8), "de": A(si, 48 + 8 * c, 8),
+             "old": A("wf", 256 + 128 * c, 128), "t": A("wf", 512 + 128 * c, 128), "dv": A("ps%d" % (6 + c), 256, 128) if aside(s) else A(RB, 256 + 128 * c, 128),
+             "R": A(RB, 0, 128), "cn": A("ps5", 0, 128) if PAR["APART"] else A(RB, 128, 128),
+             "km": A("ps5", 128 + 128 * c, 128) if PAR["APART"] else A(RB, 256 + 128 * c, 128)}
+        for i, x in enumerate(["j16", "o0", "o1", "oK", "ja16"]):
             d[x] = A("l16_%d" % c, 8 * i, 8)
-        for i, x in enumerate(["e5", "ed", "b"]):
-            d[x] = A("li%d" % c, 8 * i, 8)
-        d["c1"], d["c2"] = A("lf%d" % c, 24, 8), A("lf%d" % c, 112, 8)
-        d["df"], d["m1"], d["m2"] = A("lf%d" % c, 0, 8), A("lf%d" % c, 8, 8), A("lf%d" % c, 16, 8)
-        d["ea"], d["e4"] = A("lf%d" % c, 96, 8), A("lf%d" % c, 104, 8)
-        for i, x in enumerate(["x0", "old", "dv", "t", "Rs", "r"]):
+        for i, x in enumerate(["Rs", "r"]):
             d[x] = A("rf%d" % c, 128 * i, 128)
-        d["dv"] = A(RB, 128 + 128 * c, 128)
-        for i, x in enumerate(["xi", "v", "bt", "bt2"]):
+        for i, x in enumerate(["bt", "bt2"]):
             d[x] = A("ri%d" % c, 128 * i, 128)
-        for i, x in enumerate(["cr", "thq", "mid", "h", "okb", "X", "oh", "gb", "F", "ohq", "cB", "y1p", "ad", "zg", "E"]):
+        for i, x in enumerate(["cr", "mid", "h", "okb", "X", "oh", "gb", "ohq", "cB", "zg", "ad", "thq"]):
             d[x] = A("rb%d" % c, 128 * i, 128)
-        for i, x in enumerate(["J", "f", "jn0", "nf", "row", "lab", "s0", "s1"]):
+        for i, x in enumerate(["J", "f", "n0", "E"]):
             d[x] = A("stk%d" % c, 128 * i, 128)
+        for i, x in enumerate(["ne", "s0", "s1", "D"]):
+            d[x] = A("sh%d" % c, 128 * i, 128)
         return d
 
     def early(s, c):
         d = names(s, c)
-        nv = VSHARE[(s, c)]
-        pieces = []
-        if s > 0 and LANE0[c] == 0 and SPLIT[s]:
-            e, e16 = d["e"], d["e16"]
-            for hf in range(2):
-                cp(A(e16[0], e16[1] + 4 * hf, 4), A(e[0], 8 * hf, 4, 2))
-                cp(A(d["c16"], 64 * hf, 64), IND(WL, A(e16[0], e16[1] + 4 * hf, 4)))
-            parts = [(0, 64, min(SPLIT[s] - 1, nv)), (64, 128, min(64, nv - min(SPLIT[s] - 1, nv)))]
-        else:
-            cp(d["e16"], d["e"])
-            cp(A(d["c16"], 0, 128), IND(WL, d["e16"]))
-            parts = [(0, 128, nv)]
-        for lo, end, k in parts:
-            if k:
-                pieces.append(("V", lo, k))
-            lo += k
-            while lo < end:
-                hi = min(end, lo + GP[0])
-                pieces.append(("S", lo, hi - lo))
-                lo = hi
+        cp(d["e16"], d["e"])
+        cp(A(d["c16"], 0, 128), IND(WL, d["e16"]))
+        nv = PAR["VSHARE"][s][c]
+        pieces = [("V", 128 - nv, nv)] if nv else []
+        lo = 0
+        while lo < 128 - nv:
+            hi = min(128 - nv, lo + PAR["GP"])
+            pieces.append(("S", lo, hi - lo))
+            lo = hi
+        if s == 0 and PAR["UN"][s][c][0][0] == 8:
+            pieces = [x for h in (0, 64) for x in (("V", h, nv // 2), ("S", h + nv // 2, 64 - nv // 2))]
         for e, lo, n in pieces:
             o, i = A(d["Y"], 16 * lo, 16 * n), IND(TAB, A(d["c16"], lo, n))
             if e == "V":
-                cp(o, i)
+                ts(o, i, -125.0, OP.add)
             else:
-                act(o, i, AF.Copy)
+                act(o, i, AF.Identity, bias=-125.0)
         if s == 0:
-            act(d["mid"], IND(A("tk", 0, 1024), d["e16"]), AF.Identity, bias=-6.0)
-            ts(d["K"], d["mid"], -125.0, OP.add)
-        tt(d["ea"], d["e"], d["A"], OP.add)
-        cp(d["ea16"], d["ea"])
-        act(d["e4"], d["e"], AF.Identity, bias=1.0, scale=4.0)
-        tt(d["e5"], d["e4"], d["ea"], OP.add)
-        ts(d["ed"], d["e5"], 1023, OP.bitwise_and)
-        cp(d["ed16"], d["ed"])
-        act(A("lq%d" % c, 56, 8), d["e"], AF.Identity, bias=160 - 0.498, scale=1.0 / 256)
-        tt(d["df"], A("lq%d" % c, 56, 8), A("lanel", 8 * c, 8), OP.add)
-        ts(d["d16"], d["df"], 256.0, OP.mult)
-        act(d["x0"], IND(WL, d["e16"]), AF.Copy, scale=37.0)
-        act(d["old"], IND(WL, d["d16"]), AF.Copy)
-        tt(d["xi"], IND(A("iot", 0, 1032), d["ea16"]), d["x0"], OP.add)
-        ts(d["v"], d["xi"], 8191, OP.bitwise_and)
-        tt(d["dv"], d["v"], d["old"], OP.subtract)
-        act(d["Kd"], IND(A("tk", 0, 1024), d["ed16"]), AF.Identity, bias=NEG)
+            act(d["K"], IND(A("tk", 0, 1024), d["e16"]), AF.Identity, bias=NEG)
+
+    def side(s, c):
+        u16, si = "u16_%d" % (s % 2), "si%d" % (s % 2)
+        e, a = A("el%d" % s, 0, 16, 2), A("el%d" % s, 1, 16, 2)
+        ea, ed, dd, de, e4, e5, dq = [A(si, 16 * i, 16) for i in range(7)]
+        ts(e4, e, 4.0, OP.mult, 1.0, OP.add)
+        ts(dq, e, 5.0, OP.mult, 1.0, OP.add)
+        tt(e5, dq, a, OP.add)
+        tt(ea, e5, e4, OP.subtract)
+        ts(ed, e5, 1023, OP.bitwise_and)
+        ts(dq, e, 768, OP.bitwise_and)
+        tt(dd, dq, A("lanel", 0, 16), OP.add)
+        tt(de, ed, e, OP.subtract)
+        cp(A(u16, 16, 48), A(si, 0, 48))
+        x0, old, xi, v = A("wf", 0, 256), A("wf", 256, 256), A("wi", 0, 256), A("wi", 256, 256)
+        act(x0, IND(WL, A(u16, 0, 16)), AF.Copy, scale=37.0)
+        act(old, IND(WL, A(u16, 48, 16)), AF.Copy)
+        tt(xi, IND(A("iot", 0, 1032), A(u16, 16, 16)), x0, OP.add)
+        ts(v, xi, 8191, OP.bitwise_and)
+        if aside(s):
+            for k in range(2):
+                d = names(s, k)
+                act(d["dv"], d["old"], AF.Copy)
+                tt(d["dv"], A("wi", 256 + 128 * k, 128), d["dv"], OP.subtract)
+        elif PAR["OFF"][0][s % 2]:
+            act(A(RB, 256, 256), old, AF.Copy)
+            tt(A(RB, 256, 256), v, A(RB, 256, 256), OP.subtract)
+        else:
+            tt(A(RB, 256, 256), v, old, OP.subtract)
+        for k in range(2):
+            d = names(s, k)
+            act(d["Kd"], IND(A("tk", 0, 1024), d["ed16"]), AF.Identity, bias=NEG)
+
+    def test(out, bank, how):
+        if how:
+            a2 = A("ab%d" % (ring["e"] % 3), 0, cnt(out))
+            ring["e"] += 1
+            act(a2, bank, AF.Abs)
+            if how == 1:
+                ts(out, a2, 7.9, OP.is_le)
+            else:
+                act(out, a2, AF.Sign, bias=7.9, scale=-1.0)
+        else:
+            ts(out, bank, CM, OP.add, CM, OP.is_equal)
 
     def bulk(s, c):
         d = names(s, c)
-        ts(d["cr"], d["K"], -128.0, OP.is_gt)
+        units = PAR["UN"][s][c]
+        dv = s and any(x[2] for x in units)
         if s > 0:
-            ts(d["thq"], d["K"], -128.0, OP.is_lt, 10.0 / 1024, OP.max)
-            u = A("ps5", 0, 128)
-            mm(grp(u, [(M("ih"), d["P0"]), (M("ih"), d["P1"]), (M("in512"), d["cr"])]))
+            ts(d["cr"], d["K"], -128.0, OP.is_gt)
+            if PAR["OFF"][s][c]:
+                act(d["n0"], d["P0"], AF.Relu, bias=-130.0, scale=-1.0)
+            else:
+                ts(d["n0"], d["P0"], -128.0, OP.is_lt)
+            u = slot()
+            half = [(M("i1"), d["P0"])] if s == 1 else [(M("ih"), d["P0"]), (M("ih"), d["P1"])]
+            mm(grp(u, half + [(M("in512"), d["cr"])]))
             tt(d["mid"], u, d["K"], OP.max)
-            if s > 1:
-                hh = A("ps6", 0, 128)
-                mm(grp(hh, [(M("i1"), d["P0"]), (M("in1"), d["P1"])]))
-                act(d["h"], hh, AF.Abs, scale=0.5)
-            anyv = any(DV[(s, c)])
-            items = [(A(TB, 128 * j, 128), M("i1k"), d["thq"], True, True) for j in range(2 if anyv else 4)]
-            if anyv:
-                items.append((A(TB, 256, 128), M("i1"), d["mid"], True, True))
-            mm(items)
-        R = A(RB, 0, 128)
-        for b in range(4):
-            if s > 0 and DV[(s, c)][b]:
+            thq = d["cr"]
+        if s > 1:
+            thq = d["thq"]
+            ts(thq, d["K"], -128.0, OP.is_lt, 10.0 / 1024, OP.max)
+            hh = slot()
+            mm(grp(hh, [(M("i1"), d["P0"]), (M("in1"), d["P1"])]))
+            act(d["h"], hh, AF.Abs, scale=0.5)
+            w3 = slot()
+            mm(grp(w3, [(M("bd"), d["h"])]))
+            act(d["ad"], w3, AF.Sign, bias=0.5, scale=-1.0)
+        if s > 0:
+            mm([(A(TB, 128 * j, 128), M("i10" if s == 1 else "i1k"), thq, True, True) for j in range(4)])
+        if dv:
+            mm([(A("ps%d" % (6 + c), 384, 128), M("i1"), d["mid"], True, True)])
+        if s == 0 and units[0][0] == 8:
+            for h in range(2):
+                for b in range(2):
+                    bank = "ps%d" % (ring["b"] % NB)
+                    ring["b"] += 1
+                    items = []
+                    for j in range(8):
+                        items += grp(A(bank, 64 * j, 64), [(M("i15"), A(d["Y"], 1024 * h + 8 * b + j, 64, 16)),
+                                                           (M("in15"), A(d["K"][0], 402 + 192 * h, 64, 3))])
+                    mm(items)
+                    sg = 8 * b < signs(s, c)
+                    test(A(d["me"], 1024 * h + 512 * b, 512), A(bank, 0, 512), 2 if sg else min(units[b][1], 1))
+                    mm(grp(A(RB, 64 * h, 64), [(Z(1 + 3 * sg, 8 * b + j), A(d["me"], 1024 * h + 512 * b + 64 * j, 64)) for j in range(8)],
+                           start=b == 0, stop=b == 1))
+                    ops[-1]["w"].append(d["R"])
+            return
+        k0 = 0
+        for b, (nk, how, byv) in enumerate(units):
+            w = 128 * nk
+            if byv and s:
                 bank = "dd%d" % (ring["d"] % 2)
                 ring["d"] += 1
-                for j in range(4):
-                    tt(A(bank, 128 * j, 128), A(d["Y"], 4 * b + j, 128, 16), A(TB, 256, 128), OP.subtract)
+                for j in range(nk):
+                    tt(A(bank, 128 * j, 128), A(d["Y"], k0 + j, 128, 16), A("ps%d" % (6 + c), 384, 128), OP.subtract)
             else:
-                bank = "ps%d" % (ring["b"] % 3)
+                bank = "ps%d" % (ring["b"] % (PAR["NB1"] if s else NB))
                 ring["b"] += 1
                 items = []
-                for j in range(4):
-                    items += grp(A(bank, 128 * j, 128), [(M("i15" if s == 0 else "i1"), A(d["Y"], 4 * b + j, 128, 16)),
-                                                         (M("in15" if s == 0 else "in1"), d["mid"])])
-                mm(items)
-            me = A(d["me"], 512 * b, 512)
+                for j in range(nk):
+                    items += grp(A(bank, 128 * j, 128), [(M("i1" if s else "i15"), A(d["Y"], k0 + j, 128, 16)),
+                                                         (M("in1"), d["mid"]) if s else (M("in15"), d["K"])])
+                mms(items, A(bank, 0, w))
+            x = A(bank, 0, w)
+            me = A(d["me"], 128 * k0, w)
             if s > 0:
-                a, n = A("aa%d" % (ring["a"] % 3), 0, 512), A("nc%d" % (ring["a"] % 3), 0, 512)
+                a, n = A("aa%d" % (ring["a"] % 3), 0, w), A("nc%d" % (ring["a"] % 3), 0, w)
                 ring["a"] += 1
-                act(a, A(bank, 0, 512), AF.Abs, bias=-125.0 * SC, scale=SC)
-                if NCS[(s, c)][b]:
-                    bank = "ps%d" % (ring["b"] % 3)
-                    ring["b"] += 1
-                    mm([(A(bank, 0, 512), M("i1"), a, True, False)]
-                       + [(A(bank, 128 * j, 128), M("in1k"), d["thq"], False, j == 3) for j in range(4)])
-                    act(n, A(bank, 0, 512), AF.Relu)
-                elif anyv:
-                    for hf in range(2):
-                        tt(A(n[0], 256 * hf, 256), A(a[0], 256 * hf, 256), A(TB, 0, 256), OP.is_ge)
-                else:
-                    tt(n, a, A(TB, 0, 512), OP.is_ge)
-                bank = "ps%d" % (ring["b"] % 3)
-                ring["b"] += 1
-                x = A(bank, 0, 512)
-                items = [(x, M("ilam"), a, True, False)]
-                if s > 1:
-                    items += [(A(bank, 128 * j, 128), M("inls"), d["h"], False, False) for j in range(4)]
-                items += [(x, M("bd1k"), n, False, True)]
-                mm(items)
-            sg = s == 1 and EARLY[(s, c)]
-            if sg:
-                act(me, A(bank, 0, 512), AF.Sign, bias=7.9, scale=-1.0)
-            elif ABS2[(s, c)][b]:
-                a2 = A("ab%d" % (ring["e"] % 2), 0, 512)
-                ring["e"] += 1
-                act(a2, A(bank, 0, 512), AF.Abs)
-                ts(me, a2, 7.9, OP.is_le)
+                act(a, x, AF.Abs, scale=SC)
+                tt(n, a, A(TB, 0, w), OP.is_lt if s == 1 else OP.is_ge)
+                bank = "ps%d" % (PAR["NB1"] + ring["c"] % (NB - PAR["NB1"]))
+                ring["c"] += 1
+                x = A(bank, 0, w)
+            sg = k0 < signs(s, c)
+            if s == 1 and sg:
+                mm([(x, M("in1"), a, True, False), (x, M("bd10"), n, False, True)])
+                act(me, x, AF.Sign, bias=-0.25)
+            elif s == 1:
+                mm([(x, M("bd10"), n, True, True)])
+                tt(me, a, x, OP.is_lt)
             else:
-                ts(me, A(bank, 0, 512), CM, OP.add, CM, OP.is_equal)
-            terms = [(M("w2"), d["cr"])] if b == 0 else []
-            if sg and b == 0:
-                terms.append((M("w2h"), M("ones")))
-            terms += [(Z(3 if sg else 0, 4 * b + j), A(d["me"], 512 * b + 128 * j, 128)) for j in range(4)]
-            mm(grp(R, terms, start=b == 0, stop=b == 3))
+                if s > 1:
+                    mms([(x, M("ilam"), a, True, False)]
+                       + [(A(bank, 128 * j, 128), M("inls"), d["h"], False, False) for j in range(nk)] + [(x, M("bd1k"), n, False, True)])
+                test(me, x, 2 if sg else min(how, 1))
+            mes = [A(d["me"], 128 * (k0 + j), 128) for j in range(nk)]
+            terms = [(M("w2"), d["cr"])] if b == 0 and s > 0 else []
+            terms += [(Z((0 if s else 1) + 3 * sg, k0 + j), mes[j]) for j in range(nk)]
+            k0 += nk
+            apart = PAR["APART"]
+            items = grp(d["R"], terms, start=b == 0, stop=k0 == 16 and (s == 0 or apart))
+            if s > 0:
+                terms = [(M("in32"), d["cr"])] if b == 0 else []
+                km = PAR["KM"][s][c]
+                more = grp(d["cn"], terms + [(M("ih" if sg else "i1"), m) for m in mes], start=apart and b == 0, stop=k0 == 16 and not km)
+                if km:
+                    more += grp(d["km"], [(A("kmw", 128 * (k0 - nk + j), 128), m) for j, m in enumerate(mes)], start=False, stop=k0 == 16)
+                if apart:
+                    mms(items)
+                    items = []
+                items += more
+            mms(items, d["cn"] if apart and s else A(RB, 0, 256))
 
     def join(s, c):
         d = names(s, c)
-        R = A(RB, 0, 128)
-        ts(d["okb"], R, 0.0, OP.is_equal)
+        sg = signs(s, c)
+        ts(d["okb"], d["R"], A("sgc", 3 * sg + (s == 0), 1) if sg else 0.0 if s else 1.0, OP.is_equal)
         if s > 0:
-            act(d["Rs"], R, AF.Relu)
+            act(d["X"], d["cn"], AF.Exp, bias=0.5 * sg * math.log(64.0) if sg else None, scale=math.log(64.0))
+            if not PAR["KM"][s][c]:
+                act(d["Rs"], d["R"], AF.Relu, bias=A("sgc", 3 * sg + 2, 1) if sg else None)
         u1 = slot()
         mm(grp(u1, [(M("w1"), d["okb"])]))
         act(d["f"], u1, AF.Relu)
@@ -433,13 +557,26 @@ def build():
     def tail(s, c):
         d = names(s, c)
         last = s == STEPS - 1
+        soon = s > 1 and PAR["EARLY"][s][c]
         J = d["f"]
-        if s > 0:
+        km = s > 0 and PAR["KM"][s][c]
+        if km:
+            J, oh = d["J"], d["oh"]
+            rg = slot()
+            if km > 1:
+                oh = d["gb"]
+                mm(grp(rg, [(M("warg"), d["X"])]))
+                ts(oh, rg, -8.0, OP.is_lt)
+            mm(grp(rg, [(M("warg"), d["X"]), (M("bdbig"), d["f"])]))
+            ts(d["oh"], rg, -8.0, OP.is_lt)
+            tt(d["mid"], d["km"], oh, OP.mult)
+            slot()
+            u2 = slot()
+            u2 = A(u2[0], 0, 128)
+            mm(grp(u2, [(M("bd"), d["mid"]), (M("tri"), d["f"])]))
+            ts(J, u2, col(KT), OP.is_ge)
+        elif s > 0:
             J = d["J"]
-            cn = slot()
-            sg = s == 1 and EARLY[(s, c)]
-            mm(grp(cn, [(M("in32"), d["cr"])] + [(M("ih" if sg else "i1"), A(d["me"], 128 * k, 128)) for k in range(16)]))
-            act(d["X"], cn, AF.Exp, bias=8 * math.log(64.0) if sg else None, scale=math.log(64.0))
             rg = slot()
             mm(grp(rg, [(M("warg"), d["X"]), (M("bdbig"), d["f"])]))
             ts(d["oh"], rg, -8.0, OP.is_lt)
@@ -451,98 +588,83 @@ def build():
             u2 = slot()
             mm(grp(u2, [(M("i1"), d["f"]), (M("w1"), d["gb"])]))
             act(J, u2, AF.Relu)
-            w0 = slot()
-            mm(grp(w0, [(M("bd"), d["f"]), (M("in1"), d["P0"])]))
-            act(d["jn0"], w0, AF.Relu, bias=NEG / 16, scale=1.0 / 16)
-        t = min(s, 2)
-        YW = A(d["Y"], 0, 2048)
+        YW = A(d["Y"], 0, 2064)
         base = (A("basel", 0, 8), M("i1"))
-        zg = d["z"]
-        if s > 1:
-            w2 = slot()
-            mm(grp(w2, [(M("bd"), d["f"]), (M("bdh"), d["h"])]))
-            ts(d["nf"], w2, 1.0, OP.is_le, 1.0 / 16, OP.mult)
-            if last:
-                w3 = slot()
-                mm(grp(w3, [(M("bd"), d["h"])]))
-                act(d["ad"], w3, AF.Relu, bias=1.0, scale=-1.0)
-            if EARLY[(s, c)]:
-                l0 = slot(8)
-                tolist(l0, 2, d["f"], 8, [base])
-                cp(d["ja16"], l0)
-                act(d["z"], IND(YW, d["ja16"]), AF.Identity, bias=-125.0)
-                zg = d["zg"]
-        nq = 8 * (1, 3, 4)[t]
-        l1 = slot(nq)
-        tolist(l1, 2, J, nq, [base])
-        cp(d["j16"], A(l1[0], l1[1], 8))
-        act(zg, IND(YW, d["j16"]), AF.Identity, bias=-125.0)
-        lq, lf = "lq%d" % c, "lf%d" % c
-        tt(A(lq, 0, nq), l1, A("thl", 0, nq), OP.is_ge)
-        q2 = slot(48)
-        items = []
-        for i, (_, _, terms) in enumerate(ST2[t]):
-            if last and i == 1:
-                terms = [("in384", FF), ("i384", JN0), ("in384", NF), ("i1", JJ), ("in1", FF)]
-            items += grp(A(q2[0], q2[1] + 8 * i, 8), [(M(m), A(lq, 8 * x, 8)) for m, x in terms])
-        mm(items)
-        tt(A(lf, 32, 48), q2, A("con", 56 * t, 48), OP.add)
-        dead, keep, again = [A(lf, 32 + 8 * i, 8) for i in (3, 4, 5)]
-        sl, sb = "sl%d%d" % (s, c), "sb%d%d" % (s, c)
-        lo = LANE0[c]
-        en = A("oye", lo // 16, 8) if last else A(sl, 0, 8, 2)
-        tt(d["m1"], dead, d["ed"], OP.mult)
-        tt(d["m2"], keep, d["e"], OP.mult)
-        tt(en if s == 0 else d["c1"], d["m1"], d["m2"], OP.add)
-        tt(A("oya", lo // 16, 8) if last else A(sl, 1, 8, 2), again, d["A"], OP.add)
+        zg = zf = d["z"]
         if s > 1:
             m01 = slot()
-            terms = [(M("ih"), d["P0"]), (M("ih"), d["P1"]), (M("in1"), d["h"]), (M("i16k"), d["nf"])]
+            mm(grp(m01, [(M("ih"), d["P0"]), (M("ih"), d["P1"]), (M("in1"), d["h"]), (M("i512"), d["ad"]), (M("bdn1k"), d["f"])]))
+            act(d["E"], m01, AF.Identity, bias=1536.0)
+        if soon:
+            l0 = slot(8)
+            tolist(l0, 2, d["f"], 8, [base])
+            cp(d["ja16"], l0)
+            zf = d["zg"]
+            tt(zf, IND(YW, d["ja16"]), d["E"], OP.min)
+        nq = 8 * (1, 3, 4, 4)[s]
+        l1 = slot(nq)
+        if km:
+            tolist(l1, 1, J, nq, [(A("basel", 0, 8), M("in1"))])
+            ts(d["j16"], A(l1[0], l1[1], 8), -1.0, OP.mult, 32.0, OP.add)
+        else:
+            tolist(l1, 2, J, nq, [base])
+            cp(d["j16"], A(l1[0], l1[1], 8))
+        if s > 1:
+            tt(zg, IND(YW, d["j16"]), d["E"], OP.min)
+        else:
+            act(zg, IND(YW, d["j16"]), AF.Copy)
+        lq, lf, li = "lq%d" % c, "lf%d" % c, "li%d" % c
+        tt(A(lq, 0, nq), l1, A("thl", 32 * bool(km), nq), OP.is_lt)
+        q2 = slot(32)
+        items = []
+        for i, terms in enumerate(ST2[s]):
+            items += grp(A(q2[0], q2[1] + 8 * i, 8), [(M(m), A(lq, 8 * x, 8)) for m, x in terms])
+        mm(items)
+        tt(A(lf, 0, 24), A(q2[0], q2[1], 24), A("con", 24 * last, 24), OP.add)
+        sl, sb = "sl%d%d" % (s, c), "sb%d%d" % (s, c)
+        lo = 128 * c
+        en = A(sl, 0, 8, 2)
+        tt(A("oya", 8 * c, 8) if last else A(sl, 1, 8, 2), A(q2[0], q2[1] + 24, 8), d["A"], OP.add)
+        tt(A(lf, 24, 8), A(lq, 8 * DD, 8), d["de"], OP.mult)
+        tt(en if s == 0 else A(lf, 32, 8), A(lf, 24, 8), d["e"], OP.add)
+        if s > 1:
             v = slot()
-            if EARLY[(s, c)]:
-                mm(grp(m01, terms + [(M("in1"), d["z"])]))
-                act(d["E"], m01, AF.Relu, scale=-1.0)
-                mm(grp(v, [(M("inp"), M("ones")), (M("i8"), d["nf"]), (M("bd"), d["z"]), (M("bdn"), d["E"])]))
-            else:
-                mm(grp(m01, terms))
-                tt(d["F"], m01, d["z"], OP.min)
-                mm(grp(v, [(M("inp"), M("ones")), (M("i8"), d["nf"]), (M("bd"), d["F"])]))
+            mm(grp(v, [(M("inq"), d["ad"]), (M("bdp"), d["f"]), (M("bd"), zf)]))
             ts(d["r"], v, CM, OP.add, CM, OP.subtract)
             tt(d["ohq"], v, d["r"], OP.is_equal)
-            items = []
+            items, s01 = [], slot(256)
             for i, p in enumerate(("P0", "P1")):
-                more = [(M("in1k"), d["ad"])] if last and i else []
-                items += grp(A("ps7", 256 + 128 * i, 128), [(M("i15"), d[p])] + more + [(M("i1k"), d["oh"]), (M("in15"), zg)])
+                more = [(M("i512"), d["ad"]), (M("i1536"), d["oh"])] if last and i else [(M("i1k"), d["oh"])]
+                items += grp(A(s01[0], s01[1] + 128 * i, 128), [(M("i15"), d[p])] + more + [(M("in15"), zg)])
             mm(items)
-            ts(A(d["s0"][0], d["s0"][1], 256), A("ps7", 256, 256), CM - 1024, OP.add, CM, OP.is_equal)
+            ts(A(d["s0"][0], d["s0"][1], 256), s01, CM - 1024, OP.add, CM, OP.is_equal)
         if s > 0:
             cand = slot()
-            if s == 1:
-                mm(grp(cand, [(M("i1k"), d["oh"]), (M("i1"), zg)]))
-            elif EARLY[(s, c)]:
-                mm(grp(cand, [(M("i1k"), d["oh"]), (M("i1k"), d["ohq"]), (M("in1"), d["E"]), (M("i1"), zg)]))
-            else:
-                mm(grp(cand, [(M("i1k"), d["oh"]), (M("i1"), d["F"]), (M("i1k"), d["ohq"])]))
-            rw = slot()
-            mm(grp(rw, [(M("irow"), d["oh"])] + ([(M("irow"), d["ohq"])] if s > 1 else [])))
-            act(d["row"], rw, AF.Copy)
-            act(d["lab"], cand, AF.Relu, bias=-65.125, scale=0.25)
-            act(d["cB"], cand, AF.Identity, bias=-1024.0)
-            l2 = slot(16 * t)
-            tolist(l2, 1, d["row"], 16 * t, [])
-            tt(d["c2"], A(l2[0], l2[1], 8), d["c1"], OP.add)
-            tt(en, A(l2[0], l2[1] + 8, 8), d["c2"], OP.add)
+            more = [(M("iw"), d["ohq"])] if s > 1 else []
+            mm(grp(cand, [(M("iw"), d["oh"]), (M("iq"), zg)] + more))
+            ts(d["ne"], cand, 30.875 - 1024, OP.add, 0.0, OP.max)
+            act(d["cB"], cand, AF.Identity, bias=col(NW4), scale=4.0)
+            n2 = 8 if s == 1 else 24
+            l2 = slot(n2)
+            tolist(l2, "h", d["ne"], n2, [])
+            tt(A(li, 0, 8), A(l2[0], l2[1], 8), A(lf, 32, 8), OP.max)
+            ts(en, A(li, 0, 8), 1023, OP.bitwise_and)
         if not last:
-            send(s, c, "l", sl, "el%d%d" % (s + 1, c), 8)
+            send(s, c, "l", sl, "el%d" % (s + 1), 16 * c, 8)
+        else:
+            cp(A("oye", 8 * c, 8), en)
         if last:
-            ts(A(lf, 80, 16), A(l2[0], l2[1] + 16, 16), -384.0, OP.mult)
-            tt(A(lf, 32, 8), A(lf, 32, 8), A(l2[0], l2[1] + 16, 8), OP.subtract)
-            tt(A(lf, 40, 8), A(lf, 40, 8), A(lf, 80, 8), OP.add)
-            tt(A(lf, 40, 8), A(lf, 40, 8), A(lf, 88, 8), OP.add)
-        elif s > 1:
-            tt(A(lf, 32, 8), A(lf, 32, 8), A(l2[0], l2[1] + 16, 8), OP.subtract)
-            tt(A(lf, 40, 8), A(lf, 40, 8), A(l2[0], l2[1] + 24, 8), OP.add)
-        cp(A("l16_%d" % c, 40, 24), A(lf, 32, 24))
+            cp(d["oK"], A(lf, 16, 8))
+            tt(A(lf, 8, 8), A(lf, 8, 8), A(l2[0], l2[1] + 8, 8), OP.add)
+            tt(A(lf, 0, 8), A(lf, 0, 8), A(l2[0], l2[1] + 8, 8), OP.subtract)
+            tt(A(lf, 8, 8), A(lf, 8, 8), A(l2[0], l2[1] + 16, 8), OP.add)
+            cp(d["o0"], A(lf, 0, 8))
+            ts(d["o1"], A(lf, 8, 8), 2048.0, OP.mult)
+        else:
+            if s > 1:
+                tt(A(lf, 0, 8), A(lf, 0, 8), A(l2[0], l2[1] + 8, 8), OP.subtract)
+                tt(A(lf, 8, 8), A(lf, 8, 8), A(l2[0], l2[1] + 16, 8), OP.add)
+            cp(A("l16_%d" % c, 8, 24), A(lf, 0, 24))
         if not last:
             act(A(sb, 0, 128, 3), IND(d["win"], d["o0"]), AF.Copy)
             act(A(sb, 1, 128, 3), IND(d["win"], d["o1"]), AF.Copy)
@@ -550,16 +672,16 @@ def build():
                 cp(A(sb, 2, 128, 3), IND(d["win"], d["oK"]))
             else:
                 tt(A(sb, 2, 128, 3), IND(d["win"], d["oK"]), d["cB"], OP.max)
-            send(s, c, "r", sb, "win%d%d" % (s + 1, c), 192)
+            send(s, c, "r", sb, "win%d%d" % (s + 1, c), 400, 192)
         else:
             y0, y1, yk = A("oy0", lo, 128), A("oy1", lo, 128), A("oyk", lo, 128)
-            ts(y0, IND(d["win"], d["o0"]), 125.0, OP.add, -1.0, OP.max)
-            ts(y1, IND(d["win"], d["o1"]), 125.0, OP.add, -1.0, OP.max)
+            act(y0, IND(d["win"], d["o0"]), AF.Identity, bias=125.0)
+            act(y1, IND(d["win"], d["o1"]), AF.Identity, bias=125.0)
             tt(A(sb, 0, 128), IND(d["win"], d["oK"]), d["cB"], OP.max)
             ts(yk, A(sb, 0, 128), 125.0, OP.add, -1.0, OP.max)
 
-    def send(s, c, kind, src, dst, w):
-        blocks = [(h, LANE0[c] // 64 + h) for h in range(2)]
+    def send(s, c, kind, src, dst, at, w):
+        blocks = [(h, 2 * c + h) for h in range(2)]
         far = [(h, b) for h, b in blocks if b % N]
         name = "ar%s%d%d" % (kind, s + 1, c)
 
@@ -573,32 +695,31 @@ def build():
                 mask = sum(1 << e for e in eng[i * k:(i + 1) * k])
                 ad = topo.addr(to)
                 trs.append(RemoteDMATransfer(dst_ids=[DstId(rid=ad[0], pnc=ad[1])], dma_engine_mask=mask, remote_sem=T.sem[name],
-                                             src=R(A(src, h * w, w)), dst=R(A(dst, h * w, w))))
+                                             src=R(A(src, h * w, w)), dst=R(A(dst, at + h * w, w))))
                 X["sent"][0] += k
             return q.remote_dma_fused(trs, local_sem=T.sem["sent"])
-        add("G", call, [A(dst, h * w, w) for h, b in far], [A(src, h * w, w) for h, b in far], 700, sem=(name, "far"),
+        add("G", call, [A(dst, at + h * w, w) for h, b in far], [A(src, h * w, w) for h, b in far], 700, sem=(name, "far"),
             lat=1700 + 600 * len(far))
         for h, b in blocks:
             if b % N == 0:
-                act(A(dst, h * w, w), A(src, h * w, w), AF.Copy)
+                dma(A(dst, at + h * w, w), A(src, h * w, w), "lo%s%d" % (kind, s + 1), 2200)
 
     for s in range(STEPS):
-        for k, (part, c) in enumerate(((early, 0), (early, 1), (bulk, 0), (join, 0), (bulk, 1), (tail, 0), (join, 1), (tail, 1))):
+        for k, (part, c) in enumerate(((early, 0), (early, 1), (side, 0), (bulk, 0), (join, 0), (bulk, 1), (tail, 0), (join, 1), (tail, 1))):
             first = len(ops)
+            ring["t"] = places(part, s, c)
             part(s, c)
             for o in ops[first:]:
-                o["bias"] = BIAS[s][k]
+                o["part"] = (s, k)
 
     def store(name, buf, n):
-        add("Y", lambda q, R, X: q.dma_start(X["T"][name][:], R(A(buf, 0, n))), [], [A(buf, 0, n)], 60, sem=("outs", 16), lat=2500)
+        add("Y", lambda q, R, X: q.dma_start(X["T"][name][:], R(A(buf, 0, n))), [], [A(buf, 0, n)], 60, sem=("outs", 16), lat=2300 + 2 * n)
     for name, buf, n in (("yi", "wl", 1024), ("ye", "oye", 16), ("ya", "oya", 16), ("y0", "oy0", 256), ("yk", "oyk", 256), ("y1", "oy1", 256)):
         store(name, buf, n)
     return ops
 
 
-def plan():
-    ops = build()
-    n = len(ops)
+def links(ops):
     acc = {}
     pred = [set() for _ in ops]
     for i, o in enumerate(ops):
@@ -615,7 +736,274 @@ def plan():
                     old = [x for x in old if not (a[3] == 1 and a[1] <= x[2] and x[3] <= a[2])]
                 acc[a[0]] = old + [(i, kind, a[1], a[2], a[3])]
         o["banks"] = sorted(set(a[0] for a in o["r"] + o["w"] if isps(a)))
-        o["dep"] = sorted(pred[i])
+    return pred
+
+
+def arrange(ops, pred, succ, prio):
+    n = len(ops)
+    eng = [o["eng"] for o in ops]
+    left = [len(p) for p in pred]
+    dep = [0.0] * n
+    ready = {e: [] for e in "VSPGY"}
+    for i in range(n):
+        if left[i] == 0:
+            ready[eng[i]].append(i)
+    free = {e: 0.0 for e in "VSPGY"}
+    fin = [0.0] * n
+    bank, extra, order = {}, [[] for _ in ops], []
+    while len(order) < n:
+        best = None
+        for e in "VSPGY":
+            st = []
+            for i in ready[e]:
+                t = max(free[e], dep[i])
+                for b in ops[i]["banks"]:
+                    for e2, j in bank.get(b, {}).items():
+                        if e2 != e:
+                            t = max(t, fin[j] + HOP)
+                st.append((t, i))
+            if st:
+                t0 = min(st)[0]
+                if best is None or t0 < best[0]:
+                    best = (t0, st)
+        t, i = max((x for x in best[1] if x[0] <= best[0] + PAR["WIN"]), key=lambda x: (prio[x[1]], -x[1]))
+        o, e = ops[i], eng[i]
+        o["t"] = t
+        free[e] = t + o["cost"]
+        fin[i] = t + o["cost"] + o["lat"]
+        for b in o["banks"]:
+            extra[i] += [j for e2, j in bank.get(b, {}).items() if e2 != e]
+            bank.setdefault(b, {})[e] = i
+        order.append(i)
+        ready[e].remove(i)
+        for k in succ[i]:
+            if not (e == "P" and eng[k] == "P"):
+                dep[k] = max(dep[k], fin[i] + HOP)
+            left[k] -= 1
+            if left[k] == 0:
+                ready[eng[k]].append(k)
+    return max(fin), order, extra, fin
+
+
+def place(ops, gap, back, key, least):
+    n = len(ops)
+    left = [len(x) for x in gap]
+    est = list(least)
+    st = [0.0] * n
+    ready = [i for i in range(n) if left[i] == 0]
+    busy = {}
+    while ready:
+        i = min(ready, key=lambda x: key[x])
+        ready.remove(i)
+        o = ops[i]
+        c, e = o["cost"], o["eng"]
+        lists = [(busy.setdefault(e, []), 0.0)]
+        for b in o["banks"]:
+            lists += [(busy.setdefault(b + e2, []), HOP) for e2 in "VSP" if e2 != e]
+        t, moved = est[i], True
+        while moved:
+            moved = False
+            for l, pad in lists:
+                k = len(l) - 1
+                while k >= 0 and l[k][1] + pad > t:
+                    k -= 1
+                for a, z in l[k + 1:]:
+                    if a - pad >= t + c:
+                        break
+                    t, moved = z + pad, True
+        st[i] = t
+        for name in [e] + [b + e for b in o["banks"]]:
+            l = busy.setdefault(name, [])
+            k = len(l)
+            while k > 0 and l[k - 1][0] > t:
+                k -= 1
+            l.insert(k, (t, t + c))
+        for k, x in back[i]:
+            est[k] = max(est[k], t + c + x)
+            left[k] -= 1
+            if left[k] == 0:
+                ready.append(k)
+    return st
+
+
+def polish(ops, gap, back, order, rng):
+    n = len(ops)
+    code = {e: k for k, e in enumerate("VSPGY")}
+    eng = [code[o["eng"]] for o in ops]
+    cost = [o["cost"] for o in ops]
+    banks = [[int(b[2:]) for b in o["banks"]] for o in ops]
+    ends = [i for i in range(n) if not back[i]]
+
+    def run(order):
+        fin, why, last = [0.0] * n, [-1] * n, [-1] * 5
+        used = [[-1] * 3 for _ in range(8)]
+        for i in order:
+            e = eng[i]
+            t, w = 0.0, -1
+            for j, x in gap[i]:
+                if fin[j] + x > t:
+                    t, w = fin[j] + x, j
+            j = last[e]
+            if j >= 0 and fin[j] > t:
+                t, w = fin[j], j + n
+            for b in banks[i]:
+                u = used[b]
+                for e2 in range(3):
+                    if e2 != e and u[e2] >= 0 and fin[u[e2]] + HOP > t:
+                        t, w = fin[u[e2]] + HOP, u[e2] + n
+                u[e] = i
+            fin[i], why[i], last[e] = t + cost[i], w, i
+        i = max(ends, key=lambda x: fin[x] + ops[x]["lat"])
+        end = fin[i] + ops[i]["lat"]
+        return end + PAR["SOFT"] * sum(fin[x] for x in marks) / len(marks), fin, why, i, end
+    marks = [i for i in range(n) if ops[i]["part"] and (eng[i] == 3 or ops[i]["w"][0][0] == "wl")] + ends[-6:]
+    now = run(order)
+    best = (now[4], now[1])
+    moves = PAR["MOVES"]
+    for k in range(moves):
+        i = now[3] if rng.random() < 0.3 else marks[int(rng.integers(len(marks)))]
+        pairs = []
+        while i >= 0 and len(pairs) < 40:
+            w = now[2][i]
+            if w >= n:
+                w -= n
+                pairs.append((w, i))
+            i = w
+        if not pairs:
+            continue
+        j, i = pairs[int(rng.integers(len(pairs)))]
+        pos = {x: p for p, x in enumerate(order)}
+        a, b = pos[j], pos[i]
+        mid = order[a:b + 1]
+        keep = rng.random() < PAR["KEEP"]
+        if rng.random() < 0.5:
+            go, held = {i}, set() if eng[i] == eng[j] else {eng[i]}
+            for y in mid[-2::-1]:
+                if (keep and eng[y] in held) or any(z in go for z, _ in back[y]):
+                    go.add(y)
+                    held.add(eng[y])
+            if j in go:
+                continue
+            new = order[:a] + [x for x in mid if x in go] + [x for x in mid if x not in go] + order[b + 1:]
+        else:
+            go, held = {j}, set() if eng[i] == eng[j] else {eng[j]}
+            for y in mid[1:]:
+                if (keep and eng[y] in held) or any(z in go for z, _ in gap[y]):
+                    go.add(y)
+                    held.add(eng[y])
+            if i in go:
+                continue
+            new = order[:a] + [x for x in mid if x not in go] + [x for x in mid if x in go] + order[b + 1:]
+        got = run(new)
+        if got[0] <= now[0] + PAR["TEMP"] * (1.0 - k / moves) * rng.exponential():
+            now, order = got, sorted(new, key=lambda x: got[1][x] - cost[x])
+            if got[4] < best[0]:
+                best = (got[4], got[1])
+    return best[0], [best[1][i] - cost[i] for i in range(n)]
+
+
+def polish(ops, gap, back, order, rng):
+    n = len(ops)
+    eng = ["VSPGY".index(o["eng"]) for o in ops]
+    cost = [o["cost"] for o in ops]
+    banks = [[int(b[2:]) for b in o["banks"]] for o in ops]
+    other = ((1, 2), (0, 2), (0, 1))
+
+    def run(part, fin, why, last, used):
+        for i in part:
+            e = eng[i]
+            t, w = 0.0, -1
+            for j, x in gap[i]:
+                if fin[j] + x > t:
+                    t, w = fin[j] + x, j
+            j = last[e]
+            if fin[j] > t:
+                t, w = fin[j], j + n
+            for b in banks[i]:
+                for e2 in other[e]:
+                    j = used[3 * b + e2]
+                    if fin[j] + HOP > t:
+                        t, w = fin[j] + HOP, j + n
+                used[3 * b + e] = i
+            fin[i], why[i], last[e] = t + cost[i], w, i
+
+    def whole(order):
+        fin = [0.0] * n + [-1e9]
+        run(order, fin, [-1] * n, [n] * 5, [n] * 24)
+        return max(fin[i] + ops[i]["lat"] for i in range(n)), fin
+    best = whole(order)
+    sweeps, span = PAR["SWEEPS"], PAR["SPAN"]
+    for sweep in range(sweeps):
+        temp = PAR["TEMP"] * (1.0 - sweep / sweeps) ** 2
+        for lo in range(int(rng.integers(-span // 2, 1)), n - 20, span // 2):
+            a0, hi = max(lo, 0), min(n, lo + span)
+            fin0, last0, used0 = [0.0] * n + [-1e9], [n] * 5, [n] * 24
+            run(order[:a0], fin0, [-1] * n, last0, used0)
+            rest, nxt, nb = [0.0] * n + [-1e9], [n] * 5, [n] * 24
+            for i in order[:hi - 1:-1] if hi < n else ():
+                e = eng[i]
+                r = max([ops[i]["lat"], rest[nxt[e]]] + [x + rest[k] for k, x in back[i]])
+                for b in banks[i]:
+                    r = max(r, HOP + rest[nb[3 * b + other[e][0]]], HOP + rest[nb[3 * b + other[e][1]]])
+                    nb[3 * b + e] = i
+                rest[i], nxt[e] = r + cost[i], i
+            part = order[a0:hi]
+            inside = set(part)
+            outs = [(i, max([ops[i]["lat"]] + [x + rest[k] for k, x in back[i] if k not in inside])) for i in part]
+            top = max(x for _, x in outs)
+            outs = [y for y in outs if y[1] > top - 15000.0]
+            qe = [rest[nxt[e]] for e in range(5)]
+            qb = [HOP + max(rest[nb[3 * (k // 3) + e2]] for e2 in other[k % 3]) for k in range(24)]
+
+            def score(part):
+                fin, why, last, used = fin0[:], [-1] * n, last0[:], used0[:]
+                run(part, fin, why, last, used)
+                ts = [(fin[i] + x, i) for i, x in outs] + [(fin[last[e]] + qe[e], last[e]) for e in range(5)]
+                ts += [(fin[used[k]] + qb[k], used[k]) for k in range(24) if qb[k] > 0]
+                ts.sort(reverse=True)
+                ts = ts[:8]
+                return ts[0][0] + PAR["SOFT"] * sum(t for t, _ in ts) / len(ts), fin, why, ts
+            now = score(part)
+            for _ in range(PAR["MOVES"]):
+                i = now[3][int(rng.integers(len(now[3]))) if rng.random() < 0.5 else 0][1]
+                pairs = []
+                while i in inside:
+                    w = now[2][i]
+                    if w >= n:
+                        w -= n
+                        if w in inside:
+                            pairs.append((w, i))
+                    i = w
+                if not pairs:
+                    continue
+                j, i = pairs[int(rng.integers(len(pairs)))]
+                a, b = part.index(j), part.index(i)
+                mid = part[a:b + 1]
+                keep = rng.random() < PAR["KEEP"]
+                early = rng.random() < 0.5
+                go, held = {i if early else j}, set() if eng[i] == eng[j] else {eng[i if early else j]}
+                for y in mid[-2::-1] if early else mid[1:]:
+                    if (keep and eng[y] in held) or any(z in go for z, _ in (back if early else gap)[y]):
+                        go.add(y)
+                        held.add(eng[y])
+                if i in go and j in go:
+                    continue
+                new = part[:a] + [x for x in mid if (x in go) == early] + [x for x in mid if (x in go) != early] + part[b + 1:]
+                got = score(new)
+                if got[0] <= now[0] + temp * rng.exponential():
+                    now, part = got, sorted(new, key=lambda x: got[1][x] - cost[x])
+            order = order[:a0] + part + order[hi:]
+        got = whole(order)
+        order = sorted(order, key=lambda x: got[1][x] - cost[x])
+        if got[0] < best[0]:
+            best = got
+    return best[0], [best[1][i] - cost[i] for i in range(n)]
+
+
+def plan():
+    ops = build()
+    n = len(ops)
+    pred = links(ops)
     succ = [[] for _ in ops]
     for i in range(n):
         for j in pred[i]:
@@ -623,48 +1011,49 @@ def plan():
     prio = [0.0] * n
     for i in range(n - 1, -1, -1):
         prio[i] = ops[i]["cost"] + ops[i]["lat"] + max([prio[k] + HOP for k in succ[i]] + [0.0])
+        if ops[i]["eng"] == "G" and ops[i]["part"]:
+            prio[i] += PAR["PUSH"][ops[i]["part"][0]][ops[i]["part"][1] // 8]
     for i in range(n):
-        prio[i] += ops[i].get("bias", BIAS[STEPS][0])
-    left = [len(p) for p in pred]
-    ready = set(i for i in range(n) if left[i] == 0)
-    free = {e: 0.0 for e in "VSPGY"}
-    fin = [0.0] * n
-    bank = {}
-    order = []
-
-    def start(i):
-        o = ops[i]
-        t = free[o["eng"]]
-        for j in pred[i]:
-            if not (o["eng"] == "P" and ops[j]["eng"] == "P"):
-                t = max(t, fin[j] + HOP)
-        for b in o["banks"]:
-            for e, j in bank.get(b, {}).items():
-                if e != o["eng"]:
-                    t = max(t, fin[j] + HOP)
-        return t
-    while ready:
-        st = {i: start(i) for i in ready}
-        i0 = min(ready, key=lambda k: (st[k], k))
-        i = max((k for k in ready if st[k] <= st[i0] + GP[1] and ops[k]["eng"] == ops[i0]["eng"]), key=lambda k: (prio[k], -k))
-        if ORDER:
-            i = ORDER[len(order)]
-            assert i in ready
-        o = ops[i]
-        o["t"] = st[i]
-        free[o["eng"]] = st[i] + o["cost"]
-        fin[i] = st[i] + o["cost"] + o["lat"]
-        for b in o["banks"]:
-            for e, j in bank.get(b, {}).items():
-                if e != o["eng"]:
-                    pred[i].add(j)
-            bank.setdefault(b, {})[o["eng"]] = i
-        order.append(i)
-        ready.discard(i)
-        for k in succ[i]:
-            left[k] -= 1
-            if left[k] == 0:
-                ready.add(k)
+        p = ops[i]["part"]
+        prio[i] += PAR["BIAS"][p[0]][p[1]] if p else -4000.0
+    for i in range(3):
+        prio[i] = 1e9 - i
+    total, order, extra, fin = arrange(ops, pred, succ, prio)
+    gap = [[(j, 0.0 if ops[j]["eng"] == "P" and ops[i]["eng"] == "P" else ops[j]["lat"] + HOP) for j in pred[i]] for i in range(n)]
+    for i in (1, 2):
+        gap[i].append((i - 1, 0.0))
+    back = [[] for _ in ops]
+    for i in range(n):
+        for j, x in gap[i]:
+            back[j].append((i, x))
+    best = (total, [o["t"] for o in ops])
+    if PAR["FIFO"]:
+        turn = (0, 1, 1, 0, 0, 1, 0, 1, 1)
+        key = [PAR["FIFO"] * (2 * o["part"][0] + turn[o["part"][1]]) - prio[i] if o["part"] else -prio[i] for i, o in enumerate(ops)]
+        st = place(ops, gap, back, key, [0.0] * n)
+        best = (max(st[i] + ops[i]["cost"] + ops[i]["lat"] for i in range(n)), st)
+    rng = np.random.default_rng(PAR["SEED"])
+    for k in range(PAR["ROUNDS"]):
+        st = best[1]
+        noise = rng.normal(0.0, PAR["NOISE"] if k else 0.0, n)
+        late = place(ops, back, gap, [-(st[i] + ops[i]["cost"]) + noise[i] for i in range(n)], [o["lat"] for o in ops])
+        st = place(ops, gap, back, [-(late[i] + ops[i]["cost"]) for i in range(n)], [0.0] * n)
+        end = max(st[i] + ops[i]["cost"] + ops[i]["lat"] for i in range(n))
+        if end <= best[0]:
+            best = (end, st)
+    if PAR["MOVES"]:
+        best = polish(ops, gap, back, sorted(range(n), key=lambda i: (best[1][i], i)), rng)
+    if PAR["ROUNDS"]:
+        total = best[0]
+        order = sorted(range(n), key=lambda i: (best[1][i], i))
+        bank, extra = {}, [[] for _ in ops]
+        for i in order:
+            o = ops[i]
+            o["t"] = best[1][i]
+            fin[i] = o["t"] + o["cost"] + o["lat"]
+            for b in o["banks"]:
+                extra[i] += [j for e2, j in bank.get(b, {}).items() if e2 != o["eng"]]
+                bank.setdefault(b, {})[o["eng"]] = i
     pos = {}
     seen = {e: {} for e in "VSPGY"}
     know = [None] * n
@@ -677,7 +1066,7 @@ def plan():
         o = ops[i]
         e = o["eng"]
         waits = []
-        for j in sorted(pred[i], key=lambda x: -fin[x]):
+        for j in sorted(pred[i] | set(extra[i]), key=lambda x: -fin[x]):
             p = ops[j]
             if p["sem"] is not None:
                 key, val = ("d", j), 1
@@ -693,7 +1082,6 @@ def plan():
                 if seen[e].get(kk, 0) < vv:
                     seen[e][kk] = vv
         o["waits"] = waits
-        o["pred"] = pred[i]
         kn = dict(seen[e])
         if o["sem"] is not None:
             kn[("d", i)] = 1
@@ -706,7 +1094,19 @@ def plan():
         if o["sem"] is None and i in need:
             tot[o["eng"]] += 1
             o["inc"] = tot[o["eng"]]
-    return ops, order, tot, max(fin)
+    return ops, order, tot, total
+
+
+def resolver(T):
+    def R(a):
+        if not isinstance(a, tuple):
+            return a
+        if a[0] == "ind":
+            return R(a[1]).indirect(R(a[2]))
+        if a[3] == 1:
+            return T[a[0]][:, a[1]:a[2]]
+        return T[a[0]][:, a[1]:a[2]:a[3]]
+    return R
 
 
 PLAN = {}
@@ -722,15 +1122,7 @@ def rank_program(g, core, T, topo):
     Q = {"V": g.vector, "S": g.scalar, "P": g.tensor, "G": g, "Y": g.sync}
     X = {"T": T, "topo": topo, "core": core, "rank": rank, "sent": [0]}
     nfar = len(topo.engines(core, T.cores[(rank + 1) % N]))
-
-    def R(a):
-        if not isinstance(a, tuple):
-            return a
-        if a[0] == "ind":
-            return R(a[1]).indirect(R(a[2]))
-        if a[3] == 1:
-            return T[a[0]][:, a[1]:a[2]]
-        return T[a[0]][:, a[1]:a[2]:a[3]]
+    R = resolver(T)
     nout = 0
     for i in order:
         o = ops[i]

@@ -1,51 +1,51 @@
 import math
 import numpy as np
 from concourse.bass import DstId, RemoteDMATransfer
-from concourse.mybir import AluOpType as OP, AxisListType, ActivationFunctionType as AF
+from concourse.mybir import AluOpType as OP, ActivationFunctionType as AF
 
 N, STEPS = 4, 4
 CM = 1.5 * 2 ** 27
+C1 = 1.5 * 2 ** 23
 NEG = -131.0
-NB = 3
 SC, LAM = 1.75, 0.8125
+GK, GB, C0 = 128.0, 2.0 ** 18, 24576.0
 
 PAR = {
-    "VSHARE": [[64, 64], [16, 16], [32, 32], [32, 32]],
-    "DV": [[0, 0], [0, 0], [0, 0], [0, 0]],
-    "ABS2": [[2, 2], [0, 0], [0, 0], [0, 0]],
-    "EARLY": [[0, 0], [0, 0], [0, 1], [0, 1]],
-    "GP": 64, "WIN": 100.0, "ROUNDS": 0, "SEED": 1, "NOISE": 200.0, "PUSH": [[0, 0], [0, 0], [0, 0], [0, 0]], "MOVES": 0, "APART": 0, "KM": [[0, 0], [0, 0], [0, 0], [0, 0]], "KEEP": 0.7, "FIFO": 0, "SOFT": 1.0, "PS": 512, "STEP": 1500.0, "RUN": 8, "TEMP": 100.0, "NB": 3, "NB1": 1, "SG": [[0, 0], [0, 0], [0, 0], [0, 0]], "OFF": [[0, 0], [0, 0], [0, 0], [0, 0]],
-    "BIAS": [[0.0] * 9 for _s in range(STEPS)],
+    "VSHARE": [[64, 48], [32, 32], [32, 32], [32, 32]],
+    "UN": [[[[8, 0, 0], [8, 1, 0]], [[8, 2, 0], [8, 0, 0]]], [[[4, 0, 0]] * 4] * 2] + [[[[4, 1, 0], [4, 1, 0], [4, 0, 0], [4, 0, 0]], [[4, 1, 0], [4, 1, 0], [4, 0, 0], [4, 0, 1]]]] * 2,
+    "WAY": [[None, None], ["bit", "bit"], ["bit", "bit"], ["bit", "bit"]],
+    "SPEC": [[0, 0], [0, 0], [0, 0], [1, 1]],
+    "EARLY": [[0, 0], [0, 0], [0, 0], [0, 1]],
+    "HALF": [[0, 0], [1, 0], [1, 0], [1, 0]], "TB4": 1, "WG": 0, "FIRST": 0,
+    "GP": [[[32] * 4] * 2] * 4, "GE": [["SVSV", "SVSS"], ["SVSS", "SSSS"], ["SVSS", "SSSS"], ["SVSS", "SSSS"]],
+    "FREE": 0.5, "IDLE": 0.5, "SPAN": 6000.0, "BACK": 0.9, "SOFT": 0.1, "LEAN": 0.2, "CASES": [(1.3, 1.0, 1.0, 1.0, 0.0, 0.82), (0.95, 1.3, 1.0, 0.8, 2.0, 1.0)],
+    "POLISH": None, "NB": 4, "NB1": 2, "B2": [["ps2", "ps3"], ["ps2", "ps3"]], "ONS": ["i15", "in15", "in2k", "i8k", "in1", "ih", "iq", "i2k", "cb", "igb", "inb", "i384", "in384"], "KMW": "G" * 16,
+    "WIN": 50.0, "SEED": 1, "ROUNDS": 5500, "NOISE": 300.0, "TEMP": 250.0,
+    "PUSH": [[4000, 4000], [4000, 0], [4000, 0], [2000, 0]],
+    "BIAS": [[2000, 0, -1000, 0, 5000, -2000, 5000, 0, 3000], [0, 0, -3000, 0, 7000, 2000, 5000, 0, 5000],
+             [500, 0, -3000, 0, 5000, 0, 5000, -1000, 5000], [0, 0, -3000, 3000, 5000, 0, 4500, 0, 0]],
 }
-
-PAR.update({'VSHARE': [[64, 64], [48, 16], [16, 32], [32, 32]], 'ABS1': [[0, 0], [0, 0], [0, 0], [0, 0]], 'ABS2': [[2, 4], [0, 0], [0, 0], [3, 0]], 'EARLY': [[0, 0], [0, 0], [0, 1], [1, 1]], 'GP': 128, 'WIN': 100.0, 'ROUNDS': 300, 'SEED': 1, 'BIAS': [[1000.0, 2000.0, 8500.0, 9000.0, 2000.0, -1000.0, 0.0, 2500.0, 4500.0], [-7500.0, 9500.0, -1000.0, 0.0, 1500.0, 0.0, 8000.0, -3000.0, 3500.0], [11000.0, 8000.0, 3500.0, -1000.0, 2000.0, -1500.0, 0.0, -2500.0, 4500.0], [-6500.0, 9000.0, 500.0, -5500.0, 3000.0, 0.0, 0.0, 0.0, 1000.0]]})
-
-PAR.update({'VSHARE': [[64, 64], [48, 16], [32, 32], [32, 32]], 'DV': [[0, 0], [0, 2], [2, 2], [0, 2]], 'ABS2': [[1, 2], [4, 0], [1, 3], [0, 1]], 'EARLY': [[0, 0], [0, 0], [0, 1], [0, 0]], 'GP': 32, 'WIN': 100.0, 'ROUNDS': 2000, 'SEED': 1, 'BIAS': [[6500, -2000, 1500, 3500, -2500, -3000, 20500, -7500, -3500], [7500, 3500, -500, 9000, -2500, -1500, 7000, 8500, 7500], [3000, 500, -7500, -8500, 2000, 500, 14000, 14500, 500], [-4000, -7000, -9500, 0, 6000, 1000, 4000, 4500, 4000]]})
-PAR.update({'VSHARE': [[64, 32], [64, 16], [64, 16], [64, 16]], 'EARLY': [[0, 0], [0, 0], [0, 0], [0, 1]], 'GP': 32, 'WIN': 100.0, 'ROUNDS': 1, 'SEED': 1, 'NOISE': 200.0, 'PUSH': [[4000, 4000], [4000, 0], [4000, 0], [2000, 0]], 'NB': 4, 'NB1': 2, 'OFF': [[1, 1], [1, 1], [1, 1], [1, 1]], 'BIAS': [[2000, 0, -1000, 0, 5000, -2000, 5000, 0, 3000], [0, 0, -3000, 0, 7000, 2000, 5000, 0, 5000], [500, 0, -3000, 0, 5000, 0, 5000, -1000, 5000], [0, 0, -3000, 3000, 5000, 0, 4500, 0, 0]],
-            "MOVES": 80000, "TEMP": 500.0, "SOFT": 1.0, "KEEP": 0.8, "PS": 2000})
-PAR["UN"] = [[[[4, h[b], d[b]] for b in range(4)] for h, d in x] for x in (
-    (([1, 1, 0, 0], [0] * 4), ([1, 1, 0, 0], [0] * 4)), (([2, 2, 0, 0], [0] * 4), ([2, 0, 0, 0], [0] * 4)),
-    (([1, 1, 1, 0], [0, 0, 0, 1]), ([1, 1, 1, 0], [0, 0, 0, 1])), (([1, 1, 1, 0], [0, 0, 0, 1]), ([1, 1, 1, 0], [0, 0, 0, 1])))]
-PAR.update({"SWEEPS": 30, "TEMP": 800.0, "SPAN": 100, "SOFT": 2.0, "MOVES": 250, "OFF": [[0, 0], [1, 1], [1, 1], [1, 1]],
-            "VSHARE": [[64, 48], [48, 0], [48, 16], [48, 16]]})
-PAR["UN"] = [[[[8, 0, 0], [8, 1, 0]], [[8, 2, 0], [8, 0, 0]]], [[[4, 0, 0]] * 4] * 2] + [[[[4, 1, 0]] * 3 + [[4, 0, 1]]] * 2] * 2
-SCALED = {"i1": 1.0, "in1": -1.0, "i15": 1.5, "in15": -1.5, "ih": 0.5, "iq": 0.25, "inq": -0.25,
-          "in512": -512.0, "i512": 512.0, "i1k": 1024.0, "i1536": 1536.0, "in32": -32.0, "i384": 384.0, "in384": -384.0,
-          "in2k": -2048.0, "ia": -1.8125, "ib": 1.0 / 2048, "i10": 10.0, "ilam": LAM, "inls": -LAM * SC}
-MATS = list(SCALED) + ["iw", "bd", "bdbig", "bdp", "bd1k", "bd10", "bdn1k", "w1", "warg", "w2", "wpw", "tri"]
+SCALED = {"i1": 1.0, "in1": -1.0, "i15": 1.5, "in15": -1.5, "ih": 0.5, "iq": 0.25, "inq": -0.25, "in512": -512.0, "i512": 512.0,
+          "i1k": 1024.0, "i1536": 1536.0, "i384": 384.0, "in384": -384.0, "in2k": -2048.0, "i2k": 2048.0, "ia": -1.625, "i768": 768.0, "in768": -768.0,
+          "ib": 1.0 / 2048, "i10": 10.0, "ilam": LAM, "inls": -LAM * SC,
+          "ck": -17 * GK, "ic0": C0, "cb": -17 * GB, "igb": GB, "inb": -192 * GB, "i8k": 8192.0}
+BLOCK = {"bdn": -1.0, "bdbig": 2.0 ** 99, "bd10": 8192.0, "bd1k": 1024.0, "bdn1k": -1024.0, "bd40": 2.0 ** 40}
+MATS = list(SCALED) + list(BLOCK) + ["iw", "bd", "bdp", "w1", "wok", "wargb", "wrot", "wpw", "tri", "one", "wgk", "wgb",
+                                     "w16k", "wn16k"]
 MOFF = {m: 128 * i for i, m in enumerate(MATS)}
 
 SCRATCH = {
     "tab": ("sbuf", [128, 8192], "bfloat16"), "ivi": ("sbuf", [128, 1024], "int32"), "wl": ("sbuf", [128, 1024], "float32"),
     "e0i": ("sbuf", [128, 16], "int32"), "mats": ("sbuf", [128, 128 * len(MATS)], "bfloat16"),
-    "zz": ("sbuf", [128, 5 * 144], "bfloat16"), "sgc": ("sbuf", [128, 56], "float32"), "zh": ("sbuf", [128, 144 + 128], "float16"),
+    "zz": ("sbuf", [128, 3 * 144], "bfloat16"), "zh": ("sbuf", [128, 144], "float16"),
     "iot": ("sbuf", [128, 1032], "float32"), "tk": ("sbuf", [128, 1024], "bfloat16"), "tmpb": ("sbuf", [128, 80], "bfloat16"),
-    "cols": ("sbuf", [128, 16], "float32"), "coli": ("sbuf", [128, 8], "int32"), "cf": ("sbuf", [128, 512], "float32"),
-    "cb": ("sbuf", [128, 512], "bfloat16"), "basel": ("sbuf", [128, 8], "bfloat16"), "lanel": ("sbuf", [128, 16], "float32"),
-    "con": ("sbuf", [128, 2 * 24], "float32"), "thl": ("sbuf", [128, 64], "float32"), "kmw": ("sbuf", [128, 2048], "bfloat16"),
+    "cols": ("sbuf", [128, 16], "float32"), "coli": ("sbuf", [128, 8], "int32"), "cf": ("sbuf", [128, 896], "float32"),
+    "cb": ("sbuf", [128, 896], "bfloat16"), "ones": ("sbuf", [128, 256], "bfloat16"), "basel": ("sbuf", [128, 16], "bfloat16"), "lanel": ("sbuf", [128, 16], "float32"),
+    "con": ("sbuf", [128, 80], "float32"), "thl": ("sbuf", [128, 96], "float32"), "kmw": ("sbuf", [128, 2048], "bfloat16"),
+    "wkm": ("sbuf", [128, 2048], "bfloat16"), "wbit": ("sbuf", [128, 2048], "bfloat16"),
     "oyk": ("sbuf", [128, 256], "bfloat16"), "oy0": ("sbuf", [128, 256], "bfloat16"), "oy1": ("sbuf", [128, 256], "bfloat16"),
     "oye": ("sbuf", [128, 16], "float32"), "oya": ("sbuf", [128, 16], "float32"),
-    "wf": ("sbuf", [128, 256 * 3], "float32"), "wi": ("sbuf", [128, 256 * 2], "int32"),
+    "wf": ("sbuf", [128, 256 * 4], "float32"), "wi": ("sbuf", [128, 256 * 2], "int32"),
 }
 for _b in range(8):
     SCRATCH["ps%d" % _b] = ("psum", [128, 512], "float32")
@@ -55,31 +55,34 @@ for _k in range(3):
     SCRATCH["aa%d" % _k] = ("sbuf", [128, 512], "bfloat16")
 for _c in range(2):
     SCRATCH["dd%d" % _c] = ("sbuf", [128, 512], "float32")
-    SCRATCH["yy%d" % _c] = ("sbuf", [128, 2064], "bfloat16")
     SCRATCH["me%d" % _c] = ("sbuf", [128, 2048], "bfloat16")
-    SCRATCH["tb%d" % _c] = ("sbuf", [128, 512], "bfloat16")
     SCRATCH["c16_%d" % _c] = ("sbuf", [128, 128], "uint16")
-    SCRATCH["l16_%d" % _c] = ("sbuf", [128, 40], "uint16")
     SCRATCH["u16_%d" % _c] = ("sbuf", [128, 64], "uint16")
     SCRATCH["si%d" % _c] = ("sbuf", [128, 128], "int32")
-    SCRATCH["li%d" % _c] = ("sbuf", [128, 16], "int32")
-    SCRATCH["lf%d" % _c] = ("sbuf", [128, 64], "float32")
-    SCRATCH["lq%d" % _c] = ("sbuf", [128, 40], "bfloat16")
-    SCRATCH["rf%d" % _c] = ("sbuf", [128, 128 * 2], "float32")
-    SCRATCH["ri%d" % _c] = ("sbuf", [128, 128 * 2], "int32")
-    SCRATCH["rb%d" % _c] = ("sbuf", [128, 128 * 12], "bfloat16")
-    SCRATCH["stk%d" % _c] = ("sbuf", [128, 128 * 4], "bfloat16")
-    SCRATCH["sh%d" % _c] = ("sbuf", [128, 128 * 4], "float16")
-    for _s in range(STEPS):
+    SCRATCH["al%d" % _c] = ("sbuf", [128, 16], "bfloat16")
+    SCRATCH["eh%d" % _c] = ("sbuf", [128, 4, 8], "float16")
+    for _s in range(STEPS - 1):
         SCRATCH["win%d%d" % (_s, _c)] = ("sbuf", [128, 784], "bfloat16")
         SCRATCH["sb%d%d" % (_s, _c)] = ("sbuf", [128, 384], "bfloat16")
-        SCRATCH["sl%d%d" % (_s, _c)] = ("sbuf", [128, 16], "int32")
+        SCRATCH["sl%d%d" % (_s, _c)] = ("sbuf", [128, 4, 4], "uint16")
+for _c, _l in enumerate((128, 128, 256)):
+    SCRATCH["yy%d" % _c] = ("sbuf", [128, 16 * _l + 16], "bfloat16")
+    SCRATCH["l16_%d" % _c] = ("sbuf", [128, 5 * _l // 16], "uint16")
+    SCRATCH["th%d" % _c] = ("sbuf", [128, _l // 8], "float16")
+    SCRATCH["lf%d" % _c] = ("sbuf", [128, _l // 2], "float32")
+    SCRATCH["lq%d" % _c] = ("sbuf", [128, _l // 4], "bfloat16")
+    SCRATCH["rf%d" % _c] = ("sbuf", [128, _l * 3], "float32")
+    SCRATCH["rb%d" % _c] = ("sbuf", [128, _l * 13], "bfloat16")
+    SCRATCH["stk%d" % _c] = ("sbuf", [128, _l * 4], "bfloat16")
+    SCRATCH["sh%d" % _c] = ("sbuf", [128, _l * 3], "float16")
+SCRATCH["win32"] = ("sbuf", [128, 16 + 6 * 256], "bfloat16")
+WINS = ["win%d%d" % (_s, _c) for _s in range(STEPS - 1) for _c in range(2)] + ["win32"]
 for _s in range(STEPS):
-    SCRATCH["el%d" % _s] = ("sbuf", [128, 32], "int32")
+    SCRATCH["el%d" % _s] = ("sbuf", [128, 8, 4], "uint16")
 
 SEMAPHORES = (["qV", "qS", "qP", "qG", "sent", "ld0", "ld1", "ld2", "outs"]
               + ["ar%s%d%d" % (k, s, c) for k in "lr" for s in range(1, STEPS) for c in range(2)]
-              + ["lo%s%d" % (k, s) for k in "lr" for s in range(1, STEPS)])
+              + ["%s%d" % (w, k) for w in ("wkm", "wbit") for k in range(6)])
 
 CY = 0.83 * 1.15
 PECY = 0.42 * 1.15
@@ -91,6 +94,16 @@ def A(name, lo, n, step=1):
     return (name, lo, lo + (n - 1) * step + 1, step)
 
 
+def B(name, lo, n, step=1):
+    w = SCRATCH[name][1][2]
+    hi = lo + (n - 1) * step + 1
+    return (name, lo * w, hi * w, 1, (lo, hi, step), n * w)
+
+
+def sub(a, lo, n):
+    return A(a[0], a[1] + lo * a[3], n, a[3])
+
+
 def IND(win, off):
     return ("ind", win, off)
 
@@ -98,7 +111,7 @@ def IND(win, off):
 def cnt(a):
     if a[0] == "ind":
         return 16 * cnt(a[2])
-    return (a[2] - a[1] - 1) // a[3] + 1
+    return a[5] if len(a) > 4 else (a[2] - a[1] - 1) // a[3] + 1
 
 
 def two(a):
@@ -112,26 +125,15 @@ def isps(a):
 def flat(xs):
     out = []
     for a in xs:
-        if not isinstance(a, tuple):
-            continue
-        if a[0] == "ind":
-            out += [a[1], a[2]]
-        else:
-            out.append(a)
+        if isinstance(a, tuple):
+            out += [a[1], a[2]] if a[0] == "ind" else [a]
     return out
-
-
-def signs(s, c):
-    k = 0
-    for nk, how, _ in PAR["UN"][s][c]:
-        if how < 2 or (s and PAR["KM"][s][c]):
-            break
-        k += nk
-    return k
 
 
 def build():
     ops = []
+    ways = set(w for x in PAR["WAY"] for w in x)
+    used = set()
 
     def add(eng, call, outs, ins, cost, sem=None, lat=0.0):
         w = []
@@ -142,7 +144,8 @@ def build():
                 r.append(a[2])
             else:
                 w.append(a)
-        ops.append({"eng": eng, "call": call, "w": w, "r": r, "cost": cost, "sem": sem, "lat": lat, "part": None})
+        ops.append({"eng": eng, "call": call, "w": w, "r": r, "cost": cost, "sem": sem, "lat": lat, "part": None,
+                    "ind": cost - FIX if any(isinstance(a, tuple) and a[0] == "ind" for a in ins) else 0.0})
 
     def ecost(out, ins, base):
         n = cnt(ins[0]) if ins else cnt(out)
@@ -152,15 +155,30 @@ def build():
             return FIX + n * GA * CY
         return FIX + max(n * base, 16) * CY
 
-    def cp(out, a):
-        add("V", lambda q, R, X: q.tensor_copy(R(out), R(a)), [out], [a], ecost(out, [a], 0.5 if two(out) and two(a) else 1))
+    def real(*xs):
+        return all(SCRATCH[(x[1] if x[0] == "ind" else x)[0]][2] in ("float32", "bfloat16") for x in xs)
 
-    def ts(out, a, s1, o1, s2=None, o2=None):
+    def either(first=False):
+        o = ops.pop()
+        if o["eng"] == "S" and not first:
+            ops[-1], o = o, ops[-1]
+        ops[-1]["alt"] = (o["eng"], o["call"], o["cost"])
+
+    def cp(out, a, alone=False):
+        add("V", lambda q, R, X: q.tensor_copy(R(out), R(a)), [out], [a], ecost(out, [a], 0.5 if two(out) and two(a) else 1))
+        if not alone and real(out, a) and out[0] != "ind":
+            act(out, a, AF.Copy, alone=True)
+            either()
+
+    def ts(out, a, s1, o1, s2=None, o2=None, alone=False):
         def call(q, R, X):
             if o2 is None:
                 return q.tensor_scalar(R(out), R(a), R(s1), None, o1)
             return q.tensor_scalar(R(out), R(a), R(s1), R(s2), o1, o2)
         add("V", call, [out], [a, s1, s2], ecost(out, [a], 0.5 if two(out) and two(a) else 1))
+        if not alone and real(out, a) and (o1, o2) in ((OP.mult, None), (OP.add, None), (OP.mult, OP.add)):
+            act(out, a, AF.Identity, bias=s1 if o1 == OP.add else s2, scale=s1 if o1 == OP.mult else 1.0, alone=True)
+            either(cnt(out) > 128)
 
     def tt(out, a, b, o):
         add("V", lambda q, R, X: q.tensor_tensor(R(out), R(a), R(b), o), [out], [a, b],
@@ -169,32 +187,28 @@ def build():
     def ms(out, v):
         add("V", lambda q, R, X: q.memset(R(out), v), [out], [], ecost(out, [], 0.5 if two(out) else 1))
 
-    def act(out, a, f, bias=None, scale=1.0, extra=0.0):
+    def act(out, a, f, bias=None, scale=1.0, extra=0.0, alone=False):
         def call(q, R, X):
             if bias is None:
                 return q.activation(R(out), R(a), f, scale=R(scale))
             return q.activation(R(out), R(a), f, bias=R(bias), scale=R(scale))
         add("S", call, [out], [a, bias, scale], ecost(out, [a], 1) + extra)
+        if not alone and (f in (AF.Copy, AF.Identity) or (f == AF.Relu and bias is None)):
+            if f == AF.Relu:
+                ts(out, a, scale, OP.mult, 0.0, OP.max)
+            elif bias is None:
+                ts(out, a, scale, OP.mult, alone=True)
+            else:
+                ts(out, a, scale, OP.mult, bias, OP.add, alone=True)
+            either()
 
-    def mms(items, whole=None):
-        part, n = [], 0
-        for x in items + [None]:
-            if part and (x is None or n + cnt(x[2]) > PAR["PS"]):
-                mm(part)
-                if whole:
-                    ops[-1]["w"].append(whole)
-                part, n = [], 0
-            if x:
-                part.append(x)
-                n += cnt(x[2])
-
-    def mm(items):
+    def mm(items, whole=None):
         def call(q, R, X):
             last = None
             for o, l, r, st, sp in items:
                 last = q.matmul(R(o), R(l), R(r), bool(st), bool(sp))
             return last
-        add("P", call, [x[0] for x in items], [x[1] for x in items] + [x[2] for x in items],
+        add("P", call, [x[0] for x in items] + ([whole] if whole else []), [x[1] for x in items] + [x[2] for x in items],
             20 + sum(max(64, cnt(x[2])) * PECY + 4 for x in items))
 
     def grp(out, terms, start=True, stop=True):
@@ -208,6 +222,7 @@ def build():
         add("G", call, [out], [], 130 + 2 * cnt(out) * CY)
 
     def M(name):
+        used.add(name)
         return A("mats", MOFF[name], 128)
 
     def Z(t, k):
@@ -216,209 +231,225 @@ def build():
     def col(i):
         return A("cols", i, 1)
 
-    def dma(out, a, sem, lat):
-        add("Y", lambda q, R, X: q.dma_start(R(out), R(a)), [out], [a], 60, sem=(sem, 16), lat=lat)
+    def dma(out, a, sem, lat, after=()):
+        add("Y", lambda q, R, X: q.dma_start(R(out), R(a)), [out], [a] + list(after), 60, sem=(sem, 16), lat=lat)
 
-    add("Y", lambda q, R, X: q.dma_start(R(A("e0i", 0, 16)), X["T"].e0[:]), [A("e0i", 0, 16)], [], 60, sem=("ld0", 16), lat=2200)
-    add("Y", lambda q, R, X: q.dma_start(R(A("ivi", 0, 1024)), X["T"].iv[:]), [A("ivi", 0, 1024)], [A("cols", 15, 1)][:0], 60,
-        sem=("ld1", 16), lat=3500)
-    add("Y", lambda q, R, X: q.dma_start(R(A("tab", 0, 8192)), X["T"].st[:]), [A("tab", 0, 8192)], [], 60, sem=("ld2", 16), lat=8000)
-
-    P, G16, PW, NPW, IPW, K16, WP, KT, G, NW4 = range(10)
-    iota(A("coli", 0, 1), [[1, 1]], 0, 1)
-    iota(A("iot", 0, 1032), [[1, 1032]], 0, 0)
-    iota(A("cf", 0, 128), [[1, 8], [0, 16]], 0, 0)
-    iota(A("cf", 128, 128), [[0, 8], [1, 16]], 0, 0)
-    iota(A("cf", 256, 128), [[1, 128]], 0, -1)
-    iota(A("cf", 384, 32), [[0, 2], [1, 16]], 0, 0)
-    ts(A("coli", 1, 1), A("coli", 0, 1), 15, OP.bitwise_and)
-    ts(A("coli", 2, 1), A("coli", 0, 1), 4, OP.arith_shift_right)
-    cp(col(P), A("coli", 1, 1))
-    cp(col(G), A("coli", 2, 1))
-    ts(col(G16), col(G), 16.0, OP.mult, 15.0, OP.add)
-    ts(col(K16), col(P), 16.0, OP.add)
-    ts(col(WP), col(P), 64.0, OP.mult, 2048.0, OP.add)
-    ts(col(NW4), col(WP), -4.0, OP.mult)
-    act(A("tmpb", 64, 1), col(P), AF.Exp, scale=math.log(2.0), extra=1300.0)
-    act(A("tmpb", 66, 1), col(P), AF.Exp, bias=15 * math.log(2.0), scale=-math.log(2.0))
-    cp(col(PW), A("tmpb", 64, 1))
-    cp(col(IPW), A("tmpb", 66, 1))
-    ts(A("cf", 432, 16), A("cf", 384, 16), col(P), OP.is_equal)
-    ts(col(NPW), col(PW), -1.0, OP.mult)
-    ts(M("i1"), A("cf", 256, 128), 0.0, OP.is_equal)
-    ts(M("bd"), A("cf", 0, 128), col(G), OP.is_equal)
-    for m, v in SCALED.items():
-        if m != "i1":
-            act(M(m), M("i1"), AF.Copy, scale=float(v))
-    ts(M("iw"), M("i1"), col(WP), OP.mult)
-    for m, v in (("bdbig", 2.0 ** 96), ("bd10", 10.0), ("bd1k", 1024.0), ("bdn1k", -1024.0), ("w2", col(NPW)), ("wpw", col(IPW))):
-        ts(M(m), M("bd"), v, OP.mult)
-    ts(A("cb", 256, 128), A("cf", 128, 128), -1.0, OP.mult, -0.25, OP.add)
-    tt(M("bdp"), A("cb", 256, 128), M("bd"), OP.mult)
-    ts(A("cb", 0, 128), A("cf", 128, 128), col(P), OP.is_gt, -1.0, OP.mult)
-    tt(A("cb", 128, 128), A("cb", 0, 128), M("bd"), OP.mult)
-    tt(M("w1"), A("cb", 128, 128), M("i1"), OP.add)
-    ts(A("cb", 256, 128), A("cb", 0, 128), -63.0 / 32, OP.mult, 1.0 / 32, OP.add)
-    tt(A("cb", 384, 128), A("cb", 256, 128), M("bd"), OP.mult)
-    ts(A("cb", 0, 128), M("i1"), -33.0 / 32, OP.mult)
-    tt(M("warg"), A("cb", 384, 128), A("cb", 0, 128), OP.add)
-    ts(A("zz", 144, 144), A("iot", 0, 144), col(G16), OP.is_equal)
-    ts(A("zz", 0, 144), A("zz", 144, 144), col(PW), OP.mult)
-    ts(A("zz", 288, 144), A("zz", 144, 144), col(K16), OP.mult)
-    cp(A("zh", 0, 144), A("zz", 144, 144))
-    act(A("zz", 432, 288), A("zz", 0, 288), AF.Copy, scale=0.5)
-    for sg in sorted(set(signs(s, c) for s in range(1, STEPS) for c in range(2)) - {0}):
-        ts(A("sgc", 3 * sg, 1), col(P), sg - 0.5, OP.is_lt, -32767.5, OP.mult)
-        ts(A("sgc", 3 * sg + 2, 1), col(P), sg - 0.5, OP.is_lt, 32767.5, OP.mult)
-    for sg in sorted(set(signs(0, c) for c in range(2)) - {0}):
-        ts(A("cf", 448, 1), col(P), sg - 0.5, OP.is_lt, -8.0, OP.mult)
-        ts(A("sgc", 3 * sg + 1, 1), A("cf", 448, 1), 1.0, OP.add)
-    iota(A("tmpb", 0, 64), [[4, 64]], 6, 0)
-    for r in range(16):
-        if r % 2:
-            ts(A("tk", 64 * r, 64), A("tmpb", 0, 64), A("cf", 432 + r, 1), OP.mult)
-        else:
-            act(A("tk", 64 * r, 64), A("tmpb", 0, 64), AF.Copy, scale=A("cf", 432 + r, 1))
-    ts(A("lanel", 0, 16), A("cf", 384, 16), 16.0, OP.mult, col(P), OP.add)
-    U = A("lanel", 0, 8)
-    ts(A("basel", 0, 8), U, 16.0, OP.mult, -16.0, OP.add)
-    ms(A("thl", 8, 16), 0.5)
-    ms(A("thl", 24, 8), 200000.0)
-    ts(A("thl", 0, 8), U, 16.0, OP.mult, -0.5, OP.add)
-    for c in range(2):
-        ms(A("yy%d" % c, 2048, 16), 0.0)
-    if any(PAR["KM"][s][c] for s in range(1, STEPS) for c in range(2)):
-        ms(A("thl", 40, 16), 0.5)
-        ms(A("thl", 56, 8), 8000.0)
-        ts(A("thl", 32, 8), U, -16.0, OP.mult, 16.5, OP.add)
-        for k in range(16):
-            if k % 2:
-                ts(A("kmw", 128 * k, 128), M("i1"), 4.0 ** (15 - k), OP.mult)
-            else:
-                act(A("kmw", 128 * k, 128), M("i1"), AF.Copy, scale=4.0 ** (15 - k))
-        ts(col(KT), col(IPW), col(IPW), OP.mult, 0.9, OP.mult)
-        ts(A("cb", 384, 128), A("cf", 128, 128), col(P), OP.is_ge, 2.0 ** 41, OP.mult)
-        ts(A("cb", 384, 128), A("cb", 384, 128), -2.0 ** 40, OP.add)
-        tt(M("tri"), A("cb", 384, 128), M("bd"), OP.mult)
+    WL, TAB = A("wl", 0, 1024), A("tab", 0, 8192)
+    P, G16, IPW, K16, WP, KT, G, NW4, P1 = range(9)
     DD, NF, NN, FL = range(4)
-    for i, (c0, w) in enumerate(((16, 1), (16, 1), (402, 1), (16, 1), (16 - 2048, 2048), (402, 1))):
-        act(A("con", 8 * i, 8), U, AF.Identity, bias=c0 / w, scale=3.0 / w)
+
+    def setup():
+        for name, buf, sem, lat in (("e0", A("e0i", 0, 16), "ld0", 2200), ("iv", A("ivi", 0, 1024), "ld1", 3500), ("st", TAB, "ld2", 8000)):
+            add("Y", lambda q, R, X, name=name, buf=buf: q.dma_start(R(buf), X["T"][name][:]), [buf], [], 60, sem=(sem, 16), lat=lat)
+        I1, BD, CK = A("mats", MOFF["i1"], 128), A("mats", MOFF["bd"], 128), A("cf", 128, 128)
+        iota(A("coli", 0, 1), [[1, 1]], 0, 1)
+        iota(A("iot", 0, 144), [[1, 144]], 0, 0)
+        iota(A("iot", 144, 888), [[1, 888]], 144, 0)
+        iota(A("cf", 0, 128), [[1, 8], [0, 16]], 0, 0)
+        iota(CK, [[0, 8], [1, 16]], 0, 0)
+        iota(A("ones", 0, 256), [[0, 256]], 1, 0)
+        ZERO = A("cb", 768, 128)
+        ms(ZERO, 0.0)
+
+        def pick(out, a, op, fill):
+            add("G", lambda q, R, X: q.affine_select(R(out), R(a), [[1, 128]], op, fill, 0, -1), [out], [a], 170 + 256 * CY)
+
+        def scaled(out, v, eng):
+            if eng == "G":
+                pick(out, ZERO, OP.not_equal, v)
+            elif eng == "S":
+                act(out, I1, AF.Copy, scale=v)
+            else:
+                ts(out, I1, v, OP.mult)
+
+        def upper(out, v, diag):
+            ts(out, BD, v, OP.mult)
+            pick(out, out, OP.is_gt, 0.0)
+            if diag:
+                pick(out, out, OP.not_equal, diag)
+        scaled(I1, 1.0, "G")
+        ts(A("coli", 1, 1), A("coli", 0, 1), 15, OP.bitwise_and)
+        ts(A("coli", 2, 1), A("coli", 0, 1), 4, OP.arith_shift_right)
+        cp(A("cols", P, 2, G - P), A("coli", 1, 2))
+        ts(col(G16), col(G), 16.0, OP.mult, 15.0, OP.add)
+        ts(col(K16), col(P), 16.0, OP.add)
+        ts(col(WP), col(P), 64.0, OP.mult, 2048.0, OP.add)
+        ts(col(NW4), col(WP), -4.0, OP.mult)
+        ts(A("cf", 432, 16), A("cf", 128, 16), col(P), OP.is_equal)
+        ts(BD, A("cf", 0, 128), col(G), OP.is_equal)
+        for m, v in SCALED.items():
+            if m != "i1" and m in used:
+                scaled(M(m), float(v), "S" if m in PAR["ONS"] else "G")
+        ts(M("iw"), I1, col(WP), OP.mult)
+        for m, v in BLOCK.items():
+            if m in used:
+                ts(M(m), BD, v, OP.mult)
+        ts(A("cb", 256, 128), CK, -1.0, OP.mult, -0.25, OP.add)
+        tt(M("bdp"), A("cb", 256, 128), BD, OP.mult)
+        for m, v in (("w1", 1.0), ("w16k", 16384.0), ("wn16k", -16384.0)):
+            if m in used:
+                upper(M(m), -v, v)
+        for i, (m, we, wl, own) in enumerate((("wok", -2048.0, -32.0, 1024.0), ("wargb", 8.0, 1.0 / 128, -1.0))):
+            if m in used:
+                x, y = A("cb", 384 + 128 * i, 128), A("cb", 128, 128)
+                upper(x, we, 0)
+                ts(y, BD, wl, OP.mult)
+                tt(M(m), x, y, OP.max if we > 0 else OP.min)
+                pick(M(m), M(m), OP.not_equal, own)
+        ts(A("zz", 144, 144), A("iot", 0, 144), col(G16), OP.is_equal)
+        ts(A("zz", 288, 144), A("zz", 144, 144), col(K16), OP.mult)
+        act(A("zz", 0, 144), A("zz", 144, 144), AF.Copy, scale=0.5)
+        cp(A("zh", 0, 144), A("zz", 144, 144))
+        ts(col(P1), col(P), 7.5, OP.is_lt, 8.0, OP.mult)
+        iota(A("tmpb", 0, 64), [[4, 64]], 6, 0)
+        for r in range(16):
+            if r % 2:
+                ts(A("tk", 64 * r, 64), A("tmpb", 0, 64), A("cf", 432 + r, 1), OP.mult)
+            else:
+                act(A("tk", 64 * r, 64), A("tmpb", 0, 64), AF.Copy, scale=A("cf", 432 + r, 1))
+        ts(A("lanel", 0, 16), A("cf", 128, 16), 16.0, OP.mult, col(P), OP.add)
+        U = A("lanel", 0, 8)
+        ts(A("basel", 0, 16), A("lanel", 0, 16), 16.0, OP.mult, -16.0, OP.add)
+        for o, m in ((0, 8), (32, 16)):
+            ts(A("thl", o, m), A("lanel", 0, m), 16.0, OP.mult, -0.5, OP.add)
+            iota(A("thl", o + m, 2 * m), [[0, 2 * m]], 1, 0)
+            iota(A("thl", o + 3 * m, m), [[0, m]], 200000, 0)
+        for c, o in enumerate((2048, 2048, 4096)):
+            iota(A("yy%d" % c, o, 16), [[0, 16]], 0, 0)
+        first = [1300.0]
+
+        def power(out, a, scale, bias):
+            act(out, a, AF.Exp, bias=bias * math.log(2.0), scale=scale * math.log(2.0), extra=first[0])
+            first[0] = 0.0
+        if "km" in ways:
+            ms(A("thl", 40, 16), 0.5)
+            ms(A("thl", 56, 8), 8000.0)
+            ts(A("thl", 32, 8), U, -16.0, OP.mult, 16.5, OP.add)
+            for k in range(16):
+                scaled(A("kmw", 128 * k, 128), 4.0 ** (15 - k), PAR["KMW"][k])
+            power(A("tmpb", 66, 1), col(P), -2.0, 30.0)
+            ts(col(KT), A("tmpb", 66, 1), 0.9, OP.mult)
+            x = A("cb", 256, 128)
+            ts(x, CK, col(P), OP.is_ge, 2.0 ** 45 + 2.0 ** 40, OP.mult)
+            ts(x, x, -2.0 ** 40, OP.add)
+            tt(M("tri"), x, BD, OP.mult)
+        if "bit" in ways:
+            x, y, z = A("cf", 512, 128), A("cf", 640, 128), A("cf", 768, 128)
+            ts(x, CK, -1.0, OP.mult, col(P), OP.add)
+            ts(y, x, 0.5, OP.is_lt, 16.0, OP.mult)
+            tt(z, x, y, OP.add)
+            x, y = A("cb", 0, 128), A("cb", 256, 128)
+            power(x, z, 1.0, -1.0)
+            tt(M("wrot"), x, BD, OP.mult)
+            power(y, z, -1.0, 0.0)
+            tt(M("wpw"), y, BD, OP.mult)
+        for way, m, g, src in (("km", "wgk", GK, BD), ("bit", "wgb", GB, A("mats", MOFF["wrot"], 128))):
+            if way in ways:
+                w = "w" + way
+                ts(A(w, 0, 128), I1, g, OP.mult)
+                tt(M(m), A(w, 0, 128), src, OP.add)
+                for k in range(6):
+                    n = 128 if k < 3 else 512
+                    dma(A(w, n * (k % 3 + 1), n), A(w, 0, n), "%s%d" % (w, k), 2200 + n, [A("tab", 0, 1)])
+                for k in range(16):
+                    o, a = A(w, 128 * k + k, 8, 16), A("mats", MOFF[m] + k, 8, 16)
+                    if k >= PAR["WG"]:
+                        cp(o, a)
+                        continue
+                    add("G", lambda q, R, X, o=o, a=a: q.affine_select(R(o), R(a), [[0, 8]], OP.is_gt, 0.0, 1, 0), [o], [a], 170 + 16 * CY)
+        for o, m, c0, w in ((0, 8, 17, 1), (8, 8, 16, 1), (16, 8, 16, 1), (24, 8, 402, 1),
+                            (32, 16, 16, 1), (48, 16, 16 - 2048, 2048), (64, 16, 786, 1)):
+            act(A("con", o, m), A("lanel", 0, m), AF.Identity, bias=c0 / w, scale=3.0 / w)
+        cp(WL, A("ivi", 0, 1024))
+        for w in WINS:
+            iota(A(w, 0, 16), [[0, 16]], -126 if w == WINS[-1] else int(NEG), 0)
+        for x in (A("win10", 401, 64, 3), A("sb00", 193, 64, 3), A("sb01", 1, 128, 3)):
+            iota(x, [[0, cnt(x)]], int(NEG), 0)
+        ms(B("el0", 1, 4, 2), 0)
+        cp(B("el0", 0, 4, 2), A("e0i", 0, 16))
+
     ST2 = {
-        0: [[("in2k", DD)], [("in2k", DD)], [("in384", DD)], [("i1", DD)]],
-        1: [[("in2k", DD), ("i1", NF), ("i384", NN)], [("in2k", DD), ("i384", NF)], [("in384", DD)], [("i1", DD)]],
+        0: [[("i1", DD)], [("in2k", DD)], [], [("i1", DD)]],
+        1: [[("in2k", DD), ("i384", NN)], [("in2k", DD), ("i384", NF)], [("in384", DD)], [("i1", DD)]],
         2: [[("in2k", DD), ("i1", NF), ("i384", NN), ("in2k", FL)], [("in2k", DD), ("i384", NF), ("in2k", FL)],
             [("in384", DD), ("in2k", FL)], [("i1", DD), ("i1", FL)]],
     }
-    ST2[3] = [ST2[2][0], [("ia", NF), ("ib", NF), ("i1", NN), ("in1", FL)], ST2[2][2], ST2[2][3]]
-    cp(A("wl", 0, 1024), A("ivi", 0, 1024))
-    for s in range(STEPS):
-        for c in range(2):
-            w = 400 if s else 784
-            iota(A("win%d%d" % (s, c), 0, w), [[0, w]], -126 if s == STEPS - 1 else int(NEG), 0)
-    ms(A("el0", 0, 32), 0)
-    cp(A("el0", 0, 16, 2), A("e0i", 0, 16))
-
-    WL, TAB = A("wl", 0, 1024), A("tab", 0, 8192)
-    ring = {"b": 0, "c": 0, "t": 0, "a": 0, "e": 0, "d": 0}
+    ST2[3] = [[("in2k", DD), ("i1", NF), ("i768", NN), ("in2k", FL)], [("ia", NF), ("ib", NF), ("i1", NN), ("in1", FL)],
+              [("in768", DD), ("in2k", FL)], ST2[2][3]]
+    ring = {"b": 0, "c": 0, "a": 0, "e": 0, "d": 0}
+    merged = [False]
     NB = PAR["NB"]
-    RB, TB = "ps%d" % NB, "ps%d" % (NB + 1)
-
-    def slot(n=128):
-        b, o = ring["t"].pop(0)
-        return A(b, o, n)
-
-    def places(part, s, c):
-        own = "ps%d" % (6 + c)
-        l0, l1, q2, l2 = [(own, o) for o in (320, 256, 288, 128)]
-        soon = s > 1 and PAR["EARLY"][s][c]
-        v = (own, 384) if soon else (own, 128)
-        m01, s01 = (own, 384), (own, 256)
-        if NB == 3 and not PAR["APART"]:
-            l0, l1, q2, l2, m01 = [("ps5", 256 * c + o) for o in (96, 0, 32, 64, 128)]
-        if (s, c) == (STEPS - 1, 1):
-            l0, l1, q2, l2, m01, v, s01 = [("ps%d" % b, o) for b, o in ((0, 0), (1, 0), (0, 128), (1, 128), (2, 0), (2, 128), (0, 256))]
-        if part is tail:
-            return (([(own, 128), (own, 0), (own, 128)] if s else []) + ([m01] if s > 1 else []) + ([l0] if soon else [])
-                    + [l1, q2] + ([v, s01] if s > 1 else []) + [(own, 0), l2])
-        return [(own, 0), (own, 128), (own, 0)]
-
-    def aside(s):
-        return not PAR["APART"] and s > 0 and any(PAR["KM"][s])
+    RB, TB = "ps4", "ps5"
+    TURN = col(15)
 
     def names(s, c):
-        w = "win%d%d" % (s, c)
-        u16, si = "u16_%d" % (s % 2), "si%d" % (s % 2)
-        d = {"P0": A(w, 400, 128, 3), "P1": A(w, 401, 128, 3), "K": A(w, 402, 128, 3), "z": A(w, 16, 128, 3), "Kd": A(w, 18, 128, 3),
-             "win": A(w, 0, 784), "e": A("el%d" % s, 16 * c, 8, 2), "A": A("el%d" % s, 16 * c + 1, 8, 2),
-             "c16": "c16_%d" % c, "Y": "yy%d" % c, "me": "me%d" % c, "tb": "tb%d" % c,
-             "e16": A(u16, 8 * c, 8), "ed16": A(u16, 32 + 8 * c, 8), "d16": A(u16, 48 + 8 * c, 8), "de": A(si, 48 + 8 * c, 8),
-             "old": A("wf", 256 + 128 * c, 128), "t": A("wf", 512 + 128 * c, 128), "dv": A("ps%d" % (6 + c), 256, 128) if aside(s) else A(RB, 256 + 128 * c, 128),
-             "R": A(RB, 0, 128), "cn": A("ps5", 0, 128) if PAR["APART"] else A(RB, 128, 128),
-             "km": A("ps5", 128 + 128 * c, 128) if PAR["APART"] else A(RB, 256 + 128 * c, 128)}
+        b, L = (2, 256) if s == STEPS - 1 else (c, 128)
+        W = 256 if c == 2 else 128
+        lo, g0, m = (128 * c if b == 2 and c < 2 else 0), 128 * (c % 2), W // 16
+        w, rows = "win%d%d" % (s, b), 16 + 3 * L + 3 * lo
+        u16, si, eh = "u16_%d" % (s % 2), "si%d" % (s % 2), "eh%d" % (s % 2)
+        d = {"P0": A(w, rows, W, 3), "P1": A(w, rows + 1, W, 3), "K": A(w, rows + 2 if s else 17, W, 3), "z": A(w, 16 + 3 * lo, W, 3),
+             "Kd": A(w, 18 + 3 * lo, W, 3), "cr": A(w, 17 + 3 * lo, W, 3), "win": A(w, 0, 16 + (6 if s else 3) * L),
+             "c16": "c16_%d" % c, "Y": "yy%d" % b, "y0": 16 * lo, "YW": A("yy%d" % b, 0, 16 * L + 16), "me": "me%d" % c,
+             "e16": A(u16, 16 + g0 // 16, m), "ed16": A(u16, g0 // 16, m), "d16": A(u16, 48 + g0 // 16, m), "e": A(si, 16 + g0 // 16, m),
+             "de": A(si, 96 + g0 // 16, m), "A": A("al%d" % (s % 2), g0 // 16, m),
+             "eh": B(eh, 0, 4) if c == 2 else B(eh, c, 2, 2), "ee": B(eh, 2, 2) if c == 2 else B(eh, 2 + c, 1),
+             "old": A("wf", 256 + g0, W), "t": A("wf", 512 + g0, W), "t2": A("wf", 768 + g0, W), "v": A("wi", 256 + g0, W),
+             "R": A(RB, g0, W), "one": A("ones", 0, W), "W": W, "b": b}
         for i, x in enumerate(["j16", "o0", "o1", "oK", "ja16"]):
-            d[x] = A("l16_%d" % c, 8 * i, 8)
-        for i, x in enumerate(["Rs", "r"]):
-            d[x] = A("rf%d" % c, 128 * i, 128)
-        for i, x in enumerate(["bt", "bt2"]):
-            d[x] = A("ri%d" % c, 128 * i, 128)
-        for i, x in enumerate(["cr", "mid", "h", "okb", "X", "oh", "gb", "ohq", "cB", "zg", "ad", "thq"]):
-            d[x] = A("rb%d" % c, 128 * i, 128)
-        for i, x in enumerate(["J", "f", "n0", "E"]):
-            d[x] = A("stk%d" % c, 128 * i, 128)
-        for i, x in enumerate(["ne", "s0", "s1", "D"]):
-            d[x] = A("sh%d" % c, 128 * i, 128)
+            d[x] = A("l16_%d" % b, m * i, m)
+        for buf, xs in (("rf", ["Rs", "r", "rb"]), ("stk", ["J", "f", "n0", "E"]), ("sh", ["ne", "s0", "s1"]),
+                        ("rb", ["mid", "h", "okb", "X", "oh", "gb", "ohq", "cB", "zg", "ad", "thq", "oh1", "hi"])):
+            for i, x in enumerate(xs):
+                d[x] = A("%s%d" % (buf, b), L * i + lo, W)
+        soon = PAR["EARLY"][s][c // 2 | c % 2]
+        at = {"u": 0, "hh": 128, "w3": 0, "midc": 384, "u1": 0, "u1b": 384, "rg": 128, "rg2": 384, "cp": 384, "pw": 256, "bt": 128,
+              "u2": 128, "m01": 384, "l1": 256, "q2": 288, "l0": 352, "v": 384 if soon else 128, "s01": 256, "cand": 0, "l2": 128}
+        at = {x: ("ps%d" % (6 + c), o) for x, o in at.items()}
+        if c == 2:
+            at = {x: ("ps%d" % k, o) for x, k, o in (
+                ("cp", 0, 0), ("u1", 1, 0), ("u1b", 1, 256), ("rg", 2, 0), ("rg2", 7, 256), ("pw", 3, 0), ("bt", 2, 256), ("u2", 3, 256),
+                ("m01", 5, 0), ("l1", 6, 0), ("q2", 7, 0), ("l0", 1, 0), ("v", 5, 256), ("s01", 0, 0), ("cand", 2, 0), ("l2", 6, 128))}
+        d["at"] = lambda x, n=W, o=0: A(at[x][0], at[x][1] + o, n)
         return d
 
     def early(s, c):
         d = names(s, c)
-        cp(d["e16"], d["e"])
-        cp(A(d["c16"], 0, 128), IND(WL, d["e16"]))
-        nv = PAR["VSHARE"][s][c]
-        pieces = [("V", 128 - nv, nv)] if nv else []
+        for h in range(2):
+            cp(A(d["c16"], 64 * h, 64), IND(WL, B("el%d" % s, 4 * c + 2 * h, 1)))
         lo = 0
-        while lo < 128 - nv:
-            hi = min(128 - nv, lo + PAR["GP"])
-            pieces.append(("S", lo, hi - lo))
-            lo = hi
-        if s == 0 and PAR["UN"][s][c][0][0] == 8:
-            pieces = [x for h in (0, 64) for x in (("V", h, nv // 2), ("S", h + nv // 2, 64 - nv // 2))]
-        for e, lo, n in pieces:
-            o, i = A(d["Y"], 16 * lo, 16 * n), IND(TAB, A(d["c16"], lo, n))
+        for n, e in zip(PAR["GP"][s][c], PAR["GE"][s][c]):
+            o, i = A(d["Y"], d["y0"] + 16 * lo, 16 * n), IND(TAB, A(d["c16"], lo, n))
             if e == "V":
                 ts(o, i, -125.0, OP.add)
             else:
                 act(o, i, AF.Identity, bias=-125.0)
-        if s == 0:
-            act(d["K"], IND(A("tk", 0, 1024), d["e16"]), AF.Identity, bias=NEG)
+            lo += n
 
     def side(s, c):
-        u16, si = "u16_%d" % (s % 2), "si%d" % (s % 2)
-        e, a = A("el%d" % s, 0, 16, 2), A("el%d" % s, 1, 16, 2)
-        ea, ed, dd, de, e4, e5, dq = [A(si, 16 * i, 16) for i in range(7)]
-        ts(e4, e, 4.0, OP.mult, 1.0, OP.add)
-        ts(dq, e, 5.0, OP.mult, 1.0, OP.add)
+        u16, si, a = "u16_%d" % (s % 2), "si%d" % (s % 2), A("al%d" % (s % 2), 0, 16)
+        ed, e, ea, dd, dq, e5, de = [A(si, 16 * i, 16) for i in range(7)]
+        cp(e, B("el%d" % s, 0, 4, 2))
+        cp(a, B("el%d" % s, 1, 4, 2))
+        ts(dq, B("el%d" % s, 0, 4, 2), 5.0, OP.mult, 1.0, OP.add)
         tt(e5, dq, a, OP.add)
-        tt(ea, e5, e4, OP.subtract)
+        tt(ea, e, a, OP.add)
         ts(ed, e5, 1023, OP.bitwise_and)
         ts(dq, e, 768, OP.bitwise_and)
         tt(dd, dq, A("lanel", 0, 16), OP.add)
-        tt(de, ed, e, OP.subtract)
-        cp(A(u16, 16, 48), A(si, 0, 48))
-        x0, old, xi, v = A("wf", 0, 256), A("wf", 256, 256), A("wi", 0, 256), A("wi", 256, 256)
-        act(x0, IND(WL, A(u16, 0, 16)), AF.Copy, scale=37.0)
-        act(old, IND(WL, A(u16, 48, 16)), AF.Copy)
-        tt(xi, IND(A("iot", 0, 1032), A(u16, 16, 16)), x0, OP.add)
-        ts(v, xi, 8191, OP.bitwise_and)
-        if aside(s):
+        cp(A(u16, 0, 64), A(si, 0, 64))
+        if s:
+            ts(B("eh%d" % (s % 2), 0, 4), A(si, 0, 32), 1024.0, OP.add)
+        else:
+            tt(de, ed, e, OP.subtract)
             for k in range(2):
                 d = names(s, k)
-                act(d["dv"], d["old"], AF.Copy)
-                tt(d["dv"], A("wi", 256 + 128 * k, 128), d["dv"], OP.subtract)
-        elif PAR["OFF"][0][s % 2]:
-            act(A(RB, 256, 256), old, AF.Copy)
-            tt(A(RB, 256, 256), v, A(RB, 256, 256), OP.subtract)
-        else:
-            tt(A(RB, 256, 256), v, old, OP.subtract)
+                act(d["K"], IND(A("tk", 0, 1024), d["e16"]), AF.Identity, bias=NEG)
+        x0, old, xi, v = A("wf", 0, 256), A("wf", 256, 256), A("wi", 0, 256), A("wi", 256, 256)
+        act(x0, IND(WL, A(u16, 16, 16)), AF.Copy, scale=37.0)
+        act(old, IND(WL, A(u16, 48, 16)), AF.Copy)
+        tt(xi, IND(A("iot", 0, 1032), A(u16, 32, 16)), x0, OP.add)
+        ts(v, xi, 8191, OP.bitwise_and)
         for k in range(2):
             d = names(s, k)
             act(d["Kd"], IND(A("tk", 0, 1024), d["ed16"]), AF.Identity, bias=NEG)
@@ -435,252 +466,256 @@ def build():
         else:
             ts(out, bank, CM, OP.add, CM, OP.is_equal)
 
-    def bulk(s, c):
+    def bulk0(s, c):
         d = names(s, c)
+        for h in range(2):
+            for b in range(2):
+                bank = "ps%d" % (ring["b"] % NB)
+                ring["b"] += 1
+                mm([(A(bank, 64 * j, 64), M("in15"), A(d["K"][0], 17 + 192 * h, 64, 3), j == 0, False) for j in range(8)])
+                mm([(A(bank, 64 * j, 64), M("i15"), A(d["Y"], 1024 * h + 8 * b + j, 64, 16), False, j == 7) for j in range(8)])
+                how = PAR["UN"][s][c][b][1]
+                test(A(d["me"], 1024 * h + 512 * b, 512), A(bank, 0, 512), how)
+                mm(grp(A(RB, d["R"][1] + 64 * h, 64),
+                       [(Z(int(how < 2), 8 * b + j), A(d["me"], 1024 * h + 512 * b + 64 * j, 64)) for j in range(8)],
+                       start=b == 0, stop=b == 1), TURN)
+
+    def bulk(s, c):
+        if s == 0:
+            return bulk0(s, c)
+        d = names(s, c)
+        at = d["at"]
         units = PAR["UN"][s][c]
-        dv = s and any(x[2] for x in units)
-        if s > 0:
-            ts(d["cr"], d["K"], -128.0, OP.is_gt)
-            if PAR["OFF"][s][c]:
+        km = PAR["WAY"][s][c] == "km"
+        nl, used_me = 64 if PAR["HALF"][s][c] else 128, 0
+        nk = 512 // nl
+
+        def ahead(lo):
+            cr, mid, thq, h, K, P0, P1 = [sub(d[x], lo, nl) for x in ("cr", "mid", "thq", "h", "K", "P0", "P1")]
+            ts(cr, K, -128.0, OP.is_gt)
+            half = [(M("i1"), P0)] if s == 1 else [(M("ih"), P0), (M("ih"), P1)]
+            mm(grp(at("u", nl, lo), half + [(M("in2k"), cr)]))
+            tt(mid, at("u", nl, lo), K, OP.max)
+            if s > 1:
+                act(thq, cr, AF.Identity, bias=1024.0, scale=10.0 - 1024.0)
+                mm(grp(at("hh", nl, lo), [(M("i1"), P0), (M("in1"), P1)]))
+                act(h, at("hh", nl, lo), AF.Abs, scale=0.5)
+            nt = 4 if PAR["TB4"] else nk
+            mm([(A(TB, 4 * lo * PAR["TB4"] + nl * j, nl), M("i1" if s > 1 else "i8k"), thq if s > 1 else cr, j == 0, j == nt - 1) for j in range(nt)])
+            terms = [(M("ck"), cr), (M("bdn"), cr), (M("ic0"), sub(M("one"), 0, nl))] if km else [(M("cb"), cr)]
+            mm(grp(sub(d["R"], lo, nl), terms, start=lo == 0, stop=False), TURN)
+        for u in range(4):
+            how, byv = units[u][1:]
+            lo, k0 = (64 * (u // 2), 8 * (u % 2)) if nl == 64 else (0, 4 * u)
+            w, end = 512, u == 3
+            if k0 == 0:
+                ahead(lo)
+                if any(x[2] for x in units[u:u + nk // 4 * 2] + (units if nl == 128 else [])):
+                    mm([(at("midc", nl, lo), M("i1"), sub(d["mid"], lo, nl), True, True)])
+            if u == 2:
                 act(d["n0"], d["P0"], AF.Relu, bias=-130.0, scale=-1.0)
-            else:
-                ts(d["n0"], d["P0"], -128.0, OP.is_lt)
-            u = slot()
-            half = [(M("i1"), d["P0"])] if s == 1 else [(M("ih"), d["P0"]), (M("ih"), d["P1"])]
-            mm(grp(u, half + [(M("in512"), d["cr"])]))
-            tt(d["mid"], u, d["K"], OP.max)
-            thq = d["cr"]
-        if s > 1:
-            thq = d["thq"]
-            ts(thq, d["K"], -128.0, OP.is_lt, 10.0 / 1024, OP.max)
-            hh = slot()
-            mm(grp(hh, [(M("i1"), d["P0"]), (M("in1"), d["P1"])]))
-            act(d["h"], hh, AF.Abs, scale=0.5)
-            w3 = slot()
-            mm(grp(w3, [(M("bd"), d["h"])]))
-            act(d["ad"], w3, AF.Sign, bias=0.5, scale=-1.0)
-        if s > 0:
-            mm([(A(TB, 128 * j, 128), M("i10" if s == 1 else "i1k"), thq, True, True) for j in range(4)])
-        if dv:
-            mm([(A("ps%d" % (6 + c), 384, 128), M("i1"), d["mid"], True, True)])
-        if s == 0 and units[0][0] == 8:
-            for h in range(2):
-                for b in range(2):
-                    bank = "ps%d" % (ring["b"] % NB)
-                    ring["b"] += 1
-                    items = []
-                    for j in range(8):
-                        items += grp(A(bank, 64 * j, 64), [(M("i15"), A(d["Y"], 1024 * h + 8 * b + j, 64, 16)),
-                                                           (M("in15"), A(d["K"][0], 402 + 192 * h, 64, 3))])
-                    mm(items)
-                    sg = 8 * b < signs(s, c)
-                    test(A(d["me"], 1024 * h + 512 * b, 512), A(bank, 0, 512), 2 if sg else min(units[b][1], 1))
-                    mm(grp(A(RB, 64 * h, 64), [(Z(1 + 3 * sg, 8 * b + j), A(d["me"], 1024 * h + 512 * b + 64 * j, 64)) for j in range(8)],
-                           start=b == 0, stop=b == 1))
-                    ops[-1]["w"].append(d["R"])
-            return
-        k0 = 0
-        for b, (nk, how, byv) in enumerate(units):
-            w = 128 * nk
-            if byv and s:
+                if s > 1:
+                    mm(grp(at("w3"), [(M("bd"), d["h"])]))
+                    act(d["ad"], at("w3"), AF.Sign, bias=0.5, scale=-1.0)
+            ys = [A(d["Y"], d["y0"] + 16 * lo + k0 + j, nl, 16) for j in range(nk)]
+            if byv:
                 bank = "dd%d" % (ring["d"] % 2)
                 ring["d"] += 1
                 for j in range(nk):
-                    tt(A(bank, 128 * j, 128), A(d["Y"], k0 + j, 128, 16), A("ps%d" % (6 + c), 384, 128), OP.subtract)
+                    tt(A(bank, nl * j, nl), ys[j], at("midc", nl, lo), OP.subtract)
             else:
-                bank = "ps%d" % (ring["b"] % (PAR["NB1"] if s else NB))
+                bank = "ps%d" % (ring["b"] % PAR["NB1"])
                 ring["b"] += 1
-                items = []
-                for j in range(nk):
-                    items += grp(A(bank, 128 * j, 128), [(M("i1" if s else "i15"), A(d["Y"], k0 + j, 128, 16)),
-                                                         (M("in1"), d["mid"]) if s else (M("in15"), d["K"])])
-                mms(items, A(bank, 0, w))
-            x = A(bank, 0, w)
-            me = A(d["me"], 128 * k0, w)
-            if s > 0:
-                a, n = A("aa%d" % (ring["a"] % 3), 0, w), A("nc%d" % (ring["a"] % 3), 0, w)
-                ring["a"] += 1
-                act(a, x, AF.Abs, scale=SC)
-                tt(n, a, A(TB, 0, w), OP.is_lt if s == 1 else OP.is_ge)
-                bank = "ps%d" % (PAR["NB1"] + ring["c"] % (NB - PAR["NB1"]))
-                ring["c"] += 1
-                x = A(bank, 0, w)
-            sg = k0 < signs(s, c)
-            if s == 1 and sg:
-                mm([(x, M("in1"), a, True, False), (x, M("bd10"), n, False, True)])
-                act(me, x, AF.Sign, bias=-0.25)
-            elif s == 1:
+                mm([(A(bank, nl * j, nl), M("in1"), sub(d["mid"], lo, nl), j == 0, False) for j in range(nk)])
+                mm([(A(bank, nl * j, nl), M("i1"), ys[j], False, j == nk - 1) for j in range(nk)])
+            me = A(d["me"], used_me, w)
+            used_me += w
+            a, n = A("aa%d" % (ring["a"] % 3), 0, w), A("nc%d" % (ring["a"] % 3), 0, w)
+            ring["a"] += 1
+            second = PAR["B2"][s > 1]
+            x = A(second[ring["c"] % len(second)], 0, w)
+            ring["c"] += 1
+            act(a, A(bank, 0, w), AF.Abs, scale=SC if s > 1 else 8192.0 / 5.5)
+            wt = 4 * nl if PAR["TB4"] else w
+            for o in range(0, w, wt):
+                tt(sub(n, o, wt), sub(a, o, wt), A(TB, 4 * lo * PAR["TB4"], wt), OP.is_lt if s == 1 else OP.is_ge)
+            if s == 1:
                 mm([(x, M("bd10"), n, True, True)])
                 tt(me, a, x, OP.is_lt)
             else:
-                if s > 1:
-                    mms([(x, M("ilam"), a, True, False)]
-                       + [(A(bank, 128 * j, 128), M("inls"), d["h"], False, False) for j in range(nk)] + [(x, M("bd1k"), n, False, True)])
-                test(me, x, 2 if sg else min(how, 1))
-            mes = [A(d["me"], 128 * (k0 + j), 128) for j in range(nk)]
-            terms = [(M("w2"), d["cr"])] if b == 0 and s > 0 else []
-            terms += [(Z((0 if s else 1) + 3 * sg, k0 + j), mes[j]) for j in range(nk)]
-            k0 += nk
-            apart = PAR["APART"]
-            items = grp(d["R"], terms, start=b == 0, stop=k0 == 16 and (s == 0 or apart))
-            if s > 0:
-                terms = [(M("in32"), d["cr"])] if b == 0 else []
-                km = PAR["KM"][s][c]
-                more = grp(d["cn"], terms + [(M("ih" if sg else "i1"), m) for m in mes], start=apart and b == 0, stop=k0 == 16 and not km)
-                if km:
-                    more += grp(d["km"], [(A("kmw", 128 * (k0 - nk + j), 128), m) for j, m in enumerate(mes)], start=False, stop=k0 == 16)
-                if apart:
-                    mms(items)
-                    items = []
-                items += more
-            mms(items, d["cn"] if apart and s else A(RB, 0, 256))
+                mm([(A(x[0], nl * j, nl), M("inls"), sub(d["h"], lo, nl), j == 0, False) for j in range(nk)])
+                mm([(x, M("ilam"), a, False, False)])
+                mm([(x, M("bd1k"), n, False, True)])
+                test(me, x, how)
+            mes = [sub(me, nl * j, nl) for j in range(nk)]
+            terms = [(A("wkm" if km else "wbit", 128 * (k0 + j), 128), mes[j]) for j in range(nk)]
+            items = grp(sub(d["R"], lo, nl), terms, start=False, stop=end and not km)
+            if km:
+                items += grp(sub(d["km"], lo, nl), [(A("kmw", 128 * (k0 + j), 128), m) for j, m in enumerate(mes)], start=False, stop=end)
+            mm(items, TURN)
 
     def join(s, c):
         d = names(s, c)
-        sg = signs(s, c)
-        ts(d["okb"], d["R"], A("sgc", 3 * sg + (s == 0), 1) if sg else 0.0 if s else 1.0, OP.is_equal)
-        if s > 0:
-            act(d["X"], d["cn"], AF.Exp, bias=0.5 * sg * math.log(64.0) if sg else None, scale=math.log(64.0))
-            if not PAR["KM"][s][c]:
-                act(d["Rs"], d["R"], AF.Relu, bias=A("sgc", 3 * sg + 2, 1) if sg else None)
-        u1 = slot()
-        mm(grp(u1, [(M("w1"), d["okb"])]))
-        act(d["f"], u1, AF.Relu)
-        tt(d["t"], d["f"], d["dv"], OP.mult)
-        tt(IND(WL, d["d16"]), d["old"], d["t"], OP.add)
+        at = d["at"]
+        if s == 0:
+            act(d["okb"], d["R"], AF.Identity, bias=col(P1) if PAR["UN"][s][c][0][1] == 2 else None)
+        else:
+            act(d["X"], d["R"], AF.Exp, bias=-8 * math.log(1024.0), scale=math.log(1024.0) / GB)
+            act(d["hi"], d["R"], AF.Identity, bias=191.875, scale=1.0 / GB)
+            act(d["Rs"], d["R"], AF.Identity, bias=0.5)
+            late([(at("cp"), M(w), d[x]) for w, x in (("inb", "one"), ("igb", "hi"), ("wrot", "cr"), ("ih", "one"))], 3, c == 2)
+            tt(d["okb"], at("cp"), d["Rs"], OP.is_equal)
+        late([(at("u1"), M("w16k"), d["okb"])], 1, False)
+        act(d["f"], at("u1"), AF.Relu, scale=1.0 / 16384)
+        late([(at("u1b"), M("i8k"), d["one"]), (at("u1b"), M("wn16k"), d["okb"])], 2, False)
+        tt(d["t"], at("u1"), d["v"], OP.min)
+        tt(d["t2"], at("u1b"), d["old"], OP.min)
+        tt(IND(WL, d["d16"]), d["t"], d["t2"], OP.max)
 
-    def tolist(out, zt, src, n, extra):
-        items = [(out, Z(zt, r), A(src[0], src[1] + r, n, 16), r == 0, r == 15) for r in range(16)]
-        items[1:1] = [(A(out[0], out[1], cnt(x)), m, x, False, False) for x, m in extra]
-        mm(items)
+    def late(items, n, apart):
+        items = [(o, l, r, i == 0, i == len(items) - 1) for i, (o, l, r) in enumerate(items)]
+        turn = A("coli", int(items[0][0][0][2:]) + 8, 1) if merged[0] else None
+        if apart and n < len(items):
+            mm(items[:-n], turn)
+            items = items[-n:]
+        mm(items, turn)
+
+    def tolist(out, zt, src, n, extra, apart=False):
+        items = [(A(out[0], out[1], cnt(x)), m, x) for x, m in extra]
+        rows = [(out, Z(zt, r), A(src[0], src[1] + r, n, 16)) for r in range(16)]
+        if apart:
+            late([(out, A("cb", 768, 128), A("ones", 0, n))] + items + rows, 16, True)
+        else:
+            late(rows[:1] + items + rows[1:], 16, False)
 
     def tail(s, c):
         d = names(s, c)
+        at = d["at"]
         last = s == STEPS - 1
-        soon = s > 1 and PAR["EARLY"][s][c]
-        J = d["f"]
-        km = s > 0 and PAR["KM"][s][c]
-        if km:
-            J, oh = d["J"], d["oh"]
-            rg = slot()
-            if km > 1:
-                oh = d["gb"]
-                mm(grp(rg, [(M("warg"), d["X"])]))
-                ts(oh, rg, -8.0, OP.is_lt)
-            mm(grp(rg, [(M("warg"), d["X"]), (M("bdbig"), d["f"])]))
-            ts(d["oh"], rg, -8.0, OP.is_lt)
-            tt(d["mid"], d["km"], oh, OP.mult)
-            slot()
-            u2 = slot()
-            u2 = A(u2[0], 0, 128)
-            mm(grp(u2, [(M("bd"), d["mid"]), (M("tri"), d["f"])]))
-            ts(J, u2, col(KT), OP.is_ge)
-        elif s > 0:
-            J = d["J"]
-            rg = slot()
-            mm(grp(rg, [(M("warg"), d["X"]), (M("bdbig"), d["f"])]))
-            ts(d["oh"], rg, -8.0, OP.is_lt)
-            pw = slot()
-            mm(grp(pw, [(M("wpw"), d["oh"])]))
-            tt(d["bt"], pw, d["Rs"], OP.mult)
-            ts(d["bt2"], d["bt"], 32768, OP.bitwise_and)
-            ts(d["gb"], d["bt2"], 0.5, OP.is_gt)
-            u2 = slot()
-            mm(grp(u2, [(M("i1"), d["f"]), (M("w1"), d["gb"])]))
-            act(J, u2, AF.Relu)
-        YW = A(d["Y"], 0, 2064)
-        base = (A("basel", 0, 8), M("i1"))
+        W, spec = d["W"], PAR["SPEC"][s][min(c, 1)]
+        m = W // 16
+        soon = s > 1 and PAR["EARLY"][s][min(c, 1)]
+        J = d["J"] if s else d["f"]
+        if s > 0:
+            warg, low = M("wargb"), -2.0 ** -75
+            oh = d["oh"]
+            if spec:
+                oh = d["oh1"]
+                late([(at("rg"), warg, d["X"])], 1, False)
+                ts(oh, at("rg"), low, OP.is_lt)
+                late([(at("rg2"), M("i1"), oh), (at("rg2"), M("bdn"), d["okb"])], 2, False)
+                act(d["oh"], at("rg2"), AF.Relu)
+            else:
+                late([(at("rg"), warg, d["X"]), (at("rg"), M("bdbig"), d["okb"])], 1, last)
+                ts(oh, at("rg"), low, OP.is_lt)
+            late([(at("pw"), M("wpw"), oh)], 1, False)
+            tt(at("bt"), at("pw"), d["Rs"], OP.mult)
+            ts(d["rb"], at("bt"), C1, OP.add, C1, OP.subtract)
+            tt(d["gb"], at("bt"), d["rb"], OP.is_lt)
+            if spec:
+                late([(at("u2"), M("wok"), d["okb"]), (at("u2"), M("w1"), d["gb"])], 1, last)
+                ts(J, at("u2"), 0.5, OP.is_gt)
+            else:
+                late([(at("u2"), M("i1"), d["f"]), (at("u2"), M("w1"), d["gb"])], 1, last)
+                act(J, at("u2"), AF.Relu)
+        YW = d["YW"]
+        base = (A("basel", 0, m), M("i1"))
         zg = zf = d["z"]
         if s > 1:
-            m01 = slot()
-            mm(grp(m01, [(M("ih"), d["P0"]), (M("ih"), d["P1"]), (M("in1"), d["h"]), (M("i512"), d["ad"]), (M("bdn1k"), d["f"])]))
-            act(d["E"], m01, AF.Identity, bias=1536.0)
+            late([(at("m01"), M(w), d[x]) for w, x in (("ih", "P0"), ("ih", "P1"), ("in1", "h"), ("i512", "ad"), ("bdn1k", "f"))], 1, last)
+            act(d["E"], at("m01"), AF.Identity, bias=1536.0)
         if soon:
-            l0 = slot(8)
-            tolist(l0, 2, d["f"], 8, [base])
-            cp(d["ja16"], l0)
+            tolist(at("l0", m), 2, d["f"], m, [base])
+            cp(d["ja16"], at("l0", m))
             zf = d["zg"]
             tt(zf, IND(YW, d["ja16"]), d["E"], OP.min)
-        nq = 8 * (1, 3, 4, 4)[s]
-        l1 = slot(nq)
-        if km:
-            tolist(l1, 1, J, nq, [(A("basel", 0, 8), M("in1"))])
-            ts(d["j16"], A(l1[0], l1[1], 8), -1.0, OP.mult, 32.0, OP.add)
-        else:
-            tolist(l1, 2, J, nq, [base])
-            cp(d["j16"], A(l1[0], l1[1], 8))
+        nq = m * (1, 3, 4, 4)[s]
+        l1 = at("l1", nq)
+        tolist(l1, 2, J, nq, [base])
+        cp(d["j16"], at("l1", m))
         if s > 1:
             tt(zg, IND(YW, d["j16"]), d["E"], OP.min)
         else:
             act(zg, IND(YW, d["j16"]), AF.Copy)
-        lq, lf, li = "lq%d" % c, "lf%d" % c, "li%d" % c
-        tt(A(lq, 0, nq), l1, A("thl", 32 * bool(km), nq), OP.is_lt)
-        q2 = slot(32)
+        lq, lf, th = "lq%d" % c, "lf%d" % c, "th%d" % c
+        sl, sb = "sl%d%d" % (s, c), "sb%d%d" % (s, c)
+        pieces = [(0, W)] if c else [(0, 64), (64, 64)]
+
+        def lists(out, row, lo, n):
+            if last:
+                return A(out, 0, m)
+            return B("el%d" % (s + 1), row, 1) if (c, lo) == (0, 0) else B(sl, lo // 32 + row, n // 64, 2)
+        tt(A(lq, 0, nq), l1, A("thl", 32 * last, nq), OP.is_lt)
+        if s == 0:
+            tt(A(lf, 24, 8), A(lq, 8 * DD, 8), d["de"], OP.mult)
+            tt(A(lf, 32, 8), A(lf, 24, 8), d["e"], OP.add)
+            for lo, n in pieces:
+                cp(lists("oye", 0, lo, n), A(lf, 32 + lo // 16, n // 16))
         items = []
         for i, terms in enumerate(ST2[s]):
-            items += grp(A(q2[0], q2[1] + 8 * i, 8), [(M(m), A(lq, 8 * x, 8)) for m, x in terms])
+            items += grp(at("q2", m, m * i), [(M(w), A(lq, m * x, m)) for w, x in terms] + ([(M("i1"), d["A"])] if i == 3 else []))
+        if s:
+            items.append((at("q2", 2 * m, 4 * m), M("i2k"), A(lq, 0, 2 * m), True, s == 1))
+            if s > 1:
+                items.append((at("q2", m, 5 * m), M("i2k"), A(lq, m * FL, m), False, True))
         mm(items)
-        tt(A(lf, 0, 24), A(q2[0], q2[1], 24), A("con", 24 * last, 24), OP.add)
-        sl, sb = "sl%d%d" % (s, c), "sb%d%d" % (s, c)
-        lo = 128 * c
-        en = A(sl, 0, 8, 2)
-        tt(A("oya", 8 * c, 8) if last else A(sl, 1, 8, 2), A(q2[0], q2[1] + 24, 8), d["A"], OP.add)
-        tt(A(lf, 24, 8), A(lq, 8 * DD, 8), d["de"], OP.mult)
-        tt(en if s == 0 else A(lf, 32, 8), A(lf, 24, 8), d["e"], OP.add)
+        no = 3 * m if s else 2 * m
+        tt(A(lf, 0, no), at("q2", no), A("con", (0, 8, 8, 32)[s], no), OP.add)
+        for lo, n in pieces:
+            cp(lists("oya", 1, lo, n), at("q2", n // 16, 3 * m + lo // 16))
+        if s:
+            tt(A(th, 0, 2 * m), at("q2", 2 * m, 4 * m), d["eh"], OP.min)
         if s > 1:
-            v = slot()
-            mm(grp(v, [(M("inq"), d["ad"]), (M("bdp"), d["f"]), (M("bd"), zf)]))
-            ts(d["r"], v, CM, OP.add, CM, OP.subtract)
-            tt(d["ohq"], v, d["r"], OP.is_equal)
-            items, s01 = [], slot(256)
+            late([(at("v"), M("inq"), d["ad"]), (at("v"), M("bdp"), d["f"]), (at("v"), M("bd"), zf)], 1, last)
+            ts(d["r"], at("v"), CM, OP.add, CM, OP.subtract)
+            tt(d["ohq"], at("v"), d["r"], OP.is_equal)
+            items = []
             for i, p in enumerate(("P0", "P1")):
                 more = [(M("i512"), d["ad"]), (M("i1536"), d["oh"])] if last and i else [(M("i1k"), d["oh"])]
-                items += grp(A(s01[0], s01[1] + 128 * i, 128), [(M("i15"), d[p])] + more + [(M("in15"), zg)])
-            mm(items)
-            ts(A(d["s0"][0], d["s0"][1], 256), s01, CM - 1024, OP.add, CM, OP.is_equal)
+                items += [(at("s01", W, W * i), l, r) for l, r in [(M("i15"), d[p])] + more]
+            late(items + [(at("s01", W, W * i), M("in15"), zg) for i in range(2)], 2, last)
+            ts(A(d["s0"][0], d["s0"][1], 2 * W), at("s01", 2 * W), CM - 1024, OP.add, CM, OP.is_equal)
         if s > 0:
-            cand = slot()
-            more = [(M("iw"), d["ohq"])] if s > 1 else []
-            mm(grp(cand, [(M("iw"), d["oh"]), (M("iq"), zg)] + more))
-            ts(d["ne"], cand, 30.875 - 1024, OP.add, 0.0, OP.max)
-            act(d["cB"], cand, AF.Identity, bias=col(NW4), scale=4.0)
-            n2 = 8 if s == 1 else 24
-            l2 = slot(n2)
-            tolist(l2, "h", d["ne"], n2, [])
-            tt(A(li, 0, 8), A(l2[0], l2[1], 8), A(lf, 32, 8), OP.max)
-            ts(en, A(li, 0, 8), 1023, OP.bitwise_and)
+            more = [(M("iq"), zg)] + ([(M("iw"), d["ohq"])] if s > 1 else [])
+            late([(at("cand"), l, r) for l, r in [(M("iw"), d["oh"])] + more[::-1 if soon else 1]], 1, last)
+            ts(d["ne"], at("cand"), 30.875 - 1024, OP.add, 0.0, OP.max)
+            act(d["cB"], at("cand"), AF.Identity, bias=col(NW4), scale=4.0)
+            n2 = m if s == 1 else 3 * m
+            tolist(at("l2", n2), "h", d["ne"], n2, [(d["ee"], M("i1")), (A(th, 0, m), M("i1")), (A(th, m, m), M("in1"))], last)
+            for lo, n in pieces:
+                ts(lists("oye", 0, lo, n), at("l2", n // 16, lo // 16), -1024.0, OP.add, 0.0, OP.max)
         if not last:
-            send(s, c, "l", sl, "el%d" % (s + 1), 16 * c, 8)
-        else:
-            cp(A("oye", 8 * c, 8), en)
+            send(s, c, "l", lambda h: B(sl, 2 * h, 2), lambda h: B("el%d" % (s + 1), 4 * c + 2 * h, 2))
         if last:
-            cp(d["oK"], A(lf, 16, 8))
-            tt(A(lf, 8, 8), A(lf, 8, 8), A(l2[0], l2[1] + 8, 8), OP.add)
-            tt(A(lf, 0, 8), A(lf, 0, 8), A(l2[0], l2[1] + 8, 8), OP.subtract)
-            tt(A(lf, 8, 8), A(lf, 8, 8), A(l2[0], l2[1] + 16, 8), OP.add)
-            cp(d["o0"], A(lf, 0, 8))
-            ts(d["o1"], A(lf, 8, 8), 2048.0, OP.mult)
-        else:
-            if s > 1:
-                tt(A(lf, 0, 8), A(lf, 0, 8), A(l2[0], l2[1] + 8, 8), OP.subtract)
-                tt(A(lf, 8, 8), A(lf, 8, 8), A(l2[0], l2[1] + 16, 8), OP.add)
-            cp(A("l16_%d" % c, 8, 24), A(lf, 0, 24))
-        if not last:
-            act(A(sb, 0, 128, 3), IND(d["win"], d["o0"]), AF.Copy)
-            act(A(sb, 1, 128, 3), IND(d["win"], d["o1"]), AF.Copy)
+            cp(d["oK"], A(lf, 2 * m, m))
+            tt(A(lf, 3 * m, m), A(lf, m, m), at("l2", m, m), OP.add)
+            tt(A(lf, 0, m), A(lf, 0, m), at("l2", m, m), OP.subtract)
+            tt(A(lf, m, m), A(lf, 3 * m, m), at("l2", m, 2 * m), OP.add)
+            cp(d["o0"], A(lf, 0, m))
+            ts(d["o1"], A(lf, m, m), 2048.0, OP.mult)
+            act(A("oy0", 0, W), IND(d["win"], d["o0"]), AF.Identity, bias=125.0)
+            act(A("oy1", 0, W), IND(d["win"], d["o1"]), AF.Identity, bias=125.0)
+            tt(d["X"], IND(d["win"], d["oK"]), d["cB"], OP.max)
+            ts(A("oyk", 0, W), d["X"], 125.0, OP.add, -1.0, OP.max)
+            return
+        if s > 1:
+            tt(A(lf, 0, 8), A(lf, 0, 8), at("l2", 8, 8), OP.subtract)
+            tt(A(lf, 8, 8), A(lf, 8, 8), at("l2", 8, 16), OP.add)
+        cp(A("l16_%d" % c, 8, no), A(lf, 0, no))
+        nxt = names(s + 1, c)["P0"]
+        for lo, n in pieces:
+            buf, o = nxt[:2] if (c, lo) == (0, 0) else (sb, 3 * lo)
+            o0, o1, oK = [IND(d["win"], sub(d[x], lo // 16, n // 16)) for x in ("o0", "o1", "oK")]
             if s == 0:
-                cp(A(sb, 2, 128, 3), IND(d["win"], d["oK"]))
+                act(A(buf, o, n, 3), o1, AF.Copy)
+                cp(A(buf, o + 2, n, 3), o0)
             else:
-                tt(A(sb, 2, 128, 3), IND(d["win"], d["oK"]), d["cB"], OP.max)
-            send(s, c, "r", sb, "win%d%d" % (s + 1, c), 400, 192)
-        else:
-            y0, y1, yk = A("oy0", lo, 128), A("oy1", lo, 128), A("oyk", lo, 128)
-            act(y0, IND(d["win"], d["o0"]), AF.Identity, bias=125.0)
-            act(y1, IND(d["win"], d["o1"]), AF.Identity, bias=125.0)
-            tt(A(sb, 0, 128), IND(d["win"], d["oK"]), d["cB"], OP.max)
-            ts(yk, A(sb, 0, 128), 125.0, OP.add, -1.0, OP.max)
+                act(A(buf, o, n, 3), o0, AF.Copy)
+                act(A(buf, o + 1, n, 3), o1, AF.Copy)
+                tt(A(buf, o + 2, n, 3), oK, sub(d["cB"], lo, n), OP.max)
+        send(s, c, "r", lambda h: A(sb, 192 * h, 192), lambda h: A(nxt[0], nxt[1] + 192 * h, 192))
 
-    def send(s, c, kind, src, dst, at, w):
+    def send(s, c, kind, src, dst):
         blocks = [(h, 2 * c + h) for h in range(2)]
         far = [(h, b) for h, b in blocks if b % N]
         name = "ar%s%d%d" % (kind, s + 1, c)
@@ -695,28 +730,28 @@ def build():
                 mask = sum(1 << e for e in eng[i * k:(i + 1) * k])
                 ad = topo.addr(to)
                 trs.append(RemoteDMATransfer(dst_ids=[DstId(rid=ad[0], pnc=ad[1])], dma_engine_mask=mask, remote_sem=T.sem[name],
-                                             src=R(A(src, h * w, w)), dst=R(A(dst, at + h * w, w))))
+                                             src=R(src(h)), dst=R(dst(h))))
                 X["sent"][0] += k
             return q.remote_dma_fused(trs, local_sem=T.sem["sent"])
-        add("G", call, [A(dst, at + h * w, w) for h, b in far], [A(src, h * w, w) for h, b in far], 700, sem=(name, "far"),
-            lat=1700 + 600 * len(far))
-        for h, b in blocks:
-            if b % N == 0:
-                dma(A(dst, at + h * w, w), A(src, h * w, w), "lo%s%d" % (kind, s + 1), 2200)
+        add("G", call, [dst(h) for h, b in far], [src(h) for h, b in far], 700, sem=(name, "far"), lat=1700 + 600 * len(far) + PAR["FIRST"] * ((s, c, kind) == (0, 0, "l")))
 
     for s in range(STEPS):
         for k, (part, c) in enumerate(((early, 0), (early, 1), (side, 0), (bulk, 0), (join, 0), (bulk, 1), (tail, 0), (join, 1), (tail, 1))):
             first = len(ops)
-            ring["t"] = places(part, s, c)
-            part(s, c)
+            if s < STEPS - 1 or part not in (join, tail):
+                part(s, c)
+            elif c:
+                merged[0] = True
+                part(s, 2)
             for o in ops[first:]:
                 o["part"] = (s, k)
-
-    def store(name, buf, n):
-        add("Y", lambda q, R, X: q.dma_start(X["T"][name][:], R(A(buf, 0, n))), [], [A(buf, 0, n)], 60, sem=("outs", 16), lat=2300 + 2 * n)
     for name, buf, n in (("yi", "wl", 1024), ("ye", "oye", 16), ("ya", "oya", 16), ("y0", "oy0", 256), ("yk", "oyk", 256), ("y1", "oy1", 256)):
-        store(name, buf, n)
-    return ops
+        add("Y", lambda q, R, X, name=name, buf=buf, n=n: q.dma_start(X["T"][name][:], R(A(buf, 0, n))), [], [A(buf, 0, n)], 60,
+            sem=("outs", 16), lat=2300 + 2 * n)
+    body = ops[:]
+    del ops[:]
+    setup()
+    return ops + body
 
 
 def links(ops):
@@ -732,8 +767,8 @@ def links(ops):
         for kind, lst in (("r", o["r"]), ("w", o["w"])):
             for a in lst:
                 old = acc.get(a[0], [])
-                if kind == "w":
-                    old = [x for x in old if not (a[3] == 1 and a[1] <= x[2] and x[3] <= a[2])]
+                if kind == "w" and a[3] == 1 and (len(a) == 4 or a[4][2] == 1):
+                    old = [x for x in old if not (a[1] <= x[2] and x[3] <= a[2])]
                 acc[a[0]] = old + [(i, kind, a[1], a[2], a[3])]
         o["banks"] = sorted(set(a[0] for a in o["r"] + o["w"] if isps(a)))
     return pred
@@ -750,8 +785,9 @@ def arrange(ops, pred, succ, prio):
             ready[eng[i]].append(i)
     free = {e: 0.0 for e in "VSPGY"}
     fin = [0.0] * n
-    bank, extra, order = {}, [[] for _ in ops], []
-    while len(order) < n:
+    start = [0.0] * n
+    bank, done = {}, 0
+    while done < n:
         best = None
         for e in "VSPGY":
             st = []
@@ -768,138 +804,19 @@ def arrange(ops, pred, succ, prio):
                     best = (t0, st)
         t, i = max((x for x in best[1] if x[0] <= best[0] + PAR["WIN"]), key=lambda x: (prio[x[1]], -x[1]))
         o, e = ops[i], eng[i]
-        o["t"] = t
+        start[i] = t
         free[e] = t + o["cost"]
         fin[i] = t + o["cost"] + o["lat"]
         for b in o["banks"]:
-            extra[i] += [j for e2, j in bank.get(b, {}).items() if e2 != e]
             bank.setdefault(b, {})[e] = i
-        order.append(i)
+        done += 1
         ready[e].remove(i)
         for k in succ[i]:
-            if not (e == "P" and eng[k] == "P"):
-                dep[k] = max(dep[k], fin[i] + HOP)
+            dep[k] = max(dep[k], start[i] if e == "P" and eng[k] == "P" else fin[i] + HOP)
             left[k] -= 1
             if left[k] == 0:
                 ready[eng[k]].append(k)
-    return max(fin), order, extra, fin
-
-
-def place(ops, gap, back, key, least):
-    n = len(ops)
-    left = [len(x) for x in gap]
-    est = list(least)
-    st = [0.0] * n
-    ready = [i for i in range(n) if left[i] == 0]
-    busy = {}
-    while ready:
-        i = min(ready, key=lambda x: key[x])
-        ready.remove(i)
-        o = ops[i]
-        c, e = o["cost"], o["eng"]
-        lists = [(busy.setdefault(e, []), 0.0)]
-        for b in o["banks"]:
-            lists += [(busy.setdefault(b + e2, []), HOP) for e2 in "VSP" if e2 != e]
-        t, moved = est[i], True
-        while moved:
-            moved = False
-            for l, pad in lists:
-                k = len(l) - 1
-                while k >= 0 and l[k][1] + pad > t:
-                    k -= 1
-                for a, z in l[k + 1:]:
-                    if a - pad >= t + c:
-                        break
-                    t, moved = z + pad, True
-        st[i] = t
-        for name in [e] + [b + e for b in o["banks"]]:
-            l = busy.setdefault(name, [])
-            k = len(l)
-            while k > 0 and l[k - 1][0] > t:
-                k -= 1
-            l.insert(k, (t, t + c))
-        for k, x in back[i]:
-            est[k] = max(est[k], t + c + x)
-            left[k] -= 1
-            if left[k] == 0:
-                ready.append(k)
-    return st
-
-
-def polish(ops, gap, back, order, rng):
-    n = len(ops)
-    code = {e: k for k, e in enumerate("VSPGY")}
-    eng = [code[o["eng"]] for o in ops]
-    cost = [o["cost"] for o in ops]
-    banks = [[int(b[2:]) for b in o["banks"]] for o in ops]
-    ends = [i for i in range(n) if not back[i]]
-
-    def run(order):
-        fin, why, last = [0.0] * n, [-1] * n, [-1] * 5
-        used = [[-1] * 3 for _ in range(8)]
-        for i in order:
-            e = eng[i]
-            t, w = 0.0, -1
-            for j, x in gap[i]:
-                if fin[j] + x > t:
-                    t, w = fin[j] + x, j
-            j = last[e]
-            if j >= 0 and fin[j] > t:
-                t, w = fin[j], j + n
-            for b in banks[i]:
-                u = used[b]
-                for e2 in range(3):
-                    if e2 != e and u[e2] >= 0 and fin[u[e2]] + HOP > t:
-                        t, w = fin[u[e2]] + HOP, u[e2] + n
-                u[e] = i
-            fin[i], why[i], last[e] = t + cost[i], w, i
-        i = max(ends, key=lambda x: fin[x] + ops[x]["lat"])
-        end = fin[i] + ops[i]["lat"]
-        return end + PAR["SOFT"] * sum(fin[x] for x in marks) / len(marks), fin, why, i, end
-    marks = [i for i in range(n) if ops[i]["part"] and (eng[i] == 3 or ops[i]["w"][0][0] == "wl")] + ends[-6:]
-    now = run(order)
-    best = (now[4], now[1])
-    moves = PAR["MOVES"]
-    for k in range(moves):
-        i = now[3] if rng.random() < 0.3 else marks[int(rng.integers(len(marks)))]
-        pairs = []
-        while i >= 0 and len(pairs) < 40:
-            w = now[2][i]
-            if w >= n:
-                w -= n
-                pairs.append((w, i))
-            i = w
-        if not pairs:
-            continue
-        j, i = pairs[int(rng.integers(len(pairs)))]
-        pos = {x: p for p, x in enumerate(order)}
-        a, b = pos[j], pos[i]
-        mid = order[a:b + 1]
-        keep = rng.random() < PAR["KEEP"]
-        if rng.random() < 0.5:
-            go, held = {i}, set() if eng[i] == eng[j] else {eng[i]}
-            for y in mid[-2::-1]:
-                if (keep and eng[y] in held) or any(z in go for z, _ in back[y]):
-                    go.add(y)
-                    held.add(eng[y])
-            if j in go:
-                continue
-            new = order[:a] + [x for x in mid if x in go] + [x for x in mid if x not in go] + order[b + 1:]
-        else:
-            go, held = {j}, set() if eng[i] == eng[j] else {eng[j]}
-            for y in mid[1:]:
-                if (keep and eng[y] in held) or any(z in go for z, _ in gap[y]):
-                    go.add(y)
-                    held.add(eng[y])
-            if i in go:
-                continue
-            new = order[:a] + [x for x in mid if x not in go] + [x for x in mid if x in go] + order[b + 1:]
-        got = run(new)
-        if got[0] <= now[0] + PAR["TEMP"] * (1.0 - k / moves) * rng.exponential():
-            now, order = got, sorted(new, key=lambda x: got[1][x] - cost[x])
-            if got[4] < best[0]:
-                best = (got[4], got[1])
-    return best[0], [best[1][i] - cost[i] for i in range(n)]
+    return start
 
 
 def polish(ops, gap, back, order, rng):
@@ -1000,60 +917,175 @@ def polish(ops, gap, back, order, rng):
     return best[0], [best[1][i] - cost[i] for i in range(n)]
 
 
+def listed(eng, cost, banks, gap, back, least, prio):
+    n, win = len(eng), PAR["WIN"]
+    left = [len(x) for x in gap]
+    dep = list(least)
+    ready = [[] for _ in range(5)]
+    for i in range(n):
+        if not left[i]:
+            ready[eng[i]].append(i)
+    free = [0.0] * 5
+    st = [0.0] * n
+    bk = [[0.0] * 8 for _ in range(3)]
+    first, times, stale = [1e18] * 5, [None] * 5, {0, 1, 2, 3, 4}
+    for _ in range(n):
+        for e in stale:
+            f, l = free[e], []
+            for i in ready[e]:
+                t = dep[i]
+                for b in banks[i]:
+                    if bk[e][b] > t:
+                        t = bk[e][b]
+                l.append(t if t > f else f)
+            first[e], times[e] = min(l) if l else 1e18, l
+        t0 = min(first)
+        e = first.index(t0)
+        l, r = times[e], ready[e]
+        bi = 0
+        if len(r) > 1:
+            t0, bp = t0 + win, -1e18
+            for x in range(len(r)):
+                if l[x] <= t0 and prio[r[x]] > bp:
+                    bi, bp = x, prio[r[x]]
+        i = r.pop(bi)
+        st[i] = l[bi]
+        z = free[e] = l[bi] + cost[i]
+        stale = {e}
+        if banks[i]:
+            stale = {0, 1, 2}
+            for b in banks[i]:
+                bk[e - 1][b] = bk[e - 2][b] = z + HOP
+        for k, x in back[i]:
+            if z + x > dep[k]:
+                dep[k] = z + x
+            left[k] -= 1
+            if not left[k]:
+                ready[eng[k]].append(k)
+                stale.add(eng[k])
+    return st
+
+
+def replay(order, eng, cost, banks, gap, lat, fc, fl):
+    fin, free, end = [0.0] * len(eng), [0.0] * 5, 0.0
+    bk = [[0.0] * 3 for _ in range(8)]
+    for i in order:
+        e = eng[i]
+        t = free[e]
+        for j, x in gap[i]:
+            if fin[j] + x > t:
+                t = fin[j] + x
+        for b in banks[i]:
+            if bk[b][e] > t:
+                t = bk[b][e]
+        t += cost[i] * fc[i]
+        fin[i] = free[e] = t
+        for b in banks[i]:
+            bk[b][e - 1] = bk[b][e - 2] = t + HOP * fl
+        if t + lat[i] > end:
+            end = t + lat[i]
+    return end
+
+
+def case(ops, gap, fc, fl, fr, fg, ff=0.0):
+    far = [bool(o["sem"]) and o["sem"][1] == "far" for o in ops]
+    return ([[(j, ops[j]["lat"] * (fr if far[j] else 1.0) + HOP * fl if x else 0.0) for j, x in g] for g in gap], [fr + ff * (o["part"][0] == 0) if x else fc * (1.0 + (fg - 1.0) * o["ind"] / o["cost"]) for x, o in zip(far, ops)], fl)
+
+
+def search(ops, gap, back):
+    n = len(ops)
+    eng = ["VSPGY".index(o["eng"]) for o in ops]
+    cost, lat = [o["cost"] for o in ops], [o["lat"] for o in ops]
+    banks = [[int(b[2:]) for b in o["banks"]] for o in ops]
+    rng = np.random.default_rng(PAR["SEED"])
+    prio = [0.0] * n
+    for i in range(n - 1, -1, -1):
+        prio[i] = cost[i] + max([prio[k] + x for k, x in back[i]] + [lat[i]])
+    both = [i for i in range(n) if "alt" in ops[i]]
+    marks = [i for i in range(n) if ops[i]["part"] and eng[i] == 3]
+    cases = [(case(ops, gap, *x[:5]), x[5]) for x in PAR["CASES"]]
+    now = best = (1e18, None, eng, cost, 1e18)
+    for it in range(PAR["ROUNDS"]):
+        eng, cost = now[2][:], now[3][:]
+        if it:
+            st = np.array(now[1])
+            near = np.abs(st - rng.random() * now[0]) < PAR["SPAN"]
+            z = rng.normal(0.0, PAR["NOISE"], n) * near * rng.random()
+            some = [i for i in both if near[i]]
+            if rng.random() < PAR["IDLE"]:
+                on = np.array(sorted((now[1][i], now[1][i] + cost[i]) for i in range(n) if eng[i] == 1) + [(1e9, 1e9)])
+                some = [i for i in some if eng[i] == 0 and on[np.searchsorted(on[:, 1], st[i] + 50.0), 0] > st[i] + 0.7 * cost[i]]
+            while some and rng.random() < PAR["FREE"]:
+                i = some[int(rng.integers(len(some)))]
+                eng[i] = 1 - eng[i]
+                cost[i] = ops[i]["cost"] if "VS"[eng[i]] == ops[i]["eng"] else ops[i]["alt"][2]
+            if rng.random() < PAR["BACK"]:
+                late = listed(eng, cost, banks, back, gap, lat, (st + cost + z).tolist())
+                prio = [late[i] + cost[i] for i in range(n)]
+            else:
+                prio = (z - st).tolist()
+        st = listed(eng, cost, banks, gap, back, [0.0] * n, prio)
+        end = max(st[i] + cost[i] + lat[i] for i in range(n))
+        end += PAR["SOFT"] * (sum(st[i] for i in marks) / len(marks) - end / 2) + PAR["LEAN"] * sum(cost[i] for i in both if not eng[i])
+        plain = end
+        if end >= now[4] + 1500.0:
+            continue
+        if PAR["CASES"] and end < now[4] + 1500.0:
+            order = sorted(range(n), key=lambda i: st[i])
+            end = (end + sum(w * replay(order, eng, cost, banks, g, lat, fc, fl) for (g, fc, fl), w in cases)) / (1 + len(cases))
+        if end <= now[0] + PAR["TEMP"] * (1.0 - it / PAR["ROUNDS"]) * rng.exponential():
+            now = (end, st, eng, cost, plain)
+            if end < best[0]:
+                best = now
+    for i in both:
+        if "VS"[best[2][i]] != ops[i]["eng"]:
+            ops[i]["eng"], ops[i]["call"], ops[i]["cost"] = ops[i]["alt"]
+    return max(best[1][i] + best[3][i] + lat[i] for i in range(n)), best[1]
+
+
 def plan():
     ops = build()
     n = len(ops)
     pred = links(ops)
+    for i in (1, 2):
+        pred[i].add(i - 1)
     succ = [[] for _ in ops]
     for i in range(n):
         for j in pred[i]:
             succ[j].append(i)
-    prio = [0.0] * n
-    for i in range(n - 1, -1, -1):
-        prio[i] = ops[i]["cost"] + ops[i]["lat"] + max([prio[k] + HOP for k in succ[i]] + [0.0])
-        if ops[i]["eng"] == "G" and ops[i]["part"]:
-            prio[i] += PAR["PUSH"][ops[i]["part"][0]][ops[i]["part"][1] // 8]
+    gap = [[(j, 0.0 if (ops[j]["eng"] == "P" and ops[i]["eng"] == "P") or i < 3 else ops[j]["lat"] + HOP) for j in pred[i]] for i in range(n)]
+    far = [{} for _ in ops]
     for i in range(n):
-        p = ops[i]["part"]
-        prio[i] += PAR["BIAS"][p[0]][p[1]] if p else -4000.0
-    for i in range(3):
-        prio[i] = 1e9 - i
-    total, order, extra, fin = arrange(ops, pred, succ, prio)
-    gap = [[(j, 0.0 if ops[j]["eng"] == "P" and ops[i]["eng"] == "P" else ops[j]["lat"] + HOP) for j in pred[i]] for i in range(n)]
-    for i in (1, 2):
-        gap[i].append((i - 1, 0.0))
+        for j, x in sorted(gap[i], reverse=True):
+            if far[i].get(j, -1.0) < x:
+                far[i][j] = x
+                for k, y in far[j].items():
+                    if k > i - 200 and far[i].get(k, -1.0) < x + y:
+                        far[i][k] = x + y
+            else:
+                gap[i].remove((j, x))
     back = [[] for _ in ops]
     for i in range(n):
         for j, x in gap[i]:
             back[j].append((i, x))
-    best = (total, [o["t"] for o in ops])
-    if PAR["FIFO"]:
-        turn = (0, 1, 1, 0, 0, 1, 0, 1, 1)
-        key = [PAR["FIFO"] * (2 * o["part"][0] + turn[o["part"][1]]) - prio[i] if o["part"] else -prio[i] for i, o in enumerate(ops)]
-        st = place(ops, gap, back, key, [0.0] * n)
-        best = (max(st[i] + ops[i]["cost"] + ops[i]["lat"] for i in range(n)), st)
-    rng = np.random.default_rng(PAR["SEED"])
-    for k in range(PAR["ROUNDS"]):
-        st = best[1]
-        noise = rng.normal(0.0, PAR["NOISE"] if k else 0.0, n)
-        late = place(ops, back, gap, [-(st[i] + ops[i]["cost"]) + noise[i] for i in range(n)], [o["lat"] for o in ops])
-        st = place(ops, gap, back, [-(late[i] + ops[i]["cost"]) for i in range(n)], [0.0] * n)
-        end = max(st[i] + ops[i]["cost"] + ops[i]["lat"] for i in range(n))
-        if end <= best[0]:
-            best = (end, st)
-    if PAR["MOVES"]:
-        best = polish(ops, gap, back, sorted(range(n), key=lambda i: (best[1][i], i)), rng)
-    if PAR["ROUNDS"]:
-        total = best[0]
-        order = sorted(range(n), key=lambda i: (best[1][i], i))
-        bank, extra = {}, [[] for _ in ops]
-        for i in order:
-            o = ops[i]
-            o["t"] = best[1][i]
-            fin[i] = o["t"] + o["cost"] + o["lat"]
-            for b in o["banks"]:
-                extra[i] += [j for e2, j in bank.get(b, {}).items() if e2 != o["eng"]]
-                bank.setdefault(b, {})[o["eng"]] = i
+    for i in (1, 2):
+        pred[i].clear()
+    total, start = search(ops, gap, back)
+    if PAR["POLISH"]:
+        keep = dict(PAR)
+        PAR.update(PAR["POLISH"])
+        total, start = polish(ops, gap, back, sorted(range(n), key=lambda i: (start[i], i)), np.random.default_rng(PAR["SEED"]))
+        PAR.update(keep)
+    fin = [0.0] * n
+    order = sorted(range(n), key=lambda i: (start[i], i))
+    bank, extra, fin = {}, [[] for _ in ops], [0.0] * n
+    for i in order:
+        o = ops[i]
+        o["t"] = start[i]
+        fin[i] = o["t"] + o["cost"] + o["lat"]
+        for b in o["banks"]:
+            extra[i] += [j for e2, j in bank.get(b, {}).items() if e2 != o["eng"]]
+            bank.setdefault(b, {})[o["eng"]] = i
     pos = {}
     seen = {e: {} for e in "VSPGY"}
     know = [None] * n
@@ -1084,6 +1116,8 @@ def plan():
         o["waits"] = waits
         kn = dict(seen[e])
         if o["sem"] is not None:
+            if o["sem"][1] == "far":
+                kn = {}
             kn[("d", i)] = 1
         else:
             kn[e] = max(kn.get(e, 0), pos[i])
@@ -1094,7 +1128,7 @@ def plan():
         if o["sem"] is None and i in need:
             tot[o["eng"]] += 1
             o["inc"] = tot[o["eng"]]
-    return ops, order, tot, total
+    return ops, order, total
 
 
 def resolver(T):
@@ -1103,6 +1137,9 @@ def resolver(T):
             return a
         if a[0] == "ind":
             return R(a[1]).indirect(R(a[2]))
+        if len(a) > 4:
+            lo, hi, step = a[4]
+            return T[a[0]][:, lo, :] if hi == lo + 1 else T[a[0]][:, lo:hi:step, :]
         if a[3] == 1:
             return T[a[0]][:, a[1]:a[2]]
         return T[a[0]][:, a[1]:a[2]:a[3]]
@@ -1118,7 +1155,7 @@ def rank_program(g, core, T, topo):
         return
     if "p" not in PLAN:
         PLAN["p"] = plan()
-    ops, order, tot, _ = PLAN["p"]
+    ops, order, _ = PLAN["p"]
     Q = {"V": g.vector, "S": g.scalar, "P": g.tensor, "G": g, "Y": g.sync}
     X = {"T": T, "topo": topo, "core": core, "rank": rank, "sent": [0]}
     nfar = len(topo.engines(core, T.cores[(rank + 1) % N]))

import math
import numpy as np
from concourse.bass import DstId, RemoteDMATransfer
from concourse.mybir import AluOpType as OP, ActivationFunctionType as AF

N, STEPS = 4, 4
CM = 1.5 * 2 ** 27
C1 = 1.5 * 2 ** 23
NEG = -131.0
SC, LAM = 1.75, 0.8125
GK, GB, C0 = 128.0, 2.0 ** 18, 24576.0

PAR = {
    "VSHARE": [[64, 48], [32, 32], [32, 32], [32, 32]],
    "UN": [[[[8, 0, 0], [8, 1, 0]], [[8, 2, 0], [8, 0, 0]]], [[[4, 0, 0]] * 4] * 2] + [[[[4, 1, 0], [4, 1, 0], [4, 0, 0], [4, 0, 0]], [[4, 1, 0], [4, 1, 0], [4, 0, 0], [4, 0, 1]]]] * 2,
    "WAY": [[None, None], ["bit", "bit"], ["bit", "bit"], ["bit", "bit"]],
    "SPEC": [[0, 0], [0, 0], [0, 0], [1, 1]],
    "EARLY": [[0, 0], [0, 0], [0, 0], [0, 1]],
    "HALF": [[0, 0], [1, 0], [1, 0], [1, 0]], "TB4": 1, "WG": 0, "FIRST": 0,
    "GP": [[[32] * 4] * 2] * 4, "GE": [["SVSV", "SVSS"], ["SVSS", "SSSS"], ["SVSS", "SSSS"], ["SVSS", "SSSS"]],
    "FREE": 0.5, "IDLE": 0.5, "SPAN": 6000.0, "BACK": 0.9, "SOFT": 0.1, "LEAN": 0.2, "CASES": [(1.3, 1.0, 1.0, 1.0, 0.0, 0.82), (0.95, 1.3, 1.0, 0.8, 2.0, 1.0)],
    "POLISH": None, "NB": 4, "NB1": 2, "B2": [["ps2", "ps3"], ["ps2", "ps3"]], "ONS": ["i15", "in15", "in2k", "i8k", "in1", "ih", "iq", "i2k", "cb", "igb", "inb", "i384", "in384"], "KMW": "G" * 16,
    "WIN": 50.0, "SEED": 1, "ROUNDS": 5500, "NOISE": 300.0, "TEMP": 250.0,
    "PUSH": [[4000, 4000], [4000, 0], [4000, 0], [2000, 0]],
    "BIAS": [[2000, 0, -1000, 0, 5000, -2000, 5000, 0, 3000], [0, 0, -3000, 0, 7000, 2000, 5000, 0, 5000],
             [500, 0, -3000, 0, 5000, 0, 5000, -1000, 5000], [0, 0, -3000, 3000, 5000, 0, 4500, 0, 0]],
}
SCALED = {"i1": 1.0, "in1": -1.0, "i15": 1.5, "in15": -1.5, "ih": 0.5, "iq": 0.25, "inq": -0.25, "in512": -512.0, "i512": 512.0,
          "i1k": 1024.0, "i1536": 1536.0, "i384": 384.0, "in384": -384.0, "in2k": -2048.0, "i2k": 2048.0, "ia": -1.625, "i768": 768.0, "in768": -768.0,
          "ib": 1.0 / 2048, "i10": 10.0, "ilam": LAM, "inls": -LAM * SC,
          "ck": -17 * GK, "ic0": C0, "cb": -17 * GB, "igb": GB, "inb": -192 * GB, "i8k": 8192.0}
BLOCK = {"bdn": -1.0, "bdbig": 2.0 ** 99, "bd10": 8192.0, "bd1k": 1024.0, "bdn1k": -1024.0, "bd40": 2.0 ** 40}
MATS = list(SCALED) + list(BLOCK) + ["iw", "bd", "bdp", "w1", "wok", "wargb", "wrot", "wpw", "tri", "one", "wgk", "wgb",
                                     "w16k", "wn16k"]
MOFF = {m: 128 * i for i, m in enumerate(MATS)}

SCRATCH = {
    "tab": ("sbuf", [128, 8192], "bfloat16"), "ivi": ("sbuf", [128, 1024], "int32"), "wl": ("sbuf", [128, 1024], "float32"),
    "e0i": ("sbuf", [128, 16], "int32"), "mats": ("sbuf", [128, 128 * len(MATS)], "bfloat16"),
    "zz": ("sbuf", [128, 3 * 144], "bfloat16"), "zh": ("sbuf", [128, 144], "float16"),
    "iot": ("sbuf", [128, 1032], "float32"), "tk": ("sbuf", [128, 1024], "bfloat16"), "tmpb": ("sbuf", [128, 80], "bfloat16"),
    "cols": ("sbuf", [128, 16], "float32"), "coli": ("sbuf", [128, 8], "int32"), "cf": ("sbuf", [128, 896], "float32"),
    "cb": ("sbuf", [128, 896], "bfloat16"), "ones": ("sbuf", [128, 256], "bfloat16"), "basel": ("sbuf", [128, 16], "bfloat16"), "lanel": ("sbuf", [128, 16], "float32"),
    "con": ("sbuf", [128, 80], "float32"), "thl": ("sbuf", [128, 96], "float32"), "kmw": ("sbuf", [128, 2048], "bfloat16"),
    "wkm": ("sbuf", [128, 2048], "bfloat16"), "wbit": ("sbuf", [128, 2048], "bfloat16"),
    "oyk": ("sbuf", [128, 256], "bfloat16"), "oy0": ("sbuf", [128, 256], "bfloat16"), "oy1": ("sbuf", [128, 256], "bfloat16"),
    "oye": ("sbuf", [128, 16], "float32"), "oya": ("sbuf", [128, 16], "float32"),
    "wf": ("sbuf", [128, 256 * 4], "float32"), "wi": ("sbuf", [128, 256 * 2], "int32"),
}
for _b in range(8):
    SCRATCH["ps%d" % _b] = ("psum", [128, 512], "float32")
for _k in range(3):
    SCRATCH["nc%d" % _k] = ("sbuf", [128, 512], "bfloat16")
    SCRATCH["ab%d" % _k] = ("sbuf", [128, 512], "bfloat16")
    SCRATCH["aa%d" % _k] = ("sbuf", [128, 512], "bfloat16")
for _c in range(2):
    SCRATCH["dd%d" % _c] = ("sbuf", [128, 512], "float32")
    SCRATCH["me%d" % _c] = ("sbuf", [128, 2048], "bfloat16")
    SCRATCH["c16_%d" % _c] = ("sbuf", [128, 128], "uint16")
    SCRATCH["u16_%d" % _c] = ("sbuf", [128, 64], "uint16")
    SCRATCH["si%d" % _c] = ("sbuf", [128, 128], "int32")
    SCRATCH["al%d" % _c] = ("sbuf", [128, 16], "bfloat16")
    SCRATCH["eh%d" % _c] = ("sbuf", [128, 4, 8], "float16")
    for _s in range(STEPS - 1):
        SCRATCH["win%d%d" % (_s, _c)] = ("sbuf", [128, 784], "bfloat16")
        SCRATCH["sb%d%d" % (_s, _c)] = ("sbuf", [128, 384], "bfloat16")
        SCRATCH["sl%d%d" % (_s, _c)] = ("sbuf", [128, 4, 4], "uint16")
for _c, _l in enumerate((128, 128, 256)):
    SCRATCH["yy%d" % _c] = ("sbuf", [128, 16 * _l + 16], "bfloat16")
    SCRATCH["l16_%d" % _c] = ("sbuf", [128, 5 * _l // 16], "uint16")
    SCRATCH["th%d" % _c] = ("sbuf", [128, _l // 8], "float16")
    SCRATCH["lf%d" % _c] = ("sbuf", [128, _l // 2], "float32")
    SCRATCH["lq%d" % _c] = ("sbuf", [128, _l // 4], "bfloat16")
    SCRATCH["rf%d" % _c] = ("sbuf", [128, _l * 3], "float32")
    SCRATCH["rb%d" % _c] = ("sbuf", [128, _l * 13], "bfloat16")
    SCRATCH["stk%d" % _c] = ("sbuf", [128, _l * 4], "bfloat16")
    SCRATCH["sh%d" % _c] = ("sbuf", [128, _l * 3], "float16")
SCRATCH["win32"] = ("sbuf", [128, 16 + 6 * 256], "bfloat16")
WINS = ["win%d%d" % (_s, _c) for _s in range(STEPS - 1) for _c in range(2)] + ["win32"]
for _s in range(STEPS):
    SCRATCH["el%d" % _s] = ("sbuf", [128, 8, 4], "uint16")

SEMAPHORES = (["qV", "qS", "qP", "qG", "sent", "ld0", "ld1", "ld2", "outs"]
              + ["ar%s%d%d" % (k, s, c) for k in "lr" for s in range(1, STEPS) for c in range(2)]
              + ["%s%d" % (w, k) for w in ("wkm", "wbit") for k in range(6)])

CY = 0.83 * 1.15
PECY = 0.42 * 1.15
FIX, HOP = 60.0, 160.0
GA, SCA = 1.6, 3.8


def A(name, lo, n, step=1):
    return (name, lo, lo + (n - 1) * step + 1, step)


def B(name, lo, n, step=1):
    w = SCRATCH[name][1][2]
    hi = lo + (n - 1) * step + 1
    return (name, lo * w, hi * w, 1, (lo, hi, step), n * w)


def sub(a, lo, n):
    return A(a[0], a[1] + lo * a[3], n, a[3])


def IND(win, off):
    return ("ind", win, off)


def cnt(a):
    if a[0] == "ind":
        return 16 * cnt(a[2])
    return a[5] if len(a) > 4 else (a[2] - a[1] - 1) // a[3] + 1


def two(a):
    return a[0] != "ind" and SCRATCH[a[0]][2] in ("bfloat16", "uint16", "float16")


def isps(a):
    return a[0] != "ind" and SCRATCH[a[0]][0] == "psum"


def flat(xs):
    out = []
    for a in xs:
        if isinstance(a, tuple):
            out += [a[1], a[2]] if a[0] == "ind" else [a]
    return out


def build():
    ops = []
    ways = set(w for x in PAR["WAY"] for w in x)
    used = set()

    def add(eng, call, outs, ins, cost, sem=None, lat=0.0):
        w = []
        r = flat(ins)
        for a in outs:
            if a[0] == "ind":
                w.append(a[1])
                r.append(a[2])
            else:
                w.append(a)
        ops.append({"eng": eng, "call": call, "w": w, "r": r, "cost": cost, "sem": sem, "lat": lat, "part": None,
                    "ind": cost - FIX if any(isinstance(a, tuple) and a[0] == "ind" for a in ins) else 0.0})

    def ecost(out, ins, base):
        n = cnt(ins[0]) if ins else cnt(out)
        if out[0] == "ind":
            return FIX + n * SCA * CY
        if ins and ins[0][0] == "ind":
            return FIX + n * GA * CY
        return FIX + max(n * base, 16) * CY

    def real(*xs):
        return all(SCRATCH[(x[1] if x[0] == "ind" else x)[0]][2] in ("float32", "bfloat16") for x in xs)

    def either(first=False):
        o = ops.pop()
        if o["eng"] == "S" and not first:
            ops[-1], o = o, ops[-1]
        ops[-1]["alt"] = (o["eng"], o["call"], o["cost"])

    def cp(out, a, alone=False):
        add("V", lambda q, R, X: q.tensor_copy(R(out), R(a)), [out], [a], ecost(out, [a], 0.5 if two(out) and two(a) else 1))
        if not alone and real(out, a) and out[0] != "ind":
            act(out, a, AF.Copy, alone=True)
            either()

    def ts(out, a, s1, o1, s2=None, o2=None, alone=False):
        def call(q, R, X):
            if o2 is None:
                return q.tensor_scalar(R(out), R(a), R(s1), None, o1)
            return q.tensor_scalar(R(out), R(a), R(s1), R(s2), o1, o2)
        add("V", call, [out], [a, s1, s2], ecost(out, [a], 0.5 if two(out) and two(a) else 1))
        if not alone and real(out, a) and (o1, o2) in ((OP.mult, None), (OP.add, None), (OP.mult, OP.add)):
            act(out, a, AF.Identity, bias=s1 if o1 == OP.add else s2, scale=s1 if o1 == OP.mult else 1.0, alone=True)
            either(cnt(out) > 128)

    def tt(out, a, b, o):
        add("V", lambda q, R, X: q.tensor_tensor(R(out), R(a), R(b), o), [out], [a, b],
            ecost(out, [a], 1 if isps(a) or isps(b) else 2))

    def ms(out, v):
        add("V", lambda q, R, X: q.memset(R(out), v), [out], [], ecost(out, [], 0.5 if two(out) else 1))

    def act(out, a, f, bias=None, scale=1.0, extra=0.0, alone=False):
        def call(q, R, X):
            if bias is None:
                return q.activation(R(out), R(a), f, scale=R(scale))
            return q.activation(R(out), R(a), f, bias=R(bias), scale=R(scale))
        add("S", call, [out], [a, bias, scale], ecost(out, [a], 1) + extra)
        if not alone and (f in (AF.Copy, AF.Identity) or (f == AF.Relu and bias is None)):
            if f == AF.Relu:
                ts(out, a, scale, OP.mult, 0.0, OP.max)
            elif bias is None:
                ts(out, a, scale, OP.mult, alone=True)
            else:
                ts(out, a, scale, OP.mult, bias, OP.add, alone=True)
            either()

    def mm(items, whole=None):
        def call(q, R, X):
            last = None
            for o, l, r, st, sp in items:
                last = q.matmul(R(o), R(l), R(r), bool(st), bool(sp))
            return last
        add("P", call, [x[0] for x in items] + ([whole] if whole else []), [x[1] for x in items] + [x[2] for x in items],
            20 + sum(max(64, cnt(x[2])) * PECY + 4 for x in items))

    def grp(out, terms, start=True, stop=True):
        return [(out, l, r, start and i == 0, stop and i == len(terms) - 1) for i, (l, r) in enumerate(terms)]

    def iota(out, pat, base, cm):
        def call(q, R, X):
            if SCRATCH[out[0]][2] == "int32":
                return q.iota(R(out), pat, base, cm)
            return q.iota(R(out), pat, base, cm, allow_small_or_imprecise_dtypes=True)
        add("G", call, [out], [], 130 + 2 * cnt(out) * CY)

    def M(name):
        used.add(name)
        return A("mats", MOFF[name], 128)

    def Z(t, k):
        return A("zh", 15 - k, 128) if t == "h" else A("zz", 144 * t + 15 - k, 128)

    def col(i):
        return A("cols", i, 1)

    def dma(out, a, sem, lat, after=()):
        add("Y", lambda q, R, X: q.dma_start(R(out), R(a)), [out], [a] + list(after), 60, sem=(sem, 16), lat=lat)

    WL, TAB = A("wl", 0, 1024), A("tab", 0, 8192)
    P, G16, IPW, K16, WP, KT, G, NW4, P1 = range(9)
    DD, NF, NN, FL = range(4)

    def setup():
        for name, buf, sem, lat in (("e0", A("e0i", 0, 16), "ld0", 2200), ("iv", A("ivi", 0, 1024), "ld1", 3500), ("st", TAB, "ld2", 8000)):
            add("Y", lambda q, R, X, name=name, buf=buf: q.dma_start(R(buf), X["T"][name][:]), [buf], [], 60, sem=(sem, 16), lat=lat)
        I1, BD, CK = A("mats", MOFF["i1"], 128), A("mats", MOFF["bd"], 128), A("cf", 128, 128)
        iota(A("coli", 0, 1), [[1, 1]], 0, 1)
        iota(A("iot", 0, 144), [[1, 144]], 0, 0)
        iota(A("iot", 144, 888), [[1, 888]], 144, 0)
        iota(A("cf", 0, 128), [[1, 8], [0, 16]], 0, 0)
        iota(CK, [[0, 8], [1, 16]], 0, 0)
        iota(A("ones", 0, 256), [[0, 256]], 1, 0)
        ZERO = A("cb", 768, 128)
        ms(ZERO, 0.0)

        def pick(out, a, op, fill):
            add("G", lambda q, R, X: q.affine_select(R(out), R(a), [[1, 128]], op, fill, 0, -1), [out], [a], 170 + 256 * CY)

        def scaled(out, v, eng):
            if eng == "G":
                pick(out, ZERO, OP.not_equal, v)
            elif eng == "S":
                act(out, I1, AF.Copy, scale=v)
            else:
                ts(out, I1, v, OP.mult)

        def upper(out, v, diag):
            ts(out, BD, v, OP.mult)
            pick(out, out, OP.is_gt, 0.0)
            if diag:
                pick(out, out, OP.not_equal, diag)
        scaled(I1, 1.0, "G")
        ts(A("coli", 1, 1), A("coli", 0, 1), 15, OP.bitwise_and)
        ts(A("coli", 2, 1), A("coli", 0, 1), 4, OP.arith_shift_right)
        cp(A("cols", P, 2, G - P), A("coli", 1, 2))
        ts(col(G16), col(G), 16.0, OP.mult, 15.0, OP.add)
        ts(col(K16), col(P), 16.0, OP.add)
        ts(col(WP), col(P), 64.0, OP.mult, 2048.0, OP.add)
        ts(col(NW4), col(WP), -4.0, OP.mult)
        ts(A("cf", 432, 16), A("cf", 128, 16), col(P), OP.is_equal)
        ts(BD, A("cf", 0, 128), col(G), OP.is_equal)
        for m, v in SCALED.items():
            if m != "i1" and m in used:
                scaled(M(m), float(v), "S" if m in PAR["ONS"] else "G")
        ts(M("iw"), I1, col(WP), OP.mult)
        for m, v in BLOCK.items():
            if m in used:
                ts(M(m), BD, v, OP.mult)
        ts(A("cb", 256, 128), CK, -1.0, OP.mult, -0.25, OP.add)
        tt(M("bdp"), A("cb", 256, 128), BD, OP.mult)
        for m, v in (("w1", 1.0), ("w16k", 16384.0), ("wn16k", -16384.0)):
            if m in used:
                upper(M(m), -v, v)
        for i, (m, we, wl, own) in enumerate((("wok", -2048.0, -32.0, 1024.0), ("wargb", 8.0, 1.0 / 128, -1.0))):
            if m in used:
                x, y = A("cb", 384 + 128 * i, 128), A("cb", 128, 128)
                upper(x, we, 0)
                ts(y, BD, wl, OP.mult)
                tt(M(m), x, y, OP.max if we > 0 else OP.min)
                pick(M(m), M(m), OP.not_equal, own)
        ts(A("zz", 144, 144), A("iot", 0, 144), col(G16), OP.is_equal)
        ts(A("zz", 288, 144), A("zz", 144, 144), col(K16), OP.mult)
        act(A("zz", 0, 144), A("zz", 144, 144), AF.Copy, scale=0.5)
        cp(A("zh", 0, 144), A("zz", 144, 144))
        ts(col(P1), col(P), 7.5, OP.is_lt, 8.0, OP.mult)
        iota(A("tmpb", 0, 64), [[4, 64]], 6, 0)
        for r in range(16):
            if r % 2:
                ts(A("tk", 64 * r, 64), A("tmpb", 0, 64), A("cf", 432 + r, 1), OP.mult)
            else:
                act(A("tk", 64 * r, 64), A("tmpb", 0, 64), AF.Copy, scale=A("cf", 432 + r, 1))
        ts(A("lanel", 0, 16), A("cf", 128, 16), 16.0, OP.mult, col(P), OP.add)
        U = A("lanel", 0, 8)
        ts(A("basel", 0, 16), A("lanel", 0, 16), 16.0, OP.mult, -16.0, OP.add)
        for o, m in ((0, 8), (32, 16)):
            ts(A("thl", o, m), A("lanel", 0, m), 16.0, OP.mult, -0.5, OP.add)
            iota(A("thl", o + m, 2 * m), [[0, 2 * m]], 1, 0)
            iota(A("thl", o + 3 * m, m), [[0, m]], 200000, 0)
        for c, o in enumerate((2048, 2048, 4096)):
            iota(A("yy%d" % c, o, 16), [[0, 16]], 0, 0)
        first = [1300.0]

        def power(out, a, scale, bias):
            act(out, a, AF.Exp, bias=bias * math.log(2.0), scale=scale * math.log(2.0), extra=first[0])
            first[0] = 0.0
        if "km" in ways:
            ms(A("thl", 40, 16), 0.5)
            ms(A("thl", 56, 8), 8000.0)
            ts(A("thl", 32, 8), U, -16.0, OP.mult, 16.5, OP.add)
            for k in range(16):
                scaled(A("kmw", 128 * k, 128), 4.0 ** (15 - k), PAR["KMW"][k])
            power(A("tmpb", 66, 1), col(P), -2.0, 30.0)
            ts(col(KT), A("tmpb", 66, 1), 0.9, OP.mult)
            x = A("cb", 256, 128)
            ts(x, CK, col(P), OP.is_ge, 2.0 ** 45 + 2.0 ** 40, OP.mult)
            ts(x, x, -2.0 ** 40, OP.add)
            tt(M("tri"), x, BD, OP.mult)
        if "bit" in ways:
            x, y, z = A("cf", 512, 128), A("cf", 640, 128), A("cf", 768, 128)
            ts(x, CK, -1.0, OP.mult, col(P), OP.add)
            ts(y, x, 0.5, OP.is_lt, 16.0, OP.mult)
            tt(z, x, y, OP.add)
            x, y = A("cb", 0, 128), A("cb", 256, 128)
            power(x, z, 1.0, -1.0)
            tt(M("wrot"), x, BD, OP.mult)
            power(y, z, -1.0, 0.0)
            tt(M("wpw"), y, BD, OP.mult)
        for way, m, g, src in (("km", "wgk", GK, BD), ("bit", "wgb", GB, A("mats", MOFF["wrot"], 128))):
            if way in ways:
                w = "w" + way
                ts(A(w, 0, 128), I1, g, OP.mult)
                tt(M(m), A(w, 0, 128), src, OP.add)
                for k in range(6):
                    n = 128 if k < 3 else 512
                    dma(A(w, n * (k % 3 + 1), n), A(w, 0, n), "%s%d" % (w, k), 2200 + n, [A("tab", 0, 1)])
                for k in range(16):
                    o, a = A(w, 128 * k + k, 8, 16), A("mats", MOFF[m] + k, 8, 16)
                    if k >= PAR["WG"]:
                        cp(o, a)
                        continue
                    add("G", lambda q, R, X, o=o, a=a: q.affine_select(R(o), R(a), [[0, 8]], OP.is_gt, 0.0, 1, 0), [o], [a], 170 + 16 * CY)
        for o, m, c0, w in ((0, 8, 17, 1), (8, 8, 16, 1), (16, 8, 16, 1), (24, 8, 402, 1),
                            (32, 16, 16, 1), (48, 16, 16 - 2048, 2048), (64, 16, 786, 1)):
            act(A("con", o, m), A("lanel", 0, m), AF.Identity, bias=c0 / w, scale=3.0 / w)
        cp(WL, A("ivi", 0, 1024))
        for w in WINS:
            iota(A(w, 0, 16), [[0, 16]], -126 if w == WINS[-1] else int(NEG), 0)
        for x in (A("win10", 401, 64, 3), A("sb00", 193, 64, 3), A("sb01", 1, 128, 3)):
            iota(x, [[0, cnt(x)]], int(NEG), 0)
        ms(B("el0", 1, 4, 2), 0)
        cp(B("el0", 0, 4, 2), A("e0i", 0, 16))

    ST2 = {
        0: [[("i1", DD)], [("in2k", DD)], [], [("i1", DD)]],
        1: [[("in2k", DD), ("i384", NN)], [("in2k", DD), ("i384", NF)], [("in384", DD)], [("i1", DD)]],
        2: [[("in2k", DD), ("i1", NF), ("i384", NN), ("in2k", FL)], [("in2k", DD), ("i384", NF), ("in2k", FL)],
            [("in384", DD), ("in2k", FL)], [("i1", DD), ("i1", FL)]],
    }
    ST2[3] = [[("in2k", DD), ("i1", NF), ("i768", NN), ("in2k", FL)], [("ia", NF), ("ib", NF), ("i1", NN), ("in1", FL)],
              [("in768", DD), ("in2k", FL)], ST2[2][3]]
    ring = {"b": 0, "c": 0, "a": 0, "e": 0, "d": 0}
    merged = [False]
    NB = PAR["NB"]
    RB, TB = "ps4", "ps5"
    TURN = col(15)

    def names(s, c):
        b, L = (2, 256) if s == STEPS - 1 else (c, 128)
        W = 256 if c == 2 else 128
        lo, g0, m = (128 * c if b == 2 and c < 2 else 0), 128 * (c % 2), W // 16
        w, rows = "win%d%d" % (s, b), 16 + 3 * L + 3 * lo
        u16, si, eh = "u16_%d" % (s % 2), "si%d" % (s % 2), "eh%d" % (s % 2)
        d = {"P0": A(w, rows, W, 3), "P1": A(w, rows + 1, W, 3), "K": A(w, rows + 2 if s else 17, W, 3), "z": A(w, 16 + 3 * lo, W, 3),
             "Kd": A(w, 18 + 3 * lo, W, 3), "cr": A(w, 17 + 3 * lo, W, 3), "win": A(w, 0, 16 + (6 if s else 3) * L),
             "c16": "c16_%d" % c, "Y": "yy%d" % b, "y0": 16 * lo, "YW": A("yy%d" % b, 0, 16 * L + 16), "me": "me%d" % c,
             "e16": A(u16, 16 + g0 // 16, m), "ed16": A(u16, g0 // 16, m), "d16": A(u16, 48 + g0 // 16, m), "e": A(si, 16 + g0 // 16, m),
             "de": A(si, 96 + g0 // 16, m), "A": A("al%d" % (s % 2), g0 // 16, m),
             "eh": B(eh, 0, 4) if c == 2 else B(eh, c, 2, 2), "ee": B(eh, 2, 2) if c == 2 else B(eh, 2 + c, 1),
             "old": A("wf", 256 + g0, W), "t": A("wf", 512 + g0, W), "t2": A("wf", 768 + g0, W), "v": A("wi", 256 + g0, W),
             "R": A(RB, g0, W), "one": A("ones", 0, W), "W": W, "b": b}
        for i, x in enumerate(["j16", "o0", "o1", "oK", "ja16"]):
            d[x] = A("l16_%d" % b, m * i, m)
        for buf, xs in (("rf", ["Rs", "r", "rb"]), ("stk", ["J", "f", "n0", "E"]), ("sh", ["ne", "s0", "s1"]),
                        ("rb", ["mid", "h", "okb", "X", "oh", "gb", "ohq", "cB", "zg", "ad", "thq", "oh1", "hi"])):
            for i, x in enumerate(xs):
                d[x] = A("%s%d" % (buf, b), L * i + lo, W)
        soon = PAR["EARLY"][s][c // 2 | c % 2]
        at = {"u": 0, "hh": 128, "w3": 0, "midc": 384, "u1": 0, "u1b": 384, "rg": 128, "rg2": 384, "cp": 384, "pw": 256, "bt": 128,
              "u2": 128, "m01": 384, "l1": 256, "q2": 288, "l0": 352, "v": 384 if soon else 128, "s01": 256, "cand": 0, "l2": 128}
        at = {x: ("ps%d" % (6 + c), o) for x, o in at.items()}
        if c == 2:
            at = {x: ("ps%d" % k, o) for x, k, o in (
                ("cp", 0, 0), ("u1", 1, 0), ("u1b", 1, 256), ("rg", 2, 0), ("rg2", 7, 256), ("pw", 3, 0), ("bt", 2, 256), ("u2", 3, 256),
                ("m01", 5, 0), ("l1", 6, 0), ("q2", 7, 0), ("l0", 1, 0), ("v", 5, 256), ("s01", 0, 0), ("cand", 2, 0), ("l2", 6, 128))}
        d["at"] = lambda x, n=W, o=0: A(at[x][0], at[x][1] + o, n)
        return d

    def early(s, c):
        d = names(s, c)
        for h in range(2):
            cp(A(d["c16"], 64 * h, 64), IND(WL, B("el%d" % s, 4 * c + 2 * h, 1)))
        lo = 0
        for n, e in zip(PAR["GP"][s][c], PAR["GE"][s][c]):
            o, i = A(d["Y"], d["y0"] + 16 * lo, 16 * n), IND(TAB, A(d["c16"], lo, n))
            if e == "V":
                ts(o, i, -125.0, OP.add)
            else:
                act(o, i, AF.Identity, bias=-125.0)
            lo += n

    def side(s, c):
        u16, si, a = "u16_%d" % (s % 2), "si%d" % (s % 2), A("al%d" % (s % 2), 0, 16)
        ed, e, ea, dd, dq, e5, de = [A(si, 16 * i, 16) for i in range(7)]
        cp(e, B("el%d" % s, 0, 4, 2))
        cp(a, B("el%d" % s, 1, 4, 2))
        ts(dq, B("el%d" % s, 0, 4, 2), 5.0, OP.mult, 1.0, OP.add)
        tt(e5, dq, a, OP.add)
        tt(ea, e, a, OP.add)
        ts(ed, e5, 1023, OP.bitwise_and)
        ts(dq, e, 768, OP.bitwise_and)
        tt(dd, dq, A("lanel", 0, 16), OP.add)
        cp(A(u16, 0, 64), A(si, 0, 64))
        if s:
            ts(B("eh%d" % (s % 2), 0, 4), A(si, 0, 32), 1024.0, OP.add)
        else:
            tt(de, ed, e, OP.subtract)
            for k in range(2):
                d = names(s, k)
                act(d["K"], IND(A("tk", 0, 1024), d["e16"]), AF.Identity, bias=NEG)
        x0, old, xi, v = A("wf", 0, 256), A("wf", 256, 256), A("wi", 0, 256), A("wi", 256, 256)
        act(x0, IND(WL, A(u16, 16, 16)), AF.Copy, scale=37.0)
        act(old, IND(WL, A(u16, 48, 16)), AF.Copy)
        tt(xi, IND(A("iot", 0, 1032), A(u16, 32, 16)), x0, OP.add)
        ts(v, xi, 8191, OP.bitwise_and)
        for k in range(2):
            d = names(s, k)
            act(d["Kd"], IND(A("tk", 0, 1024), d["ed16"]), AF.Identity, bias=NEG)

    def test(out, bank, how):
        if how:
            a2 = A("ab%d" % (ring["e"] % 3), 0, cnt(out))
            ring["e"] += 1
            act(a2, bank, AF.Abs)
            if how == 1:
                ts(out, a2, 7.9, OP.is_le)
            else:
                act(out, a2, AF.Sign, bias=7.9, scale=-1.0)
        else:
            ts(out, bank, CM, OP.add, CM, OP.is_equal)

    def bulk0(s, c):
        d = names(s, c)
        for h in range(2):
            for b in range(2):
                bank = "ps%d" % (ring["b"] % NB)
                ring["b"] += 1
                mm([(A(bank, 64 * j, 64), M("in15"), A(d["K"][0], 17 + 192 * h, 64, 3), j == 0, False) for j in range(8)])
                mm([(A(bank, 64 * j, 64), M("i15"), A(d["Y"], 1024 * h + 8 * b + j, 64, 16), False, j == 7) for j in range(8)])
                how = PAR["UN"][s][c][b][1]
                test(A(d["me"], 1024 * h + 512 * b, 512), A(bank, 0, 512), how)
                mm(grp(A(RB, d["R"][1] + 64 * h, 64),
                       [(Z(int(how < 2), 8 * b + j), A(d["me"], 1024 * h + 512 * b + 64 * j, 64)) for j in range(8)],
                       start=b == 0, stop=b == 1), TURN)

    def bulk(s, c):
        if s == 0:
            return bulk0(s, c)
        d = names(s, c)
        at = d["at"]
        units = PAR["UN"][s][c]
        km = PAR["WAY"][s][c] == "km"
        nl, used_me = 64 if PAR["HALF"][s][c] else 128, 0
        nk = 512 // nl

        def ahead(lo):
            cr, mid, thq, h, K, P0, P1 = [sub(d[x], lo, nl) for x in ("cr", "mid", "thq", "h", "K", "P0", "P1")]
            ts(cr, K, -128.0, OP.is_gt)
            half = [(M("i1"), P0)] if s == 1 else [(M("ih"), P0), (M("ih"), P1)]
            mm(grp(at("u", nl, lo), half + [(M("in2k"), cr)]))
            tt(mid, at("u", nl, lo), K, OP.max)
            if s > 1:
                act(thq, cr, AF.Identity, bias=1024.0, scale=10.0 - 1024.0)
                mm(grp(at("hh", nl, lo), [(M("i1"), P0), (M("in1"), P1)]))
                act(h, at("hh", nl, lo), AF.Abs, scale=0.5)
            nt = 4 if PAR["TB4"] else nk
            mm([(A(TB, 4 * lo * PAR["TB4"] + nl * j, nl), M("i1" if s > 1 else "i8k"), thq if s > 1 else cr, j == 0, j == nt - 1) for j in range(nt)])
            terms = [(M("ck"), cr), (M("bdn"), cr), (M("ic0"), sub(M("one"), 0, nl))] if km else [(M("cb"), cr)]
            mm(grp(sub(d["R"], lo, nl), terms, start=lo == 0, stop=False), TURN)
        for u in range(4):
            how, byv = units[u][1:]
            lo, k0 = (64 * (u // 2), 8 * (u % 2)) if nl == 64 else (0, 4 * u)
            w, end = 512, u == 3
            if k0 == 0:
                ahead(lo)
                if any(x[2] for x in units[u:u + nk // 4 * 2] + (units if nl == 128 else [])):
                    mm([(at("midc", nl, lo), M("i1"), sub(d["mid"], lo, nl), True, True)])
            if u == 2:
                act(d["n0"], d["P0"], AF.Relu, bias=-130.0, scale=-1.0)
                if s > 1:
                    mm(grp(at("w3"), [(M("bd"), d["h"])]))
                    act(d["ad"], at("w3"), AF.Sign, bias=0.5, scale=-1.0)
            ys = [A(d["Y"], d["y0"] + 16 * lo + k0 + j, nl, 16) for j in range(nk)]
            if byv:
                bank = "dd%d" % (ring["d"] % 2)
                ring["d"] += 1
                for j in range(nk):
                    tt(A(bank, nl * j, nl), ys[j], at("midc", nl, lo), OP.subtract)
            else:
                bank = "ps%d" % (ring["b"] % PAR["NB1"])
                ring["b"] += 1
                mm([(A(bank, nl * j, nl), M("in1"), sub(d["mid"], lo, nl), j == 0, False) for j in range(nk)])
                mm([(A(bank, nl * j, nl), M("i1"), ys[j], False, j == nk - 1) for j in range(nk)])
            me = A(d["me"], used_me, w)
            used_me += w
            a, n = A("aa%d" % (ring["a"] % 3), 0, w), A("nc%d" % (ring["a"] % 3), 0, w)
            ring["a"] += 1
            second = PAR["B2"][s > 1]
            x = A(second[ring["c"] % len(second)], 0, w)
            ring["c"] += 1
            act(a, A(bank, 0, w), AF.Abs, scale=SC if s > 1 else 8192.0 / 5.5)
            wt = 4 * nl if PAR["TB4"] else w
            for o in range(0, w, wt):
                tt(sub(n, o, wt), sub(a, o, wt), A(TB, 4 * lo * PAR["TB4"], wt), OP.is_lt if s == 1 else OP.is_ge)
            if s == 1:
                mm([(x, M("bd10"), n, True, True)])
                tt(me, a, x, OP.is_lt)
            else:
                mm([(A(x[0], nl * j, nl), M("inls"), sub(d["h"], lo, nl), j == 0, False) for j in range(nk)])
                mm([(x, M("ilam"), a, False, False)])
                mm([(x, M("bd1k"), n, False, True)])
                test(me, x, how)
            mes = [sub(me, nl * j, nl) for j in range(nk)]
            terms = [(A("wkm" if km else "wbit", 128 * (k0 + j), 128), mes[j]) for j in range(nk)]
            items = grp(sub(d["R"], lo, nl), terms, start=False, stop=end and not km)
            if km:
                items += grp(sub(d["km"], lo, nl), [(A("kmw", 128 * (k0 + j), 128), m) for j, m in enumerate(mes)], start=False, stop=end)
            mm(items, TURN)

    def join(s, c):
        d = names(s, c)
        at = d["at"]
        if s == 0:
            act(d["okb"], d["R"], AF.Identity, bias=col(P1) if PAR["UN"][s][c][0][1] == 2 else None)
        else:
            act(d["X"], d["R"], AF.Exp, bias=-8 * math.log(1024.0), scale=math.log(1024.0) / GB)
            act(d["hi"], d["R"], AF.Identity, bias=191.875, scale=1.0 / GB)
            act(d["Rs"], d["R"], AF.Identity, bias=0.5)
            late([(at("cp"), M(w), d[x]) for w, x in (("inb", "one"), ("igb", "hi"), ("wrot", "cr"), ("ih", "one"))], 3, c == 2)
            tt(d["okb"], at("cp"), d["Rs"], OP.is_equal)
        late([(at("u1"), M("w16k"), d["okb"])], 1, False)
        act(d["f"], at("u1"), AF.Relu, scale=1.0 / 16384)
        late([(at("u1b"), M("i8k"), d["one"]), (at("u1b"), M("wn16k"), d["okb"])], 2, False)
        tt(d["t"], at("u1"), d["v"], OP.min)
        tt(d["t2"], at("u1b"), d["old"], OP.min)
        tt(IND(WL, d["d16"]), d["t"], d["t2"], OP.max)

    def late(items, n, apart):
        items = [(o, l, r, i == 0, i == len(items) - 1) for i, (o, l, r) in enumerate(items)]
        turn = A("coli", int(items[0][0][0][2:]) + 8, 1) if merged[0] else None
        if apart and n < len(items):
            mm(items[:-n], turn)
            items = items[-n:]
        mm(items, turn)

    def tolist(out, zt, src, n, extra, apart=False):
        items = [(A(out[0], out[1], cnt(x)), m, x) for x, m in extra]
        rows = [(out, Z(zt, r), A(src[0], src[1] + r, n, 16)) for r in range(16)]
        if apart:
            late([(out, A("cb", 768, 128), A("ones", 0, n))] + items + rows, 16, True)
        else:
            late(rows[:1] + items + rows[1:], 16, False)

    def tail(s, c):
        d = names(s, c)
        at = d["at"]
        last = s == STEPS - 1
        W, spec = d["W"], PAR["SPEC"][s][min(c, 1)]
        m = W // 16
        soon = s > 1 and PAR["EARLY"][s][min(c, 1)]
        J = d["J"] if s else d["f"]
        if s > 0:
            warg, low = M("wargb"), -2.0 ** -75
            oh = d["oh"]
            if spec:
                oh = d["oh1"]
                late([(at("rg"), warg, d["X"])], 1, False)
                ts(oh, at("rg"), low, OP.is_lt)
                late([(at("rg2"), M("i1"), oh), (at("rg2"), M("bdn"), d["okb"])], 2, False)
                act(d["oh"], at("rg2"), AF.Relu)
            else:
                late([(at("rg"), warg, d["X"]), (at("rg"), M("bdbig"), d["okb"])], 1, last)
                ts(oh, at("rg"), low, OP.is_lt)
            late([(at("pw"), M("wpw"), oh)], 1, False)
            tt(at("bt"), at("pw"), d["Rs"], OP.mult)
            ts(d["rb"], at("bt"), C1, OP.add, C1, OP.subtract)
            tt(d["gb"], at("bt"), d["rb"], OP.is_lt)
            if spec:
                late([(at("u2"), M("wok"), d["okb"]), (at("u2"), M("w1"), d["gb"])], 1, last)
                ts(J, at("u2"), 0.5, OP.is_gt)
            else:
                late([(at("u2"), M("i1"), d["f"]), (at("u2"), M("w1"), d["gb"])], 1, last)
                act(J, at("u2"), AF.Relu)
        YW = d["YW"]
        base = (A("basel", 0, m), M("i1"))
        zg = zf = d["z"]
        if s > 1:
            late([(at("m01"), M(w), d[x]) for w, x in (("ih", "P0"), ("ih", "P1"), ("in1", "h"), ("i512", "ad"), ("bdn1k", "f"))], 1, last)
            act(d["E"], at("m01"), AF.Identity, bias=1536.0)
        if soon:
            tolist(at("l0", m), 2, d["f"], m, [base])
            cp(d["ja16"], at("l0", m))
            zf = d["zg"]
            tt(zf, IND(YW, d["ja16"]), d["E"], OP.min)
        nq = m * (1, 3, 4, 4)[s]
        l1 = at("l1", nq)
        tolist(l1, 2, J, nq, [base])
        cp(d["j16"], at("l1", m))
        if s > 1:
            tt(zg, IND(YW, d["j16"]), d["E"], OP.min)
        else:
            act(zg, IND(YW, d["j16"]), AF.Copy)
        lq, lf, th = "lq%d" % c, "lf%d" % c, "th%d" % c
        sl, sb = "sl%d%d" % (s, c), "sb%d%d" % (s, c)
        pieces = [(0, W)] if c else [(0, 64), (64, 64)]

        def lists(out, row, lo, n):
            if last:
                return A(out, 0, m)
            return B("el%d" % (s + 1), row, 1) if (c, lo) == (0, 0) else B(sl, lo // 32 + row, n // 64, 2)
        tt(A(lq, 0, nq), l1, A("thl", 32 * last, nq), OP.is_lt)
        if s == 0:
            tt(A(lf, 24, 8), A(lq, 8 * DD, 8), d["de"], OP.mult)
            tt(A(lf, 32, 8), A(lf, 24, 8), d["e"], OP.add)
            for lo, n in pieces:
                cp(lists("oye", 0, lo, n), A(lf, 32 + lo // 16, n // 16))
        items = []
        for i, terms in enumerate(ST2[s]):
            items += grp(at("q2", m, m * i), [(M(w), A(lq, m * x, m)) for w, x in terms] + ([(M("i1"), d["A"])] if i == 3 else []))
        if s:
            items.append((at("q2", 2 * m, 4 * m), M("i2k"), A(lq, 0, 2 * m), True, s == 1))
            if s > 1:
                items.append((at("q2", m, 5 * m), M("i2k"), A(lq, m * FL, m), False, True))
        mm(items)
        no = 3 * m if s else 2 * m
        tt(A(lf, 0, no), at("q2", no), A("con", (0, 8, 8, 32)[s], no), OP.add)
        for lo, n in pieces:
            cp(lists("oya", 1, lo, n), at("q2", n // 16, 3 * m + lo // 16))
        if s:
            tt(A(th, 0, 2 * m), at("q2", 2 * m, 4 * m), d["eh"], OP.min)
        if s > 1:
            late([(at("v"), M("inq"), d["ad"]), (at("v"), M("bdp"), d["f"]), (at("v"), M("bd"), zf)], 1, last)
            ts(d["r"], at("v"), CM, OP.add, CM, OP.subtract)
            tt(d["ohq"], at("v"), d["r"], OP.is_equal)
            items = []
            for i, p in enumerate(("P0", "P1")):
                more = [(M("i512"), d["ad"]), (M("i1536"), d["oh"])] if last and i else [(M("i1k"), d["oh"])]
                items += [(at("s01", W, W * i), l, r) for l, r in [(M("i15"), d[p])] + more]
            late(items + [(at("s01", W, W * i), M("in15"), zg) for i in range(2)], 2, last)
            ts(A(d["s0"][0], d["s0"][1], 2 * W), at("s01", 2 * W), CM - 1024, OP.add, CM, OP.is_equal)
        if s > 0:
            more = [(M("iq"), zg)] + ([(M("iw"), d["ohq"])] if s > 1 else [])
            late([(at("cand"), l, r) for l, r in [(M("iw"), d["oh"])] + more[::-1 if soon else 1]], 1, last)
            ts(d["ne"], at("cand"), 30.875 - 1024, OP.add, 0.0, OP.max)
            act(d["cB"], at("cand"), AF.Identity, bias=col(NW4), scale=4.0)
            n2 = m if s == 1 else 3 * m
            tolist(at("l2", n2), "h", d["ne"], n2, [(d["ee"], M("i1")), (A(th, 0, m), M("i1")), (A(th, m, m), M("in1"))], last)
            for lo, n in pieces:
                ts(lists("oye", 0, lo, n), at("l2", n // 16, lo // 16), -1024.0, OP.add, 0.0, OP.max)
        if not last:
            send(s, c, "l", lambda h: B(sl, 2 * h, 2), lambda h: B("el%d" % (s + 1), 4 * c + 2 * h, 2))
        if last:
            cp(d["oK"], A(lf, 2 * m, m))
            tt(A(lf, 3 * m, m), A(lf, m, m), at("l2", m, m), OP.add)
            tt(A(lf, 0, m), A(lf, 0, m), at("l2", m, m), OP.subtract)
            tt(A(lf, m, m), A(lf, 3 * m, m), at("l2", m, 2 * m), OP.add)
            cp(d["o0"], A(lf, 0, m))
            ts(d["o1"], A(lf, m, m), 2048.0, OP.mult)
            act(A("oy0", 0, W), IND(d["win"], d["o0"]), AF.Identity, bias=125.0)
            act(A("oy1", 0, W), IND(d["win"], d["o1"]), AF.Identity, bias=125.0)
            tt(d["X"], IND(d["win"], d["oK"]), d["cB"], OP.max)
            ts(A("oyk", 0, W), d["X"], 125.0, OP.add, -1.0, OP.max)
            return
        if s > 1:
            tt(A(lf, 0, 8), A(lf, 0, 8), at("l2", 8, 8), OP.subtract)
            tt(A(lf, 8, 8), A(lf, 8, 8), at("l2", 8, 16), OP.add)
        cp(A("l16_%d" % c, 8, no), A(lf, 0, no))
        nxt = names(s + 1, c)["P0"]
        for lo, n in pieces:
            buf, o = nxt[:2] if (c, lo) == (0, 0) else (sb, 3 * lo)
            o0, o1, oK = [IND(d["win"], sub(d[x], lo // 16, n // 16)) for x in ("o0", "o1", "oK")]
            if s == 0:
                act(A(buf, o, n, 3), o1, AF.Copy)
                cp(A(buf, o + 2, n, 3), o0)
            else:
                act(A(buf, o, n, 3), o0, AF.Copy)
                act(A(buf, o + 1, n, 3), o1, AF.Copy)
                tt(A(buf, o + 2, n, 3), oK, sub(d["cB"], lo, n), OP.max)
        send(s, c, "r", lambda h: A(sb, 192 * h, 192), lambda h: A(nxt[0], nxt[1] + 192 * h, 192))

    def send(s, c, kind, src, dst):
        blocks = [(h, 2 * c + h) for h in range(2)]
        far = [(h, b) for h, b in blocks if b % N]
        name = "ar%s%d%d" % (kind, s + 1, c)

        def call(q, R, X):
            topo, T, core = X["topo"], X["T"], X["core"]
            trs = []
            for i, (h, b) in enumerate(far):
                to = T.cores[(X["rank"] + b) % N]
                eng = topo.engines(core, to)
                k = len(eng) // len(far)
                mask = sum(1 << e for e in eng[i * k:(i + 1) * k])
                ad = topo.addr(to)
                trs.append(RemoteDMATransfer(dst_ids=[DstId(rid=ad[0], pnc=ad[1])], dma_engine_mask=mask, remote_sem=T.sem[name],
                                             src=R(src(h)), dst=R(dst(h))))
                X["sent"][0] += k
            return q.remote_dma_fused(trs, local_sem=T.sem["sent"])
        add("G", call, [dst(h) for h, b in far], [src(h) for h, b in far], 700, sem=(name, "far"), lat=1700 + 600 * len(far) + PAR["FIRST"] * ((s, c, kind) == (0, 0, "l")))

    for s in range(STEPS):
        for k, (part, c) in enumerate(((early, 0), (early, 1), (side, 0), (bulk, 0), (join, 0), (bulk, 1), (tail, 0), (join, 1), (tail, 1))):
            first = len(ops)
            if s < STEPS - 1 or part not in (join, tail):
                part(s, c)
            elif c:
                merged[0] = True
                part(s, 2)
            for o in ops[first:]:
                o["part"] = (s, k)
    for name, buf, n in (("yi", "wl", 1024), ("ye", "oye", 16), ("ya", "oya", 16), ("y0", "oy0", 256), ("yk", "oyk", 256), ("y1", "oy1", 256)):
        add("Y", lambda q, R, X, name=name, buf=buf, n=n: q.dma_start(X["T"][name][:], R(A(buf, 0, n))), [], [A(buf, 0, n)], 60,
            sem=("outs", 16), lat=2300 + 2 * n)
    body = ops[:]
    del ops[:]
    setup()
    return ops + body


def links(ops):
    acc = {}
    pred = [set() for _ in ops]
    for i, o in enumerate(ops):
        for kind, lst in (("r", o["r"]), ("w", o["w"])):
            for a in lst:
                for (j, k2, lo, hi, stp) in acc.get(a[0], ()):
                    if j != i and (kind == "w" or k2 == "w") and lo < a[2] and a[1] < hi:
                        if stp == 1 or stp != a[3] or (lo - a[1]) % stp == 0:
                            pred[i].add(j)
        for kind, lst in (("r", o["r"]), ("w", o["w"])):
            for a in lst:
                old = acc.get(a[0], [])
                if kind == "w" and a[3] == 1 and (len(a) == 4 or a[4][2] == 1):
                    old = [x for x in old if not (a[1] <= x[2] and x[3] <= a[2])]
                acc[a[0]] = old + [(i, kind, a[1], a[2], a[3])]
        o["banks"] = sorted(set(a[0] for a in o["r"] + o["w"] if isps(a)))
    return pred


def arrange(ops, pred, succ, prio):
    n = len(ops)
    eng = [o["eng"] for o in ops]
    left = [len(p) for p in pred]
    dep = [0.0] * n
    ready = {e: [] for e in "VSPGY"}
    for i in range(n):
        if left[i] == 0:
            ready[eng[i]].append(i)
    free = {e: 0.0 for e in "VSPGY"}
    fin = [0.0] * n
    start = [0.0] * n
    bank, done = {}, 0
    while done < n:
        best = None
        for e in "VSPGY":
            st = []
            for i in ready[e]:
                t = max(free[e], dep[i])
                for b in ops[i]["banks"]:
                    for e2, j in bank.get(b, {}).items():
                        if e2 != e:
                            t = max(t, fin[j] + HOP)
                st.append((t, i))
            if st:
                t0 = min(st)[0]
                if best is None or t0 < best[0]:
                    best = (t0, st)
        t, i = max((x for x in best[1] if x[0] <= best[0] + PAR["WIN"]), key=lambda x: (prio[x[1]], -x[1]))
        o, e = ops[i], eng[i]
        start[i] = t
        free[e] = t + o["cost"]
        fin[i] = t + o["cost"] + o["lat"]
        for b in o["banks"]:
            bank.setdefault(b, {})[e] = i
        done += 1
        ready[e].remove(i)
        for k in succ[i]:
            dep[k] = max(dep[k], start[i] if e == "P" and eng[k] == "P" else fin[i] + HOP)
            left[k] -= 1
            if left[k] == 0:
                ready[eng[k]].append(k)
    return start


def polish(ops, gap, back, order, rng):
    n = len(ops)
    eng = ["VSPGY".index(o["eng"]) for o in ops]
    cost = [o["cost"] for o in ops]
    banks = [[int(b[2:]) for b in o["banks"]] for o in ops]
    other = ((1, 2), (0, 2), (0, 1))

    def run(part, fin, why, last, used):
        for i in part:
            e = eng[i]
            t, w = 0.0, -1
            for j, x in gap[i]:
                if fin[j] + x > t:
                    t, w = fin[j] + x, j
            j = last[e]
            if fin[j] > t:
                t, w = fin[j], j + n
            for b in banks[i]:
                for e2 in other[e]:
                    j = used[3 * b + e2]
                    if fin[j] + HOP > t:
                        t, w = fin[j] + HOP, j + n
                used[3 * b + e] = i
            fin[i], why[i], last[e] = t + cost[i], w, i

    def whole(order):
        fin = [0.0] * n + [-1e9]
        run(order, fin, [-1] * n, [n] * 5, [n] * 24)
        return max(fin[i] + ops[i]["lat"] for i in range(n)), fin
    best = whole(order)
    sweeps, span = PAR["SWEEPS"], PAR["SPAN"]
    for sweep in range(sweeps):
        temp = PAR["TEMP"] * (1.0 - sweep / sweeps) ** 2
        for lo in range(int(rng.integers(-span // 2, 1)), n - 20, span // 2):
            a0, hi = max(lo, 0), min(n, lo + span)
            fin0, last0, used0 = [0.0] * n + [-1e9], [n] * 5, [n] * 24
            run(order[:a0], fin0, [-1] * n, last0, used0)
            rest, nxt, nb = [0.0] * n + [-1e9], [n] * 5, [n] * 24
            for i in order[:hi - 1:-1] if hi < n else ():
                e = eng[i]
                r = max([ops[i]["lat"], rest[nxt[e]]] + [x + rest[k] for k, x in back[i]])
                for b in banks[i]:
                    r = max(r, HOP + rest[nb[3 * b + other[e][0]]], HOP + rest[nb[3 * b + other[e][1]]])
                    nb[3 * b + e] = i
                rest[i], nxt[e] = r + cost[i], i
            part = order[a0:hi]
            inside = set(part)
            outs = [(i, max([ops[i]["lat"]] + [x + rest[k] for k, x in back[i] if k not in inside])) for i in part]
            top = max(x for _, x in outs)
            outs = [y for y in outs if y[1] > top - 15000.0]
            qe = [rest[nxt[e]] for e in range(5)]
            qb = [HOP + max(rest[nb[3 * (k // 3) + e2]] for e2 in other[k % 3]) for k in range(24)]

            def score(part):
                fin, why, last, used = fin0[:], [-1] * n, last0[:], used0[:]
                run(part, fin, why, last, used)
                ts = [(fin[i] + x, i) for i, x in outs] + [(fin[last[e]] + qe[e], last[e]) for e in range(5)]
                ts += [(fin[used[k]] + qb[k], used[k]) for k in range(24) if qb[k] > 0]
                ts.sort(reverse=True)
                ts = ts[:8]
                return ts[0][0] + PAR["SOFT"] * sum(t for t, _ in ts) / len(ts), fin, why, ts
            now = score(part)
            for _ in range(PAR["MOVES"]):
                i = now[3][int(rng.integers(len(now[3]))) if rng.random() < 0.5 else 0][1]
                pairs = []
                while i in inside:
                    w = now[2][i]
                    if w >= n:
                        w -= n
                        if w in inside:
                            pairs.append((w, i))
                    i = w
                if not pairs:
                    continue
                j, i = pairs[int(rng.integers(len(pairs)))]
                a, b = part.index(j), part.index(i)
                mid = part[a:b + 1]
                keep = rng.random() < PAR["KEEP"]
                early = rng.random() < 0.5
                go, held = {i if early else j}, set() if eng[i] == eng[j] else {eng[i if early else j]}
                for y in mid[-2::-1] if early else mid[1:]:
                    if (keep and eng[y] in held) or any(z in go for z, _ in (back if early else gap)[y]):
                        go.add(y)
                        held.add(eng[y])
                if i in go and j in go:
                    continue
                new = part[:a] + [x for x in mid if (x in go) == early] + [x for x in mid if (x in go) != early] + part[b + 1:]
                got = score(new)
                if got[0] <= now[0] + temp * rng.exponential():
                    now, part = got, sorted(new, key=lambda x: got[1][x] - cost[x])
            order = order[:a0] + part + order[hi:]
        got = whole(order)
        order = sorted(order, key=lambda x: got[1][x] - cost[x])
        if got[0] < best[0]:
            best = got
    return best[0], [best[1][i] - cost[i] for i in range(n)]


def listed(eng, cost, banks, gap, back, least, prio):
    n, win = len(eng), PAR["WIN"]
    left = [len(x) for x in gap]
    dep = list(least)
    ready = [[] for _ in range(5)]
    for i in range(n):
        if not left[i]:
            ready[eng[i]].append(i)
    free = [0.0] * 5
    st = [0.0] * n
    bk = [[0.0] * 8 for _ in range(3)]
    first, times, stale = [1e18] * 5, [None] * 5, {0, 1, 2, 3, 4}
    for _ in range(n):
        for e in stale:
            f, l = free[e], []
            for i in ready[e]:
                t = dep[i]
                for b in banks[i]:
                    if bk[e][b] > t:
                        t = bk[e][b]
                l.append(t if t > f else f)
            first[e], times[e] = min(l) if l else 1e18, l
        t0 = min(first)
        e = first.index(t0)
        l, r = times[e], ready[e]
        bi = 0
        if len(r) > 1:
            t0, bp = t0 + win, -1e18
            for x in range(len(r)):
                if l[x] <= t0 and prio[r[x]] > bp:
                    bi, bp = x, prio[r[x]]
        i = r.pop(bi)
        st[i] = l[bi]
        z = free[e] = l[bi] + cost[i]
        stale = {e}
        if banks[i]:
            stale = {0, 1, 2}
            for b in banks[i]:
                bk[e - 1][b] = bk[e - 2][b] = z + HOP
        for k, x in back[i]:
            if z + x > dep[k]:
                dep[k] = z + x
            left[k] -= 1
            if not left[k]:
                ready[eng[k]].append(k)
                stale.add(eng[k])
    return st


def replay(order, eng, cost, banks, gap, lat, fc, fl):
    fin, free, end = [0.0] * len(eng), [0.0] * 5, 0.0
    bk = [[0.0] * 3 for _ in range(8)]
    for i in order:
        e = eng[i]
        t = free[e]
        for j, x in gap[i]:
            if fin[j] + x > t:
                t = fin[j] + x
        for b in banks[i]:
            if bk[b][e] > t:
                t = bk[b][e]
        t += cost[i] * fc[i]
        fin[i] = free[e] = t
        for b in banks[i]:
            bk[b][e - 1] = bk[b][e - 2] = t + HOP * fl
        if t + lat[i] > end:
            end = t + lat[i]
    return end


def case(ops, gap, fc, fl, fr, fg, ff=0.0):
    far = [bool(o["sem"]) and o["sem"][1] == "far" for o in ops]
    return ([[(j, ops[j]["lat"] * (fr if far[j] else 1.0) + HOP * fl if x else 0.0) for j, x in g] for g in gap], [fr + ff * (o["part"][0] == 0) if x else fc * (1.0 + (fg - 1.0) * o["ind"] / o["cost"]) for x, o in zip(far, ops)], fl)


def search(ops, gap, back):
    n = len(ops)
    eng = ["VSPGY".index(o["eng"]) for o in ops]
    cost, lat = [o["cost"] for o in ops], [o["lat"] for o in ops]
    banks = [[int(b[2:]) for b in o["banks"]] for o in ops]
    rng = np.random.default_rng(PAR["SEED"])
    prio = [0.0] * n
    for i in range(n - 1, -1, -1):
        prio[i] = cost[i] + max([prio[k] + x for k, x in back[i]] + [lat[i]])
    both = [i for i in range(n) if "alt" in ops[i]]
    marks = [i for i in range(n) if ops[i]["part"] and eng[i] == 3]
    cases = [(case(ops, gap, *x[:5]), x[5]) for x in PAR["CASES"]]
    now = best = (1e18, None, eng, cost, 1e18)
    for it in range(PAR["ROUNDS"]):
        eng, cost = now[2][:], now[3][:]
        if it:
            st = np.array(now[1])
            near = np.abs(st - rng.random() * now[0]) < PAR["SPAN"]
            z = rng.normal(0.0, PAR["NOISE"], n) * near * rng.random()
            some = [i for i in both if near[i]]
            if rng.random() < PAR["IDLE"]:
                on = np.array(sorted((now[1][i], now[1][i] + cost[i]) for i in range(n) if eng[i] == 1) + [(1e9, 1e9)])
                some = [i for i in some if eng[i] == 0 and on[np.searchsorted(on[:, 1], st[i] + 50.0), 0] > st[i] + 0.7 * cost[i]]
            while some and rng.random() < PAR["FREE"]:
                i = some[int(rng.integers(len(some)))]
                eng[i] = 1 - eng[i]
                cost[i] = ops[i]["cost"] if "VS"[eng[i]] == ops[i]["eng"] else ops[i]["alt"][2]
            if rng.random() < PAR["BACK"]:
                late = listed(eng, cost, banks, back, gap, lat, (st + cost + z).tolist())
                prio = [late[i] + cost[i] for i in range(n)]
            else:
                prio = (z - st).tolist()
        st = listed(eng, cost, banks, gap, back, [0.0] * n, prio)
        end = max(st[i] + cost[i] + lat[i] for i in range(n))
        end += PAR["SOFT"] * (sum(st[i] for i in marks) / len(marks) - end / 2) + PAR["LEAN"] * sum(cost[i] for i in both if not eng[i])
        plain = end
        if end >= now[4] + 1500.0:
            continue
        if PAR["CASES"] and end < now[4] + 1500.0:
            order = sorted(range(n), key=lambda i: st[i])
            end = (end + sum(w * replay(order, eng, cost, banks, g, lat, fc, fl) for (g, fc, fl), w in cases)) / (1 + len(cases))
        if end <= now[0] + PAR["TEMP"] * (1.0 - it / PAR["ROUNDS"]) * rng.exponential():
            now = (end, st, eng, cost, plain)
            if end < best[0]:
                best = now
    for i in both:
        if "VS"[best[2][i]] != ops[i]["eng"]:
            ops[i]["eng"], ops[i]["call"], ops[i]["cost"] = ops[i]["alt"]
    return max(best[1][i] + best[3][i] + lat[i] for i in range(n)), best[1]


def plan():
    ops = build()
    n = len(ops)
    pred = links(ops)
    for i in (1, 2):
        pred[i].add(i - 1)
    succ = [[] for _ in ops]
    for i in range(n):
        for j in pred[i]:
            succ[j].append(i)
    gap = [[(j, 0.0 if (ops[j]["eng"] == "P" and ops[i]["eng"] == "P") or i < 3 else ops[j]["lat"] + HOP) for j in pred[i]] for i in range(n)]
    far = [{} for _ in ops]
    for i in range(n):
        for j, x in sorted(gap[i], reverse=True):
            if far[i].get(j, -1.0) < x:
                far[i][j] = x
                for k, y in far[j].items():
                    if k > i - 200 and far[i].get(k, -1.0) < x + y:
                        far[i][k] = x + y
            else:
                gap[i].remove((j, x))
    back = [[] for _ in ops]
    for i in range(n):
        for j, x in gap[i]:
            back[j].append((i, x))
    for i in (1, 2):
        pred[i].clear()
    total, start = search(ops, gap, back)
    if PAR["POLISH"]:
        keep = dict(PAR)
        PAR.update(PAR["POLISH"])
        total, start = polish(ops, gap, back, sorted(range(n), key=lambda i: (start[i], i)), np.random.default_rng(PAR["SEED"]))
        PAR.update(keep)
    fin = [0.0] * n
    order = sorted(range(n), key=lambda i: (start[i], i))
    bank, extra, fin = {}, [[] for _ in ops], [0.0] * n
    for i in order:
        o = ops[i]
        o["t"] = start[i]
        fin[i] = o["t"] + o["cost"] + o["lat"]
        for b in o["banks"]:
            extra[i] += [j for e2, j in bank.get(b, {}).items() if e2 != o["eng"]]
            bank.setdefault(b, {})[o["eng"]] = i
    pos = {}
    seen = {e: {} for e in "VSPGY"}
    know = [None] * n
    k = {e: 0 for e in "VSPGY"}
    for i in order:
        k[ops[i]["eng"]] += 1
        pos[i] = k[ops[i]["eng"]]
    need = set()
    for i in order:
        o = ops[i]
        e = o["eng"]
        waits = []
        for j in sorted(pred[i] | set(extra[i]), key=lambda x: -fin[x]):
            p = ops[j]
            if p["sem"] is not None:
                key, val = ("d", j), 1
            else:
                if e == "P" and p["eng"] == "P":
                    continue
                key, val = p["eng"], pos[j]
            if seen[e].get(key, 0) >= val:
                continue
            waits.append(j)
            need.add(j)
            for kk, vv in know[j].items():
                if seen[e].get(kk, 0) < vv:
                    seen[e][kk] = vv
        o["waits"] = waits
        kn = dict(seen[e])
        if o["sem"] is not None:
            if o["sem"][1] == "far":
                kn = {}
            kn[("d", i)] = 1
        else:
            kn[e] = max(kn.get(e, 0), pos[i])
        know[i] = kn
    tot = {e: 0 for e in "VSPG"}
    for i in order:
        o = ops[i]
        if o["sem"] is None and i in need:
            tot[o["eng"]] += 1
            o["inc"] = tot[o["eng"]]
    return ops, order, total


def resolver(T):
    def R(a):
        if not isinstance(a, tuple):
            return a
        if a[0] == "ind":
            return R(a[1]).indirect(R(a[2]))
        if len(a) > 4:
            lo, hi, step = a[4]
            return T[a[0]][:, lo, :] if hi == lo + 1 else T[a[0]][:, lo:hi:step, :]
        if a[3] == 1:
            return T[a[0]][:, a[1]:a[2]]
        return T[a[0]][:, a[1]:a[2]:a[3]]
    return R


PLAN = {}


def rank_program(g, core, T, topo):
    rank = T.rank_of(core)
    if rank is None:
        return
    if "p" not in PLAN:
        PLAN["p"] = plan()
    ops, order, _ = PLAN["p"]
    Q = {"V": g.vector, "S": g.scalar, "P": g.tensor, "G": g, "Y": g.sync}
    X = {"T": T, "topo": topo, "core": core, "rank": rank, "sent": [0]}
    nfar = len(topo.engines(core, T.cores[(rank + 1) % N]))
    R = resolver(T)
    nout = 0
    for i in order:
        o = ops[i]
        q = Q[o["eng"]]
        for j in o["waits"]:
            p = ops[j]
            if p["sem"] is None:
                q.wait_ge(T.sem["q" + p["eng"]], p["inc"])
            else:
                q.wait_ge(T.sem[p["sem"][0]], nfar if p["sem"][1] == "far" else p["sem"][1])
        ins = o["call"](q, R, X)
        if o["sem"] is None:
            if "inc" in o:
                ins.then_inc(T.sem["q" + o["eng"]], 1)
        elif o["sem"][1] != "far":
            ins.then_inc(T.sem[o["sem"][0]], 16)
            nout += o["sem"][0] == "outs"
    g.wait_ge(T.sem["sent"], X["sent"][0])
    g.sync.wait_ge(T.sem["outs"], 16 * nout)
